import numpy as np
import ml_dtypes


def mxq(x, axis, fmt="e4m3"):
    dtype, down = {"e4m3": (ml_dtypes.float8_e4m3fn, 7), "e5m2": (ml_dtypes.float8_e5m2, 14)}[fmt]
    v = np.moveaxis(np.asarray(x, np.float32).astype(ml_dtypes.bfloat16).astype(np.float64), axis, -1)
    blocks = v.reshape(v.shape[:-1] + (-1, 32))
    amax = np.abs(blocks).max(-1, keepdims=True)
    byte = np.maximum(np.where(amax > 0, np.frexp(amax)[1] - 1 + 127, 0) - down, 1)
    scale = np.exp2(byte - 127.0)
    codes = (blocks / scale).astype(np.float32).astype(dtype).astype(np.float64)
    return np.moveaxis((codes * scale).reshape(v.shape), -1, axis)


WIDE = False


def mx_kscale(k):
    if not WIDE:
        return np.ones(k)
    levels = np.array([10, -10, 5, -5, 0])
    if k % 512:
        return np.exp2(np.random.permutation(np.resize(levels, k // 32))).repeat(32)
    a = np.empty((k // 512, 16))
    for p in range(k // 512):
        a[p, :8] = np.random.permutation(np.resize(levels, 8))
        for g in range(8):
            far = levels[np.abs(levels - a[p, g]) >= 10]
            a[p, g + 8] = far[np.random.randint(len(far))]
    return np.exp2(a.ravel()).repeat(32)


def f64(x):
    return np.asarray(x).astype(np.float64)


def striped(idx):
    return np.tile(np.asarray(idx).reshape(-1, 16).T, (8, 1)).astype(np.uint16)


def unstriped(offs):
    return offs[:16].T.reshape(-1).astype(np.int64)


E2M1 = np.array([0.0, 0.5, 1.0, 1.5, 2.0, 3.0, 4.0, 6.0, -0.0, -0.5, -1.0, -1.5, -2.0, -3.0, -4.0, -6.0])


def pack_weight(w, fmt):
    k, n = w.shape
    w = f64(np.asarray(w, np.float32).astype(ml_dtypes.bfloat16)).reshape(k // 32, 32, n)
    amax = np.abs(w).max(1)
    if fmt == "e4m3":
        byte = np.frexp(amax)[1] - 1 + 127 - 7
    else:
        mant, ex = np.frexp(amax / 6.0)
        byte = np.where(mant > 0.5, ex, ex - 1) + 127
    byte = np.clip(np.where(amax > 0, byte, 1), 1, 254)
    scaled = (w * np.exp2(127.0 - byte)[:, None, :]).reshape(k, n).astype(np.float32)
    by_word = np.ascontiguousarray(scaled.reshape(k // 512, 128, 4, n).transpose(0, 1, 3, 2))
    if fmt == "e4m3":
        words = by_word.astype(ml_dtypes.float8_e4m3fn).view(np.uint8)
    else:
        c = by_word.astype(ml_dtypes.float4_e2m1fn).view(np.uint8) & 0xF
        words = (c[..., 0::2] | (c[..., 1::2] << 4)).reshape(k // 512, 128, 2 * n)
    return np.ascontiguousarray(words), np.ascontiguousarray(byte.astype(np.uint8).reshape(k // 512, 16, n))


def unpack_weight(words, scales, fmt):
    g, _, n = scales.shape
    words = np.ascontiguousarray(words).reshape(g, 128, n, -1)
    if fmt == "e4m3":
        vals = words.view(ml_dtypes.float8_e4m3fn).astype(np.float64)
    else:
        nib = np.empty((g, 128, n, 4), np.uint8)
        nib[..., 0::2] = words & 0xF
        nib[..., 1::2] = words >> 4
        vals = E2M1[nib]
    vals = vals * np.repeat(np.exp2(scales.astype(np.float64) - 127.0), 8, axis=1)[..., None]
    return vals.transpose(0, 1, 3, 2).reshape(g * 512, n)


B, N, T, D, NQ = 1, 512, 2048, 1024, 512
DV = 512


def sgn(shape):
    return np.random.uniform(0.5, 2.0, shape) * np.where(np.random.standard_normal(shape) < 0, -1.0, 1.0)


def setup_inputs():
    n = np.random.standard_normal
    idx = np.random.permutation(T)[:B * N]
    s = mx_kscale(D)[:, None]
    u = mx_kscale(N)
    ut = np.ones(T)
    ut[idx] = u
    kp = pack_weight(n((D, T)) / s, "e2m1")
    return {
        "qT": (n((B, D, NQ)) * s * (1.00 / np.sqrt(D))).astype(np.float32),
        "k_words": np.ascontiguousarray(kp[0].reshape(1, 2, 128, T, 2).transpose(0, 2, 3, 1, 4)).reshape(1, 128, T, 4),
        "k_scales": kp[1],
        "vT": (n((DV, T)) / ut).astype(np.float32),
        "dc": np.tile(np.random.uniform(0.1, 1.0, 2048), (128, 1)).astype(np.float32),
        "ls": (np.random.uniform(7.0, 7.6, (B, 1, NQ))).astype(np.float32),
        "lm": (np.random.uniform(0.1, 0.9, (B, NQ, 1))).astype(np.float32),
        "pa": (n((B, NQ, DV))).astype(np.float32),
        "us": (sgn((B, N, 1)) * u[:, None]).astype(np.float32),
        "offs": striped(idx),
    }


def reference(qT, k_words, k_scales, vT, dc, ls, lm, pa, us, offs):
    idx = unstriped(offs)
    pick = lambda x, which: x[:, which].reshape(x.shape[0], B, -1).transpose(1, 0, 2)
    k = unpack_weight(k_words.reshape(1, 128, T, 2, 2).transpose(0, 3, 1, 2, 4).reshape(2, 128, 2 * T), k_scales, "e2m1")
    kg = pick(k, idx)
    qq = mxq(f64(qT), 1, "e4m3")
    a = kg.transpose(0, 2, 1) @ qq
    y = np.exp(a - f64(ls)) * pick(f64(dc), idx)[:, :1, :].transpose(0, 2, 1) * f64(us)
    wq = mxq(y, 1, "e4m3")
    o = wq.transpose(0, 2, 1) @ mxq(pick(f64(vT), idx).transpose(0, 2, 1), 1, "e4m3")
    r_ = f64(lm) * o + (1.0 - f64(lm)) * f64(pa)
    return r_

@@ -1,0 +1,241 @@
+from contextlib import ExitStack
+
+import concourse.mybir as mybir
+from concourse.masks import make_identity
+
+F32 = mybir.dt.float32
+BF16 = mybir.dt.bfloat16
+I32 = mybir.dt.int32
+U32 = mybir.dt.uint32
+U16 = mybir.dt.uint16
+U8 = mybir.dt.uint8
+FP8X4 = mybir.dt.float8_e4m3fn_x4
+FP4X4 = mybir.dt.float4_e2m1fn_x4
+MULT = mybir.AluOpType.mult
+ADD = mybir.AluOpType.add
+COPY = mybir.ActivationFunctionType.Copy
+EXP = mybir.ActivationFunctionType.Exp
+
+P = 128
+PACK = 4
+N, T, D, NQ, DV = 512, 2048, 1024, 512, 512
+PASSES = D // (P * PACK)
+QB = NQ // P
+EB = DV // P
+EARLY = (EB - 1) * P
+
+FLOPS = 2 * N * NQ * D + 2 * N * NQ * DV
+BYTES = 4 * (D * NQ + P * T + DV * T + T + 2 * NQ + N + 2 * NQ * DV) + PASSES * 16 * T + 2 * P * N // 16
+
+
+def tile_attend_atb_decay_topk_kernel(tc, qT, k_words, k_scales, vT, dc, ls, lm, pa, us, offs, out):
+    nc = tc.nc
+    with ExitStack() as ctx:
+        sb = ctx.enter_context(tc.tile_pool(name="sb", bufs=1))
+        ps = ctx.enter_context(tc.psum_pool(name="ps", bufs=8))
+
+        def tile(name, shape, dtype):
+            return sb.tile(shape, dtype, name=name, align_bytes=64)
+
+        def bank(name, shape):
+            return ps.tile(shape, F32, name=name, tag="bank")
+
+        offsets = sb.tile([P, N // 16], U16, name="offsets")
+        nc.sync.dma_start(offsets[:], offs)
+
+        k_pool = tile("k_pool", [P, T], I32)
+        nc.sync.dma_start(k_pool[:], k_words[0].rearrange("p t b -> p (t b)").bitcast(I32))
+
+        s_pool = tile("s_pool", [P, PASSES, T // 4], I32)
+        nc.vector.memset(s_pool[:], 0)
+        for quad in range(4):
+            nc.scalar.dma_start(
+                s_pool[32 * quad : 32 * quad + 4, :, :],
+                k_scales[:, 4 * quad : 4 * quad + 4, :].rearrange("o f t -> f o t").bitcast(I32),
+            )
+        dc_pool = tile("dc_pool", [P, T], F32)
+        nc.vector.memset(dc_pool[:], 0.0)
+        nc.scalar.dma_start(dc_pool[0:1, :], dc[0:1, :])
+
+        q_raw = []
+        for o in range(PASSES):
+            raw = tile("q_raw%d" % o, [P, PACK, NQ], F32)
+            nc.sync.dma_start(raw[:], qT[0, o * 512 : (o + 1) * 512, :].rearrange("(p j) q -> p j q", j=PACK))
+            q_raw.append(raw)
+
+        rows = tile("rows", [P, P], F32)
+        nc.vector.memset(rows[:], 0.0)
+        nc.scalar.dma_start(rows[0:QB, :], ls[0, 0, :].rearrange("(b p) -> b p", p=P))
+        nc.scalar.dma_start(rows[QB : 2 * QB, :], lm[0].rearrange("(b p) x -> b (p x)", p=P))
+        us_t = tile("us_t", [P, PACK], F32)
+        nc.scalar.dma_start(us_t[:], us[0].rearrange("(p t) x -> p (t x)", t=PACK))
+        ident = tile("ident", [P, P], F32)
+        make_identity(nc, ident[:])
+
+        v_pool = []
+        for c in range(EB):
+            pool_c = tile("v_pool%d" % c, [P, T], F32)
+            nc.sync.dma_start(pool_c[:], vT[c * P : (c + 1) * P, :])
+            v_pool.append(pool_c)
+        pa_raw = []
+        for b in range(QB):
+            raw = tile("pa_raw%d" % b, [P, DV], F32)
+            nc.sync.dma_start(raw[:], pa[0, b * P : (b + 1) * P, :])
+            pa_raw.append(raw)
+
+        cols_ps = bank("cols_ps", [P, P])
+        nc.tensor.transpose(cols_ps[:], rows[:], ident[:])
+        neg_ls = tile("neg_ls", [P, QB], F32)
+        nc.scalar.activation(neg_ls[:], cols_ps[:, 0:QB], COPY, scale=-1.0)
+        lm_col = tile("lm_col", [P, QB], F32)
+        nc.scalar.copy(lm_col[:], cols_ps[:, QB : 2 * QB])
+        rest_col = tile("rest_col", [P, QB], F32)
+        nc.scalar.activation(rest_col[:], cols_ps[:, QB : 2 * QB], COPY, scale=-1.0, bias=1.0)
+
+        k_scale = []
+        for o in range(PASSES):
+            plane = tile("k_scale%d" % o, [P, N], U8)
+            nc.vector.tensor_copy(plane[:], s_pool[:, o, :].bitcast(U8).indirect(offsets[:]))
+            k_scale.append(plane)
+        k_pair = tile("k_pair", [P, N], U32)
+        nc.vector.tensor_copy(k_pair[:], k_pool[:].bitcast(U32).indirect(offsets[:]))
+        k_code = tile("k_code", [P, PASSES, 2 * N], U8)
+        nc.vector.tensor_copy(
+            k_code[:].bitcast(U16), k_pair[:].bitcast(U16).rearrange("p (n o) -> p o n", o=PASSES)
+        )
+
+        dc_row = tile("dc_row", [P, N], F32)
+        nc.vector.tensor_copy(dc_row[:], dc_pool[:].indirect(offsets[:]))
+        dc_ps = bank("dc_ps", [P, PACK, P])
+        for t in range(PACK):
+            nc.tensor.transpose(dc_ps[:, t, :], dc_row[:, t::PACK], ident[:])
+        weight = tile("weight", [P, PACK], F32)
+        nc.vector.tensor_tensor(weight[:], dc_ps[:, :, 0], us_t[:], MULT)
+
+        q_bf = [tile("q_bf%d" % o, [P, NQ, PACK], BF16) for o in range(PASSES)]
+        q_code = [tile("q_code%d" % o, [P, NQ], U32) for o in range(PASSES)]
+        q_scale = [tile("q_scale%d" % o, [P, NQ], U8) for o in range(PASSES)]
+
+        def interleave_q(o, lo, hi):
+            nc.scalar.copy(
+                q_bf[o][:, lo:hi, :].rearrange("p (c i) t -> p c t i", i=4),
+                q_raw[o][:, :, lo:hi].rearrange("p t (c i) -> p c t i", i=4),
+            )
+
+        def quantize_q(o, lo, hi):
+            nc.vector.quantize_mx(
+                q_code[o][:, lo:hi].bitcast(FP8X4),
+                q_scale[o][:, lo:hi],
+                q_bf[o][:, lo:hi, :].rearrange("p q t -> p (q t)"),
+            )
+
+        v_code = tile("v_code", [P, DV], U32)
+        v_scale = tile("v_scale", [P, DV], U8)
+        y_code = [tile("y_code%d" % b, [P, P], U32) for b in range(QB)]
+        y_scale = [tile("y_scale%d" % b, [P, P], U8) for b in range(QB)]
+        v_bf = [tile("v_bf%d" % c, [P, P, PACK], BF16) for c in range(EB)]
+        y_bf = [tile("y_bf%d" % b, [P, P, PACK], BF16) for b in range(QB)]
+
+        def gather_v(c):
+            picked = tile("v_picked%d" % c, [P, N], F32)
+            nc.vector.tensor_copy(picked[:], v_pool[c][:].indirect(offsets[:]))
+            turned = bank("v_turned%d" % c, [P, PACK, P])
+            for t in range(PACK):
+                nc.tensor.transpose(turned[:, t, :], picked[:, t::PACK], ident[:])
+            nc.scalar.copy(v_bf[c][:], turned[:].rearrange("p t e -> p e t"))
+
+        def quantize_v(c):
+            nc.vector.quantize_mx(
+                v_code[:, c * P : (c + 1) * P].bitcast(FP8X4),
+                v_scale[:, c * P : (c + 1) * P],
+                v_bf[c][:].rearrange("p e t -> p (e t)"),
+            )
+
+        def scores(b):
+            acc = bank("score%d" % b, [P, N])
+            for o in range(PASSES):
+                nc.tensor.matmul_mx(
+                    acc[:],
+                    lhsT=q_code[o][:, b * P : (b + 1) * P].bitcast(FP8X4),
+                    lhsT_scale=q_scale[o][:, b * P : (b + 1) * P],
+                    rhs=k_code[:, o, :].bitcast(FP4X4),
+                    rhs_scale=k_scale[o][:],
+                    start=(o == 0),
+                    stop=(o == PASSES - 1),
+                )
+            prob = tile("prob%d" % b, [P, PACK, P], F32)
+            nc.scalar.activation(
+                prob[:], acc[:].rearrange("q (m t) -> q t m", t=PACK), EXP, bias=neg_ls[:, b : b + 1]
+            )
+            turned = bank("p_turned%d" % b, [P, PACK, P])
+            for t in range(PACK):
+                nc.tensor.transpose(turned[:, t, :], prob[:, t, :], ident[:])
+            nc.vector.tensor_tensor(
+                y_bf[b][:],
+                turned[:].rearrange("p t q -> p q t"),
+                weight[:].unsqueeze(1).to_broadcast([P, P, PACK]),
+                MULT,
+            )
+
+        def quantize_y(b):
+            nc.vector.quantize_mx(
+                y_code[b][:].bitcast(FP8X4), y_scale[b][:], y_bf[b][:].rearrange("p q t -> p (q t)")
+            )
+
+        def product(dst, b, lo, hi):
+            nc.tensor.matmul_mx(
+                dst,
+                lhsT=y_code[b][:].bitcast(FP8X4),
+                lhsT_scale=y_scale[b][:],
+                rhs=v_code[:, lo:hi].bitcast(FP8X4),
+                rhs_scale=v_scale[:, lo:hi],
+                start=True,
+                stop=True,
+            )
+
+        interleave_q(0, 0, NQ)
+        quantize_q(0, 0, NQ)
+        for b in range(QB):
+            interleave_q(1, b * P, (b + 1) * P)
+            quantize_q(1, b * P, (b + 1) * P)
+        gather_v(0)
+        scores(0)
+        scores(1)
+        quantize_v(0)
+        quantize_y(0)
+        gather_v(1)
+        scores(2)
+        quantize_y(1)
+        scores(3)
+        quantize_v(1)
+        quantize_y(2)
+        gather_v(2)
+        quantize_y(3)
+        gather_v(3)
+        quantize_v(2)
+
+        early = []
+        for b in range(QB):
+            acc = bank("early%d" % b, [P, EARLY])
+            product(acc[:, 0 : 2 * P], b, 0, 2 * P)
+            product(acc[:, 2 * P : EARLY], b, 2 * P, EARLY)
+            early.append(acc)
+        quantize_v(3)
+        late = bank("late", [P, QB, P])
+        for b in range(QB):
+            product(late[:, b, :], b, EARLY, DV)
+
+        local = [tile("local%d" % b, [P, DV], F32) for b in range(QB)]
+        res_late = tile("res_late", [P, QB, P], F32)
+        for b in range(QB):
+            nc.scalar.activation(local[b][:], pa_raw[b][:], COPY, scale=rest_col[:, b : b + 1])
+            res = tile("res%d" % b, [P, EARLY], F32)
+            nc.vector.scalar_tensor_tensor(
+                res[:], early[b][:], lm_col[:, b : b + 1], local[b][:, 0:EARLY], MULT, ADD
+            )
+            nc.sync.dma_start(out[0, b * P : (b + 1) * P, 0:EARLY], res[:])
+        for b in range(QB):
+            nc.vector.scalar_tensor_tensor(
+                res_late[:, b, :], late[:, b, :], lm_col[:, b : b + 1], local[b][:, EARLY:DV], MULT, ADD
+            )
+        nc.sync.dma_start(out[0, :, EARLY:DV].rearrange("(b p) e -> p b e", p=P), res_late[:])

@@ -1,7 +1,6 @@
 from contextlib import ExitStack
 
 import concourse.mybir as mybir
-from concourse.masks import make_identity
 
 F32 = mybir.dt.float32
 BF16 = mybir.dt.bfloat16
@@ -23,6 +22,7 @@ PASSES = D // (P * PACK)
 QB = NQ // P
 EB = DV // P
 EARLY = (EB - 1) * P
+SLOTS = 3 + EB
 
 FLOPS = 2 * N * NQ * D + 2 * N * NQ * DV
 BYTES = 4 * (D * NQ + P * T + DV * T + T + 2 * NQ + N + 2 * NQ * DV) + PASSES * 16 * T + 2 * P * N // 16
@@ -32,71 +32,85 @@ def tile_attend_atb_decay_topk_kernel(tc, qT, k_words, k_scales, vT, dc, ls, lm,
     nc = tc.nc
     with ExitStack() as ctx:
         sb = ctx.enter_context(tc.tile_pool(name="sb", bufs=1))
-        ps = ctx.enter_context(tc.psum_pool(name="ps", bufs=8))
+        stream = ctx.enter_context(tc.tile_pool(name="stream", bufs=1))
+        work = ctx.enter_context(tc.tile_pool(name="work", bufs=1))
+        ps = ctx.enter_context(tc.psum_pool(name="ps", bufs=1))
 
         def tile(name, shape, dtype):
             return sb.tile(shape, dtype, name=name, align_bytes=64)
 
-        def bank(name, shape):
-            return ps.tile(shape, F32, name=name, tag="bank")
+        def shared(name, shape, dtype, place, skip=0):
+            return work.tile(shape, dtype, name=name, align_bytes=64, offset=4096 * place + skip)
+
+        def reuse(name, shape, dtype, slot, skip=0):
+            return stream.tile(shape, dtype, name=name, align_bytes=64, offset=4 * T * slot + skip)
+
+        def bank(name, shape, number):
+            return ps.tile(shape, F32, name=name, offset=2048 * number)
+
+        def q_rows(o):
+            return qT[0, o * 512 : (o + 1) * 512, :].rearrange("(p j) q -> p j q", j=PACK)
 
         offsets = sb.tile([P, N // 16], U16, name="offsets")
         nc.sync.dma_start(offsets[:], offs)
-
         k_pool = tile("k_pool", [P, T], I32)
         nc.sync.dma_start(k_pool[:], k_words[0].rearrange("p t b -> p (t b)").bitcast(I32))
 
-        s_pool = tile("s_pool", [P, PASSES, T // 4], I32)
-        nc.vector.memset(s_pool[:], 0)
+        rows = tile("rows", [P, P], F32)
+        nc.vector.memset(rows[:, 0:63], 0.0)
+        nc.vector.memset(rows[:, 63:P], 0.0)
+        nc.scalar.dma_start(rows[0:QB, :], ls[0, 0, :].rearrange("(b p) -> b p", p=P))
+        s_pool = shared("s_pool", [P, PASSES, T // 4], I32, 9)
+        s_words = s_pool[:].rearrange("p o w -> p (o w)")
+        nc.vector.memset(s_words[:, 0:511], 0)
+        nc.vector.memset(s_words[:, 511:1024], 0)
         for quad in range(4):
             nc.scalar.dma_start(
                 s_pool[32 * quad : 32 * quad + 4, :, :],
                 k_scales[:, 4 * quad : 4 * quad + 4, :].rearrange("o f t -> f o t").bitcast(I32),
             )
-        dc_pool = tile("dc_pool", [P, T], F32)
-        nc.vector.memset(dc_pool[:], 0.0)
+        dc_pool = shared("dc_pool", [P, T], F32, 10)
+        nc.gpsimd.memset(dc_pool[:], 0.0)
         nc.scalar.dma_start(dc_pool[0:1, :], dc[0:1, :])
+
+        scratch = stream.tile([P, SLOTS * T + 16], F32, name="scratch", offset=0)
+        nc.gpsimd.memset(scratch[:, 0:P], 0.0)
+        ident = tile("ident", [P, P], F32)
+        nc.gpsimd.affine_select(
+            out=ident[:],
+            in_=scratch[:, 0:P],
+            compare_op=mybir.AluOpType.not_equal,
+            fill=1.0,
+            base=0,
+            pattern=[[-1, P]],
+            channel_multiplier=1,
+        )
 
         q_raw = []
         for o in range(PASSES):
-            raw = tile("q_raw%d" % o, [P, PACK, NQ], F32)
-            nc.sync.dma_start(raw[:], qT[0, o * 512 : (o + 1) * 512, :].rearrange("(p j) q -> p j q", j=PACK))
+            raw = reuse("q_raw%d" % o, [P, PACK, NQ], F32, o)
+            nc.sync.dma_start(raw[:], q_rows(o))
             q_raw.append(raw)
-
-        rows = tile("rows", [P, P], F32)
-        nc.vector.memset(rows[:], 0.0)
-        nc.scalar.dma_start(rows[0:QB, :], ls[0, 0, :].rearrange("(b p) -> b p", p=P))
-        nc.scalar.dma_start(rows[QB : 2 * QB, :], lm[0].rearrange("(b p) x -> b (p x)", p=P))
-        us_t = tile("us_t", [P, PACK], F32)
-        nc.scalar.dma_start(us_t[:], us[0].rearrange("(p t) x -> p (t x)", t=PACK))
-        ident = tile("ident", [P, P], F32)
-        make_identity(nc, ident[:])
-
+        us_t = stream.tile([P, PACK], F32, name="us_t", offset=4 * T * SLOTS)
+        nc.sync.dma_start(us_t[:], us[0].rearrange("(p t) x -> p (t x)", t=PACK))
+        lm_col = stream.tile([P, QB], F32, name="lm_col", offset=4 * T * SLOTS + 32)
+        nc.sync.dma_start(lm_col[:], lm[0].rearrange("(p b) x -> p (b x)", b=QB))
         v_pool = []
         for c in range(EB):
-            pool_c = tile("v_pool%d" % c, [P, T], F32)
+            pool_c = stream.tile([P, T], F32, name="v_pool%d" % c, offset=4 * T * (2 + c))
             nc.sync.dma_start(pool_c[:], vT[c * P : (c + 1) * P, :])
             v_pool.append(pool_c)
         pa_raw = []
         for b in range(QB):
-            raw = tile("pa_raw%d" % b, [P, DV], F32)
-            nc.sync.dma_start(raw[:], pa[0, b * P : (b + 1) * P, :])
+            raw = stream.tile([P, DV], F32, name="pa_raw%d" % b, offset=4 * T * (2 + EB) + 4 * DV * b)
+            nc.sync.dma_start(raw[:], pa[0].rearrange("(p b) e -> p b e", b=QB)[:, b, :])
             pa_raw.append(raw)
 
-        cols_ps = bank("cols_ps", [P, P])
+        cols_ps = bank("cols_ps", [P, P], 4)
         nc.tensor.transpose(cols_ps[:], rows[:], ident[:])
         neg_ls = tile("neg_ls", [P, QB], F32)
         nc.scalar.activation(neg_ls[:], cols_ps[:, 0:QB], COPY, scale=-1.0)
-        lm_col = tile("lm_col", [P, QB], F32)
-        nc.scalar.copy(lm_col[:], cols_ps[:, QB : 2 * QB])
-        rest_col = tile("rest_col", [P, QB], F32)
-        nc.scalar.activation(rest_col[:], cols_ps[:, QB : 2 * QB], COPY, scale=-1.0, bias=1.0)
 
-        k_scale = []
-        for o in range(PASSES):
-            plane = tile("k_scale%d" % o, [P, N], U8)
-            nc.vector.tensor_copy(plane[:], s_pool[:, o, :].bitcast(U8).indirect(offsets[:]))
-            k_scale.append(plane)
         k_pair = tile("k_pair", [P, N], U32)
         nc.vector.tensor_copy(k_pair[:], k_pool[:].bitcast(U32).indirect(offsets[:]))
         k_code = tile("k_code", [P, PASSES, 2 * N], U8)
@@ -104,20 +118,26 @@ def tile_attend_atb_decay_topk_kernel(tc, qT, k_words, k_scales, vT, dc, ls, lm,
             k_code[:].bitcast(U16), k_pair[:].bitcast(U16).rearrange("p (n o) -> p o n", o=PASSES)
         )
 
-        dc_row = tile("dc_row", [P, N], F32)
+        k_scale = []
+        for o in range(PASSES):
+            plane = tile("k_scale%d" % o, [P, N], U8)
+            nc.vector.tensor_copy(plane[:], s_pool[:, o, :].bitcast(U8).indirect(offsets[:]))
+            k_scale.append(plane)
+        dc_row = shared("dc_row", [P, N], F32, 9)
         nc.vector.tensor_copy(dc_row[:], dc_pool[:].indirect(offsets[:]))
-        dc_ps = bank("dc_ps", [P, PACK, P])
+        dc_ps = bank("dc_ps", [P, PACK, P], 5)
         for t in range(PACK):
             nc.tensor.transpose(dc_ps[:, t, :], dc_row[:, t::PACK], ident[:])
-        weight = tile("weight", [P, PACK], F32)
-        nc.vector.tensor_tensor(weight[:], dc_ps[:, :, 0], us_t[:], MULT)
 
-        q_bf = [tile("q_bf%d" % o, [P, NQ, PACK], BF16) for o in range(PASSES)]
-        q_code = [tile("q_code%d" % o, [P, NQ], U32) for o in range(PASSES)]
+        q_bf = [tile("q_bf0", [P, NQ, PACK], BF16), shared("q_bf1", [P, NQ, PACK], BF16, 0)]
+        q_code = [
+            shared("q_code0", [P, NQ], U32, 10),
+            tile("q_code1", [P, NQ], U32),
+        ]
         q_scale = [tile("q_scale%d" % o, [P, NQ], U8) for o in range(PASSES)]
 
-        def interleave_q(o, lo, hi):
-            nc.scalar.copy(
+        def interleave_q(copy, o, lo, hi):
+            copy(
                 q_bf[o][:, lo:hi, :].rearrange("p (c i) t -> p c t i", i=4),
                 q_raw[o][:, :, lo:hi].rearrange("p t (c i) -> p c t i", i=4),
             )
@@ -129,113 +149,137 @@ def tile_attend_atb_decay_topk_kernel(tc, qT, k_words, k_scales, vT, dc, ls, lm,
                 q_bf[o][:, lo:hi, :].rearrange("p q t -> p (q t)"),
             )
 
-        v_code = tile("v_code", [P, DV], U32)
-        v_scale = tile("v_scale", [P, DV], U8)
-        y_code = [tile("y_code%d" % b, [P, P], U32) for b in range(QB)]
-        y_scale = [tile("y_scale%d" % b, [P, P], U8) for b in range(QB)]
-        v_bf = [tile("v_bf%d" % c, [P, P, PACK], BF16) for c in range(EB)]
-        y_bf = [tile("y_bf%d" % b, [P, P, PACK], BF16) for b in range(QB)]
+        prob = [
+            tile("prob0", [P, PACK, P], F32),
+            tile("prob1", [P, PACK, P], F32),
+            tile("prob2", [P, PACK, P], F32),
+            shared("prob3", [P, PACK, P], F32, 2, 1024),
+        ]
+        weight = shared("weight", [P, PACK], F32, 0, 2048)
+        y_bf = reuse("y_bf", [P, NQ, PACK], BF16, 3)
+        y_code = reuse("y_code", [P, NQ], U32, 5)
+        y_scale = tile("y_scale", [P, NQ], U8)
+        groups = ((0, 2 * P), (2 * P, 3 * P), (3 * P, DV))
+        v_bf = [
+            tile("v_bf0", [P, 2 * P, PACK], BF16),
+            reuse("v_bf1", [P, P, PACK], BF16, 6),
+            reuse("v_bf2", [P, P, PACK], BF16, 6, 4 * DV),
+        ]
+        v_code = [
+            reuse("v_code0", [P, 2 * P], U32, 5, 2048),
+            reuse("v_code1", [P, P], U32, 5, 4096),
+            tile("v_code2", [P, P], U32),
+        ]
+        v_scale = [tile("v_scale%d" % g, [P, hi - lo], U8) for g, (lo, hi) in enumerate(groups)]
+        v_picked = [shared("v_picked%d" % c, [P, N], F32, c) for c in range(EB)]
 
         def gather_v(c):
-            picked = tile("v_picked%d" % c, [P, N], F32)
-            nc.vector.tensor_copy(picked[:], v_pool[c][:].indirect(offsets[:]))
-            turned = bank("v_turned%d" % c, [P, PACK, P])
-            for t in range(PACK):
-                nc.tensor.transpose(turned[:, t, :], picked[:, t::PACK], ident[:])
-            nc.scalar.copy(v_bf[c][:], turned[:].rearrange("p t e -> p e t"))
+            nc.vector.tensor_copy(v_picked[c][:], v_pool[c][:].indirect(offsets[:]))
 
-        def quantize_v(c):
+        def turn_v(c):
+            turned = bank("v_turned%d" % c, [P, PACK, P], (0, 4, 5, 6)[c])
+            for t in range(PACK):
+                nc.tensor.transpose(turned[:, t, :], v_picked[c][:, t::PACK], ident[:])
+            return turned[:].rearrange("p t e -> p e t")
+
+        def quantize_v(g):
             nc.vector.quantize_mx(
-                v_code[:, c * P : (c + 1) * P].bitcast(FP8X4),
-                v_scale[:, c * P : (c + 1) * P],
-                v_bf[c][:].rearrange("p e t -> p (e t)"),
+                v_code[g][:].bitcast(FP8X4), v_scale[g][:], v_bf[g][:].rearrange("p e t -> p (e t)")
             )
 
-        def scores(b):
-            acc = bank("score%d" % b, [P, N])
-            for o in range(PASSES):
-                nc.tensor.matmul_mx(
-                    acc[:],
-                    lhsT=q_code[o][:, b * P : (b + 1) * P].bitcast(FP8X4),
-                    lhsT_scale=q_scale[o][:, b * P : (b + 1) * P],
-                    rhs=k_code[:, o, :].bitcast(FP4X4),
-                    rhs_scale=k_scale[o][:],
-                    start=(o == 0),
-                    stop=(o == PASSES - 1),
-                )
-            prob = tile("prob%d" % b, [P, PACK, P], F32)
-            nc.scalar.activation(
-                prob[:], acc[:].rearrange("q (m t) -> q t m", t=PACK), EXP, bias=neg_ls[:, b : b + 1]
+        def score_pass(acc, b, o):
+            nc.tensor.matmul_mx(
+                acc[:],
+                lhsT=q_code[o][:, b * P : (b + 1) * P].bitcast(FP8X4),
+                lhsT_scale=q_scale[o][:, b * P : (b + 1) * P],
+                rhs=k_code[:, o, :].bitcast(FP4X4),
+                rhs_scale=k_scale[o][:],
+                start=(o == 0),
+                stop=(o == PASSES - 1),
             )
-            turned = bank("p_turned%d" % b, [P, PACK, P])
+
+        def weigh(b):
+            nc.scalar.activation(
+                prob[b][:], score[b][:].rearrange("q (m t) -> q t m", t=PACK), EXP, bias=neg_ls[:, b : b + 1]
+            )
+            turned = bank("p_turned%d" % b, [P, PACK, P], 4 + b)
             for t in range(PACK):
-                nc.tensor.transpose(turned[:, t, :], prob[:, t, :], ident[:])
+                nc.tensor.transpose(turned[:, t, :], prob[b][:, t, :], ident[:])
             nc.vector.tensor_tensor(
-                y_bf[b][:],
-                turned[:].rearrange("p t q -> p q t"),
-                weight[:].unsqueeze(1).to_broadcast([P, P, PACK]),
+                y_bf[:].rearrange("p (g r) t -> p g r t", g=QB)[:, :, 32 * b : 32 * (b + 1), :],
+                turned[:].rearrange("p t (r g) -> p g r t", g=QB),
+                weight[:].unsqueeze(1).unsqueeze(1).to_broadcast([P, QB, 32, PACK]),
                 MULT,
             )
 
-        def quantize_y(b):
+        def quantize_y(lo, hi):
             nc.vector.quantize_mx(
-                y_code[b][:].bitcast(FP8X4), y_scale[b][:], y_bf[b][:].rearrange("p q t -> p (q t)")
+                y_code[:, lo:hi].bitcast(FP8X4), y_scale[:, lo:hi], y_bf[:, lo:hi, :].rearrange("p q t -> p (q t)")
             )
 
-        def product(dst, b, lo, hi):
-            nc.tensor.matmul_mx(
-                dst,
-                lhsT=y_code[b][:].bitcast(FP8X4),
-                lhsT_scale=y_scale[b][:],
-                rhs=v_code[:, lo:hi].bitcast(FP8X4),
-                rhs_scale=v_scale[:, lo:hi],
-                start=True,
-                stop=True,
-            )
+        def products(g, blocks, number):
+            lo, hi = groups[g]
+            acc = bank("o%d_%d" % (g, blocks[0]), [P, len(blocks), hi - lo], number)
+            for j, b in enumerate(blocks):
+                nc.tensor.matmul_mx(
+                    acc[:, j, :],
+                    lhsT=y_code[:, b * P : (b + 1) * P].bitcast(FP8X4),
+                    lhsT_scale=y_scale[:, b * P : (b + 1) * P],
+                    rhs=v_code[g][:].bitcast(FP8X4),
+                    rhs_scale=v_scale[g][:],
+                    start=True,
+                    stop=True,
+                )
+            return [acc[:, j, :] for j in range(len(blocks))]
 
-        interleave_q(0, 0, NQ)
+        interleave_q(lambda dst, src: nc.scalar.activation(dst, src, COPY), 0, 0, NQ)
         quantize_q(0, 0, NQ)
+        score = [bank("score%d" % b, [P, N], b) for b in range(QB)]
         for b in range(QB):
-            interleave_q(1, b * P, (b + 1) * P)
+            score_pass(score[b], b, 0)
+        for b in range(QB):
+            interleave_q(nc.scalar.copy if b % 2 else nc.vector.tensor_copy, 1, b * P, (b + 1) * P)
+        for b in range(QB):
             quantize_q(1, b * P, (b + 1) * P)
+            score_pass(score[b], b, 1)
+        nc.vector.tensor_tensor(weight[:], dc_ps[:, :, 0], us_t[:], MULT)
         gather_v(0)
-        scores(0)
-        scores(1)
-        quantize_v(0)
-        quantize_y(0)
         gather_v(1)
-        scores(2)
-        quantize_y(1)
-        scores(3)
+        for b in range(QB):
+            weigh(b)
+        for c in range(2):
+            nc.scalar.copy(v_bf[0][:, c * P : (c + 1) * P, :], turn_v(c))
+
+        rest_col = shared("rest_col", [P, QB], F32, 1)
+        nc.scalar.activation(rest_col[:], lm_col[:], COPY, scale=-1.0, bias=1.0)
+        local_head = tile("local_head", [P, 2, DV], F32)
+        local_tail = shared("local_tail", [P, 2, DV], F32, 3)
+        local = [local_head[:, 0, :], local_head[:, 1, :], local_tail[:, 0, :], local_tail[:, 1, :]]
+
+        def scale_local(b):
+            nc.scalar.activation(local[b], pa_raw[b][:], COPY, scale=rest_col[:, b : b + 1])
+
+        for c in range(2, EB):
+            gather_v(c)
+            turned = turn_v(c)
+            scale_local(c - 2)
+            nc.scalar.copy(v_bf[c - 1][:], turned)
+        scale_local(2)
+        scale_local(3)
+        quantize_y(0, NQ)
+        quantize_v(0)
+        sums = [products(0, (0, 1), 1) + products(0, (2, 3), 2)]
         quantize_v(1)
-        quantize_y(2)
-        gather_v(2)
-        quantize_y(3)
-        gather_v(3)
+        sums.append(products(1, (0, 1, 2, 3), 3))
         quantize_v(2)
+        sums.append(products(2, (0, 1), 7) + products(2, (2, 3), 0))
 
-        early = []
-        for b in range(QB):
-            acc = bank("early%d" % b, [P, EARLY])
-            product(acc[:, 0 : 2 * P], b, 0, 2 * P)
-            product(acc[:, 2 * P : EARLY], b, 2 * P, EARLY)
-            early.append(acc)
-        quantize_v(3)
-        late = bank("late", [P, QB, P])
-        for b in range(QB):
-            product(late[:, b, :], b, EARLY, DV)
-
-        local = [tile("local%d" % b, [P, DV], F32) for b in range(QB)]
-        res_late = tile("res_late", [P, QB, P], F32)
-        for b in range(QB):
-            nc.scalar.activation(local[b][:], pa_raw[b][:], COPY, scale=rest_col[:, b : b + 1])
-            res = tile("res%d" % b, [P, EARLY], F32)
-            nc.vector.scalar_tensor_tensor(
-                res[:], early[b][:], lm_col[:, b : b + 1], local[b][:, 0:EARLY], MULT, ADD
-            )
-            nc.sync.dma_start(out[0, b * P : (b + 1) * P, 0:EARLY], res[:])
-        for b in range(QB):
-            nc.vector.scalar_tensor_tensor(
-                res_late[:, b, :], late[:, b, :], lm_col[:, b : b + 1], local[b][:, EARLY:DV], MULT, ADD
-            )
-        nc.sync.dma_start(out[0, :, EARLY:DV].rearrange("(b p) e -> p b e", p=P), res_late[:])
+        rows_out = out[0].rearrange("(p b) e -> p b e", b=QB)
+        for g, (lo, hi) in enumerate(groups):
+            res = tile("res%d" % g, [P, QB, hi - lo], F32)
+            for b in range(QB):
+                nc.vector.scalar_tensor_tensor(
+                    res[:, b, :], sums[g][b], lm_col[:, b : b + 1], local[b][:, lo:hi], MULT, ADD
+                )
+                if b % 2:
+                    nc.sync.dma_start(rows_out[:, b - 1 : b + 1, lo:hi], res[:, b - 1 : b + 1, :])

@@ -92,9 +92,9 @@ def tile_attend_atb_decay_topk_kernel(tc, qT, k_words, k_scales, vT, dc, ls, lm,
             nc.sync.dma_start(raw[:], q_rows(o))
             q_raw.append(raw)
         us_t = stream.tile([P, PACK], F32, name="us_t", offset=4 * T * SLOTS)
-        nc.sync.dma_start(us_t[:], us[0].rearrange("(p t) x -> p (t x)", t=PACK))
+        nc.scalar.dma_start(us_t[:], us[0].rearrange("(p t) x -> p (t x)", t=PACK))
         lm_col = stream.tile([P, QB], F32, name="lm_col", offset=4 * T * SLOTS + 32)
-        nc.sync.dma_start(lm_col[:], lm[0].rearrange("(p b) x -> p (b x)", b=QB))
+        nc.scalar.dma_start(lm_col[:], lm[0].rearrange("(p b) x -> p (b x)", b=QB))
         v_pool = []
         for c in range(EB):
             pool_c = stream.tile([P, T], F32, name="v_pool%d" % c, offset=4 * T * (2 + c))
@@ -118,20 +118,21 @@ def tile_attend_atb_decay_topk_kernel(tc, qT, k_words, k_scales, vT, dc, ls, lm,
             k_code[:].bitcast(U16), k_pair[:].bitcast(U16).rearrange("p (n o) -> p o n", o=PASSES)
         )
 
-        k_scale = []
-        for o in range(PASSES):
-            plane = tile("k_scale%d" % o, [P, N], U8)
-            nc.vector.tensor_copy(plane[:], s_pool[:, o, :].bitcast(U8).indirect(offsets[:]))
-            k_scale.append(plane)
-        dc_row = shared("dc_row", [P, N], F32, 9)
+        dc_row = tile("dc_row", [P, N], F32)
         nc.vector.tensor_copy(dc_row[:], dc_pool[:].indirect(offsets[:]))
         dc_ps = bank("dc_ps", [P, PACK, P], 5)
         for t in range(PACK):
             nc.tensor.transpose(dc_ps[:, t, :], dc_row[:, t::PACK], ident[:])
 
+        k_scale = []
+        for o in range(PASSES):
+            plane = shared("k_scale%d" % o, [P, N], U8, 10 + o)
+            nc.vector.tensor_copy(plane[:], s_pool[:, o, :].bitcast(U8).indirect(offsets[:]))
+            k_scale.append(plane)
+
         q_bf = [tile("q_bf0", [P, NQ, PACK], BF16), shared("q_bf1", [P, NQ, PACK], BF16, 0)]
         q_code = [
-            shared("q_code0", [P, NQ], U32, 10),
+            shared("q_code0", [P, NQ], U32, 9),
             tile("q_code1", [P, NQ], U32),
         ]
         q_scale = [tile("q_scale%d" % o, [P, NQ], U8) for o in range(PASSES)]
@@ -157,30 +158,31 @@ def tile_attend_atb_decay_topk_kernel(tc, qT, k_words, k_scales, vT, dc, ls, lm,
         ]
         weight = shared("weight", [P, PACK], F32, 0, 2048)
         y_bf = reuse("y_bf", [P, NQ, PACK], BF16, 3)
-        y_code = reuse("y_code", [P, NQ], U32, 5)
+        y_code = reuse("y_code", [P, NQ], U32, 4)
         y_scale = tile("y_scale", [P, NQ], U8)
         groups = ((0, 2 * P), (2 * P, 3 * P), (3 * P, DV))
         v_bf = [
-            tile("v_bf0", [P, 2 * P, PACK], BF16),
+            shared("v_bf0", [P, 2 * P, PACK], BF16, 3),
             reuse("v_bf1", [P, P, PACK], BF16, 6),
             reuse("v_bf2", [P, P, PACK], BF16, 6, 4 * DV),
         ]
         v_code = [
-            reuse("v_code0", [P, 2 * P], U32, 5, 2048),
+            reuse("v_code0", [P, 2 * P], U32, 4, 2048),
             reuse("v_code1", [P, P], U32, 5, 4096),
             tile("v_code2", [P, P], U32),
         ]
         v_scale = [tile("v_scale%d" % g, [P, hi - lo], U8) for g, (lo, hi) in enumerate(groups)]
-        v_picked = [shared("v_picked%d" % c, [P, N], F32, c) for c in range(EB)]
+        v_picked = [shared("v_picked%d" % c, [P, 2, P, 2], BF16, c, 1024 * (c == 2)) for c in range(EB)]
 
         def gather_v(c):
-            nc.vector.tensor_copy(v_picked[c][:], v_pool[c][:].indirect(offsets[:]))
+            nc.vector.tensor_copy(v_picked[c][:].rearrange("e u m i -> e m u i"), v_pool[c][:].indirect(offsets[:]))
 
         def turn_v(c):
-            turned = bank("v_turned%d" % c, [P, PACK, P], (0, 4, 5, 6)[c])
-            for t in range(PACK):
-                nc.tensor.transpose(turned[:, t, :], v_picked[c][:, t::PACK], ident[:])
-            return turned[:].rearrange("p t e -> p e t")
+            turned = bank("v_turned%d" % c, [P, 2, P], (3, 4, 5, 6)[c])
+            words = v_picked[c][:].rearrange("e u m i -> e (u m i)").bitcast(F32)
+            for u in range(2):
+                nc.tensor.transpose(turned[:, u, :], words[:, u * P : (u + 1) * P], ident[:])
+            return turned[:].rearrange("p u e -> p e u")
 
         def quantize_v(g):
             nc.vector.quantize_mx(
@@ -232,11 +234,12 @@ def tile_attend_atb_decay_topk_kernel(tc, qT, k_words, k_scales, vT, dc, ls, lm,
                 )
             return [acc[:, j, :] for j in range(len(blocks))]
 
-        interleave_q(lambda dst, src: nc.scalar.activation(dst, src, COPY), 0, 0, NQ)
-        quantize_q(0, 0, NQ)
         score = [bank("score%d" % b, [P, N], b) for b in range(QB)]
-        for b in range(QB):
+        for b in range(0, QB, 2):
+            interleave_q(nc.scalar.copy, 0, b * P, (b + 2) * P)
+            quantize_q(0, b * P, (b + 2) * P)
             score_pass(score[b], b, 0)
+            score_pass(score[b + 1], b + 1, 0)
         for b in range(QB):
             interleave_q(nc.scalar.copy if b % 2 else nc.vector.tensor_copy, 1, b * P, (b + 1) * P)
         for b in range(QB):
@@ -248,7 +251,7 @@ def tile_attend_atb_decay_topk_kernel(tc, qT, k_words, k_scales, vT, dc, ls, lm,
         for b in range(QB):
             weigh(b)
         for c in range(2):
-            nc.scalar.copy(v_bf[0][:, c * P : (c + 1) * P, :], turn_v(c))
+            nc.scalar.copy(v_bf[0][:, c * P : (c + 1) * P, :].bitcast(F32), turn_v(c))
 
         rest_col = shared("rest_col", [P, QB], F32, 1)
         nc.scalar.activation(rest_col[:], lm_col[:], COPY, scale=-1.0, bias=1.0)
@@ -259,20 +262,23 @@ def tile_attend_atb_decay_topk_kernel(tc, qT, k_words, k_scales, vT, dc, ls, lm,
         def scale_local(b):
             nc.scalar.activation(local[b], pa_raw[b][:], COPY, scale=rest_col[:, b : b + 1])
 
-        for c in range(2, EB):
+        def last_tiles(c):
             gather_v(c)
             turned = turn_v(c)
             scale_local(c - 2)
-            nc.scalar.copy(v_bf[c - 1][:], turned)
-        scale_local(2)
-        scale_local(3)
+            nc.scalar.copy(v_bf[c - 1][:].bitcast(F32), turned)
+
+        last_tiles(2)
         quantize_y(0, NQ)
         quantize_v(0)
         sums = [products(0, (0, 1), 1) + products(0, (2, 3), 2)]
+        last_tiles(3)
+        scale_local(2)
+        scale_local(3)
         quantize_v(1)
-        sums.append(products(1, (0, 1, 2, 3), 3))
+        sums.append(products(1, (0, 1, 2, 3), 0))
         quantize_v(2)
-        sums.append(products(2, (0, 1), 7) + products(2, (2, 3), 0))
+        sums.append(products(2, (0, 1), 7) + products(2, (2, 3), 3))
 
         rows_out = out[0].rearrange("(p b) e -> p b e", b=QB)
         for g, (lo, hi) in enumerate(groups):

@@ -70,7 +70,8 @@ def tile_attend_atb_decay_topk_kernel(tc, qT, k_words, k_scales, vT, dc, ls, lm,
                 k_scales[:, 4 * quad : 4 * quad + 4, :].rearrange("o f t -> f o t").bitcast(I32),
             )
         dc_pool = shared("dc_pool", [P, T], F32, 10)
-        nc.gpsimd.memset(dc_pool[:], 0.0)
+        nc.gpsimd.memset(dc_pool[:, 0:1664], 0.0)
+        nc.vector.memset(dc_pool[:, 1664:T], 0.0)
         nc.scalar.dma_start(dc_pool[0:1, :], dc[0:1, :])
 
         scratch = stream.tile([P, SLOTS * T + 16], F32, name="scratch", offset=0)
@@ -92,14 +93,14 @@ def tile_attend_atb_decay_topk_kernel(tc, qT, k_words, k_scales, vT, dc, ls, lm,
             nc.sync.dma_start(raw[:], q_rows(o))
             q_raw.append(raw)
         us_t = stream.tile([P, PACK], F32, name="us_t", offset=4 * T * SLOTS)
-        nc.scalar.dma_start(us_t[:], us[0].rearrange("(p t) x -> p (t x)", t=PACK))
-        lm_col = stream.tile([P, QB], F32, name="lm_col", offset=4 * T * SLOTS + 32)
-        nc.scalar.dma_start(lm_col[:], lm[0].rearrange("(p b) x -> p (b x)", b=QB))
+        nc.sync.dma_start(us_t[:], us[0].rearrange("(p t) x -> p (t x)", t=PACK))
         v_pool = []
         for c in range(EB):
             pool_c = stream.tile([P, T], F32, name="v_pool%d" % c, offset=4 * T * (2 + c))
             nc.sync.dma_start(pool_c[:], vT[c * P : (c + 1) * P, :])
             v_pool.append(pool_c)
+        lm_col = stream.tile([P, QB], F32, name="lm_col", offset=4 * T * SLOTS + 32)
+        nc.sync.dma_start(lm_col[:], lm[0].rearrange("(p b) x -> p (b x)", b=QB))
         pa_raw = []
         for b in range(QB):
             raw = stream.tile([P, DV], F32, name="pa_raw%d" % b, offset=4 * T * (2 + EB) + 4 * DV * b)
@@ -164,7 +165,7 @@ def tile_attend_atb_decay_topk_kernel(tc, qT, k_words, k_scales, vT, dc, ls, lm,
         v_bf = [
             shared("v_bf0", [P, 2 * P, PACK], BF16, 3),
             reuse("v_bf1", [P, P, PACK], BF16, 6),
-            reuse("v_bf2", [P, P, PACK], BF16, 6, 4 * DV),
+            reuse("v_bf2", [P, P, PACK], BF16, 6, 3 * 4 * DV),
         ]
         v_code = [
             reuse("v_code0", [P, 2 * P], U32, 4, 2048),
@@ -241,7 +242,7 @@ def tile_attend_atb_decay_topk_kernel(tc, qT, k_words, k_scales, vT, dc, ls, lm,
             score_pass(score[b], b, 0)
             score_pass(score[b + 1], b + 1, 0)
         for b in range(QB):
-            interleave_q(nc.scalar.copy if b % 2 else nc.vector.tensor_copy, 1, b * P, (b + 1) * P)
+            interleave_q(nc.scalar.copy, 1, b * P, (b + 1) * P)
         for b in range(QB):
             quantize_q(1, b * P, (b + 1) * P)
             score_pass(score[b], b, 1)
@@ -255,26 +256,23 @@ def tile_attend_atb_decay_topk_kernel(tc, qT, k_words, k_scales, vT, dc, ls, lm,
 
         rest_col = shared("rest_col", [P, QB], F32, 1)
         nc.scalar.activation(rest_col[:], lm_col[:], COPY, scale=-1.0, bias=1.0)
-        local_head = tile("local_head", [P, 2, DV], F32)
-        local_tail = shared("local_tail", [P, 2, DV], F32, 3)
-        local = [local_head[:, 0, :], local_head[:, 1, :], local_tail[:, 0, :], local_tail[:, 1, :]]
+        local = [tile("local%d" % b, [P, DV], F32) for b in range(QB)]
 
         def scale_local(b):
-            nc.scalar.activation(local[b], pa_raw[b][:], COPY, scale=rest_col[:, b : b + 1])
+            nc.scalar.activation(local[b][:], pa_raw[b][:], COPY, scale=rest_col[:, b : b + 1])
 
-        def last_tiles(c):
+        def last_tiles(c, blocks):
             gather_v(c)
             turned = turn_v(c)
-            scale_local(c - 2)
+            for b in blocks:
+                scale_local(b)
             nc.scalar.copy(v_bf[c - 1][:].bitcast(F32), turned)
 
-        last_tiles(2)
+        last_tiles(2, (0,))
         quantize_y(0, NQ)
         quantize_v(0)
         sums = [products(0, (0, 1), 1) + products(0, (2, 3), 2)]
-        last_tiles(3)
-        scale_local(2)
-        scale_local(3)
+        last_tiles(3, (1, 2, 3))
         quantize_v(1)
         sums.append(products(1, (0, 1, 2, 3), 0))
         quantize_v(2)

@@ -1,6 +1,7 @@
 from contextlib import ExitStack
 
 import concourse.mybir as mybir
+from concourse.masks import make_identity
 
 F32 = mybir.dt.float32
 BF16 = mybir.dt.bfloat16
@@ -21,8 +22,7 @@ N, T, D, NQ, DV = 512, 2048, 1024, 512, 512
 PASSES = D // (P * PACK)
 QB = NQ // P
 EB = DV // P
-EARLY = (EB - 1) * P
-SLOTS = 3 + EB
+HALF = DV // 2
 
 FLOPS = 2 * N * NQ * D + 2 * N * NQ * DV
 BYTES = 4 * (D * NQ + P * T + DV * T + T + 2 * NQ + N + 2 * NQ * DV) + PASSES * 16 * T + 2 * P * N // 16
@@ -33,257 +33,203 @@ def tile_attend_atb_decay_topk_kernel(tc, qT, k_words, k_scales, vT, dc, ls, lm,
     with ExitStack() as ctx:
         sb = ctx.enter_context(tc.tile_pool(name="sb", bufs=1))
         stream = ctx.enter_context(tc.tile_pool(name="stream", bufs=1))
-        work = ctx.enter_context(tc.tile_pool(name="work", bufs=1))
         ps = ctx.enter_context(tc.psum_pool(name="ps", bufs=1))
 
         def tile(name, shape, dtype):
             return sb.tile(shape, dtype, name=name, align_bytes=64)
 
-        def shared(name, shape, dtype, place, skip=0):
-            return work.tile(shape, dtype, name=name, align_bytes=64, offset=4096 * place + skip)
-
-        def reuse(name, shape, dtype, slot, skip=0):
-            return stream.tile(shape, dtype, name=name, align_bytes=64, offset=4 * T * slot + skip)
+        def placed(name, shape, dtype, kib):
+            return stream.tile(shape, dtype, name=name, align_bytes=64, offset=1024 * kib)
 
         def bank(name, shape, number):
             return ps.tile(shape, F32, name=name, offset=2048 * number)
 
-        def q_rows(o):
-            return qT[0, o * 512 : (o + 1) * 512, :].rearrange("(p j) q -> p j q", j=PACK)
-
         offsets = sb.tile([P, N // 16], U16, name="offsets")
         nc.sync.dma_start(offsets[:], offs)
+        dc_pool = placed("dc_pool", [P, T], F32, 50)
+        nc.sync.dma_start(dc_pool[P - 1 : P, :], dc[0:1, :])
         k_pool = tile("k_pool", [P, T], I32)
         nc.sync.dma_start(k_pool[:], k_words[0].rearrange("p t b -> p (t b)").bitcast(I32))
 
-        rows = tile("rows", [P, P], F32)
-        nc.vector.memset(rows[:, 0:63], 0.0)
-        nc.vector.memset(rows[:, 63:P], 0.0)
-        nc.scalar.dma_start(rows[0:QB, :], ls[0, 0, :].rearrange("(b p) -> b p", p=P))
-        s_pool = shared("s_pool", [P, PASSES, T // 4], I32, 9)
-        s_words = s_pool[:].rearrange("p o w -> p (o w)")
-        nc.vector.memset(s_words[:, 0:511], 0)
-        nc.vector.memset(s_words[:, 511:1024], 0)
+        s_area = placed("s_area", [P, 42 * 256], I32, 0)
+        s_pool = s_area[:, 0 : T // 4]
+        nc.gpsimd.memset(s_pool, 0)
+        nc.gpsimd.memset(dc_pool[0 : P - 1, 0:512], 0.0)
+        nc.vector.memset(dc_pool[0 : P - 1, 512:T], 0.0)
         for quad in range(4):
-            nc.scalar.dma_start(
-                s_pool[32 * quad : 32 * quad + 4, :, :],
-                k_scales[:, 4 * quad : 4 * quad + 4, :].rearrange("o f t -> f o t").bitcast(I32),
+            nc.sync.dma_start(
+                s_area[32 * quad : 32 * quad + 8, 0 : T // 4],
+                k_scales[:, 4 * quad : 4 * quad + 4, :].bitcast(I32),
             )
-        dc_pool = shared("dc_pool", [P, T], F32, 10)
-        nc.gpsimd.memset(dc_pool[:, 0:1664], 0.0)
-        nc.vector.memset(dc_pool[:, 1664:T], 0.0)
-        nc.scalar.dma_start(dc_pool[0:1, :], dc[0:1, :])
+        q_raw = [tile("q_raw%d" % o, [P, PACK, NQ], F32) for o in range(PASSES)]
 
-        scratch = stream.tile([P, SLOTS * T + 16], F32, name="scratch", offset=0)
-        nc.gpsimd.memset(scratch[:, 0:P], 0.0)
-        ident = tile("ident", [P, P], F32)
-        nc.gpsimd.affine_select(
-            out=ident[:],
-            in_=scratch[:, 0:P],
-            compare_op=mybir.AluOpType.not_equal,
-            fill=1.0,
-            base=0,
-            pattern=[[-1, P]],
-            channel_multiplier=1,
-        )
+        def load_q(o):
+            nc.sync.dma_start(q_raw[o][:], qT[0, o * 512 : (o + 1) * 512, :].rearrange("(p j) q -> p j q", j=PACK))
 
-        q_raw = []
-        for o in range(PASSES):
-            raw = reuse("q_raw%d" % o, [P, PACK, NQ], F32, o)
-            nc.sync.dma_start(raw[:], q_rows(o))
-            q_raw.append(raw)
-        us_t = stream.tile([P, PACK], F32, name="us_t", offset=4 * T * SLOTS)
+        load_q(0)
+        ls_rows = tile("ls_rows", [P, P], F32)
+        nc.vector.memset(ls_rows[0 : P - QB, :], 0.0)
+        nc.sync.dma_start(ls_rows[P - QB : P, :], ls[0, 0, :].rearrange("(b p) -> b p", p=P))
+        load_q(1)
+        us_t = tile("us_t", [P, PACK], F32)
         nc.sync.dma_start(us_t[:], us[0].rearrange("(p t) x -> p (t x)", t=PACK))
+        lm_rows = tile("lm_rows", [P, P], F32)
+        nc.vector.memset(lm_rows[0 : P - QB, :], 0.0)
+        nc.sync.dma_start(lm_rows[P - QB : P, :], lm[0].rearrange("(b p) x -> b (p x)", p=P))
+
+        ident = tile("ident", [P, P], F32)
+        make_identity(nc, ident[:])
+
+        dc_row = tile("dc_row", [P, N], F32)
+        nc.vector.tensor_copy(dc_row[:], dc_pool[:].indirect(offsets[:]))
+        k_scale = [placed("k_scale0", [P, N], U8, 50), tile("k_scale1", [P, N], U8)]
+        nc.vector.tensor_copy(k_scale[0][:], s_pool.bitcast(U8).indirect(offsets[:]))
+        k_pair = placed("k_pair", [P, N], U32, 40)
+        nc.vector.tensor_copy(k_pair[:], k_pool[:].bitcast(U32).indirect(offsets[:]))
+        both, second = k_scale[0][:].bitcast(I32), k_scale[1][:].bitcast(I32)
+        nc.gpsimd.memset(second[96:P, :], 0)
+        for lo, count in ((0, 64), (64, 32), (96, 4)):
+            nc.sync.dma_start(second[lo : lo + count, :], both[lo + 4 : lo + 4 + count, :])
         v_pool = []
         for c in range(EB):
-            pool_c = stream.tile([P, T], F32, name="v_pool%d" % c, offset=4 * T * (2 + c))
+            pool_c = placed("v_pool%d" % c, [P, T], F32, 8 * c)
             nc.sync.dma_start(pool_c[:], vT[c * P : (c + 1) * P, :])
             v_pool.append(pool_c)
-        lm_col = stream.tile([P, QB], F32, name="lm_col", offset=4 * T * SLOTS + 32)
-        nc.sync.dma_start(lm_col[:], lm[0].rearrange("(p b) x -> p (b x)", b=QB))
         pa_raw = []
         for b in range(QB):
-            raw = stream.tile([P, DV], F32, name="pa_raw%d" % b, offset=4 * T * (2 + EB) + 4 * DV * b)
-            nc.sync.dma_start(raw[:], pa[0].rearrange("(p b) e -> p b e", b=QB)[:, b, :])
+            raw = placed("pa_raw%d" % b, [P, DV], F32, 32 + 2 * b)
+            nc.sync.dma_start(raw[:], pa[0, b * P : (b + 1) * P, :])
             pa_raw.append(raw)
-
-        cols_ps = bank("cols_ps", [P, P], 4)
-        nc.tensor.transpose(cols_ps[:], rows[:], ident[:])
-        neg_ls = tile("neg_ls", [P, QB], F32)
-        nc.scalar.activation(neg_ls[:], cols_ps[:, 0:QB], COPY, scale=-1.0)
-
-        k_pair = tile("k_pair", [P, N], U32)
-        nc.vector.tensor_copy(k_pair[:], k_pool[:].bitcast(U32).indirect(offsets[:]))
         k_code = tile("k_code", [P, PASSES, 2 * N], U8)
         nc.vector.tensor_copy(
             k_code[:].bitcast(U16), k_pair[:].bitcast(U16).rearrange("p (n o) -> p o n", o=PASSES)
         )
 
-        dc_row = tile("dc_row", [P, N], F32)
-        nc.vector.tensor_copy(dc_row[:], dc_pool[:].indirect(offsets[:]))
-        dc_ps = bank("dc_ps", [P, PACK, P], 5)
+        ls_ps = bank("ls_ps", [P, P], 7)
+        nc.tensor.transpose(ls_ps[:], ls_rows[:], ident[:])
+        neg_ls = tile("neg_ls", [P, QB], F32)
+        nc.scalar.activation(neg_ls[:], ls_ps[:, P - QB : P], COPY, scale=-1.0)
+
+        dc_ps = bank("dc_ps", [P, PACK, P], 6)
         for t in range(PACK):
             nc.tensor.transpose(dc_ps[:, t, :], dc_row[:, t::PACK], ident[:])
+        weight = tile("weight", [P, PACK], F32)
+        nc.vector.tensor_tensor(weight[:], dc_ps[:, :, P - 1], us_t[:], MULT)
 
-        k_scale = []
-        for o in range(PASSES):
-            plane = shared("k_scale%d" % o, [P, N], U8, 10 + o)
-            nc.vector.tensor_copy(plane[:], s_pool[:, o, :].bitcast(U8).indirect(offsets[:]))
-            k_scale.append(plane)
-
-        q_bf = [tile("q_bf0", [P, NQ, PACK], BF16), shared("q_bf1", [P, NQ, PACK], BF16, 0)]
         q_code = [
-            shared("q_code0", [P, NQ], U32, 9),
-            tile("q_code1", [P, NQ], U32),
+            [tile("q_code0_0", [P, 2 * P], U32), tile("q_code0_1", [P, 2 * P], U32)],
+            [tile("q_code1_0", [P, 2 * P], U32), placed("q_code1_1", [P, 2 * P], U32, 43)],
         ]
-        q_scale = [tile("q_scale%d" % o, [P, NQ], U8) for o in range(PASSES)]
+        q_scale = [[tile("q_scale%d_%d" % (o, h), [P, 2 * P], U8) for h in range(2)] for o in range(PASSES)]
 
-        def interleave_q(copy, o, lo, hi):
+        def interleave_q(copy, woven, o, lo):
+            hi = lo + woven.shape[1]
             copy(
-                q_bf[o][:, lo:hi, :].rearrange("p (c i) t -> p c t i", i=4),
+                woven[:].rearrange("p (c i) t -> p c t i", i=4),
                 q_raw[o][:, :, lo:hi].rearrange("p t (c i) -> p c t i", i=4),
             )
 
-        def quantize_q(o, lo, hi):
-            nc.vector.quantize_mx(
-                q_code[o][:, lo:hi].bitcast(FP8X4),
-                q_scale[o][:, lo:hi],
-                q_bf[o][:, lo:hi, :].rearrange("p q t -> p (q t)"),
-            )
+        def quantize(code, scale, woven):
+            nc.vector.quantize_mx(code.bitcast(FP8X4), scale, woven[:].rearrange("p q t -> p (q t)"))
 
-        prob = [
-            tile("prob0", [P, PACK, P], F32),
-            tile("prob1", [P, PACK, P], F32),
-            tile("prob2", [P, PACK, P], F32),
-            shared("prob3", [P, PACK, P], F32, 2, 1024),
-        ]
-        weight = shared("weight", [P, PACK], F32, 0, 2048)
-        y_bf = reuse("y_bf", [P, NQ, PACK], BF16, 3)
-        y_code = reuse("y_code", [P, NQ], U32, 4)
-        y_scale = tile("y_scale", [P, NQ], U8)
-        groups = ((0, 2 * P), (2 * P, 3 * P), (3 * P, DV))
-        v_bf = [
-            shared("v_bf0", [P, 2 * P, PACK], BF16, 3),
-            reuse("v_bf1", [P, P, PACK], BF16, 6),
-            reuse("v_bf2", [P, P, PACK], BF16, 6, 3 * 4 * DV),
-        ]
-        v_code = [
-            reuse("v_code0", [P, 2 * P], U32, 4, 2048),
-            reuse("v_code1", [P, P], U32, 5, 4096),
-            tile("v_code2", [P, P], U32),
-        ]
-        v_scale = [tile("v_scale%d" % g, [P, hi - lo], U8) for g, (lo, hi) in enumerate(groups)]
-        v_picked = [shared("v_picked%d" % c, [P, 2, P, 2], BF16, c, 1024 * (c == 2)) for c in range(EB)]
+        score = [bank("score%d" % b, [P, N], b) for b in range(QB)]
 
-        def gather_v(c):
-            nc.vector.tensor_copy(v_picked[c][:].rearrange("e u m i -> e m u i"), v_pool[c][:].indirect(offsets[:]))
-
-        def turn_v(c):
-            turned = bank("v_turned%d" % c, [P, 2, P], (3, 4, 5, 6)[c])
-            words = v_picked[c][:].rearrange("e u m i -> e (u m i)").bitcast(F32)
-            for u in range(2):
-                nc.tensor.transpose(turned[:, u, :], words[:, u * P : (u + 1) * P], ident[:])
-            return turned[:].rearrange("p u e -> p e u")
-
-        def quantize_v(g):
-            nc.vector.quantize_mx(
-                v_code[g][:].bitcast(FP8X4), v_scale[g][:], v_bf[g][:].rearrange("p e t -> p (e t)")
-            )
-
-        def score_pass(acc, b, o):
+        def score_pass(b, o):
             nc.tensor.matmul_mx(
-                acc[:],
-                lhsT=q_code[o][:, b * P : (b + 1) * P].bitcast(FP8X4),
-                lhsT_scale=q_scale[o][:, b * P : (b + 1) * P],
+                score[b][:],
+                lhsT=q_code[o][b // 2][:, (b % 2) * P : (b % 2 + 1) * P].bitcast(FP8X4),
+                lhsT_scale=q_scale[o][b // 2][:, (b % 2) * P : (b % 2 + 1) * P],
                 rhs=k_code[:, o, :].bitcast(FP4X4),
                 rhs_scale=k_scale[o][:],
                 start=(o == 0),
                 stop=(o == PASSES - 1),
             )
 
-        def weigh(b):
-            nc.scalar.activation(
-                prob[b][:], score[b][:].rearrange("q (m t) -> q t m", t=PACK), EXP, bias=neg_ls[:, b : b + 1]
+        for b in range(QB):
+            woven = placed("q_first%d" % b, [P, P, PACK], BF16, 58 + b % 3)
+            interleave_q(nc.scalar.copy if b < 3 else nc.vector.tensor_copy, woven, 0, b * P)
+            cols = slice((b % 2) * P, (b % 2 + 1) * P)
+            quantize(q_code[0][b // 2][:, cols], q_scale[0][b // 2][:, cols], woven)
+            score_pass(b, 0)
+        for b in range(2):
+            woven = placed("q_second%d" % b, [P, P, PACK], BF16, 42 + b)
+            interleave_q(nc.scalar.copy, woven, 1, b * P)
+            cols = slice(b * P, (b + 1) * P)
+            quantize(q_code[1][0][:, cols], q_scale[1][0][:, cols], woven)
+            score_pass(b, 1)
+        woven = tile("q_last", [P, 2 * P, PACK], BF16)
+        interleave_q(nc.vector.tensor_copy, woven, 1, 2 * P)
+        quantize(q_code[1][1][:], q_scale[1][1][:], woven)
+        score_pass(2, 1)
+        score_pass(3, 1)
+
+        y_bf = [placed("y_bf%d" % h, [P, 2 * P, PACK], BF16, 8 * h) for h in range(2)]
+        y_code = [placed("y_code%d" % h, [P, 2 * P], U32, 24 + h) for h in range(2)]
+        y_scale = [tile("y_scale%d" % h, [P, 2 * P], U8) for h in range(2)]
+        v_bf = [tile("v_bf%d" % g, [P, HALF, PACK], BF16) for g in range(2)]
+        v_code = [placed("v_code%d" % g, [P, HALF], U32, 26 + g) for g in range(2)]
+        v_scale = [tile("v_scale%d" % g, [P, HALF], U8) for g in range(2)]
+
+        def bring_v(c):
+            picked = placed("v_picked%d" % c, [P, 2, P, 2], BF16, 44 + c)
+            nc.vector.tensor_copy(picked[:].rearrange("e u m i -> e m u i"), v_pool[c][:].indirect(offsets[:]))
+            turned = bank("v_turned%d" % c, [P, 2, P], 2 if c == 0 else 7)
+            words = picked[:].rearrange("e u m i -> e (u m i)").bitcast(F32)
+            for u in range(2):
+                nc.tensor.transpose(turned[:, u, :], words[:, u * P : (u + 1) * P], ident[:])
+            nc.scalar.copy(
+                v_bf[c // 2][:, (c % 2) * P : (c % 2 + 1) * P, :].bitcast(F32), turned[:].rearrange("p u e -> p e u")
             )
-            turned = bank("p_turned%d" % b, [P, PACK, P], 4 + b)
+
+        def weigh(b):
+            prob = tile("prob%d" % b, [P, PACK, P], F32)
+            nc.scalar.activation(
+                prob[:], score[b][:].rearrange("q (m t) -> q t m", t=PACK), EXP, bias=neg_ls[:, b : b + 1]
+            )
+            turned = bank("p_turned%d" % b, [P, PACK, P], (4, 5, 6, 0)[b])
             for t in range(PACK):
-                nc.tensor.transpose(turned[:, t, :], prob[b][:, t, :], ident[:])
+                nc.tensor.transpose(turned[:, t, :], prob[:, t, :], ident[:])
             nc.vector.tensor_tensor(
-                y_bf[:].rearrange("p (g r) t -> p g r t", g=QB)[:, :, 32 * b : 32 * (b + 1), :],
-                turned[:].rearrange("p t (r g) -> p g r t", g=QB),
-                weight[:].unsqueeze(1).unsqueeze(1).to_broadcast([P, QB, 32, PACK]),
+                y_bf[b // 2][:, (b % 2) * P : (b % 2 + 1) * P, :],
+                turned[:].rearrange("p t q -> p q t"),
+                weight[:].unsqueeze(1).to_broadcast([P, P, PACK]),
                 MULT,
             )
 
-        def quantize_y(lo, hi):
-            nc.vector.quantize_mx(
-                y_code[:, lo:hi].bitcast(FP8X4), y_scale[:, lo:hi], y_bf[:, lo:hi, :].rearrange("p q t -> p (q t)")
+        for h in range(2):
+            bring_v(h)
+            weigh(2 * h)
+            weigh(2 * h + 1)
+        lm_ps = bank("lm_ps", [P, P], 3)
+        nc.tensor.transpose(lm_ps[:], lm_rows[:], ident[:])
+        lm_col = tile("lm_col", [P, QB], F32)
+        nc.scalar.copy(lm_col[:], lm_ps[:, P - QB : P])
+        rest_col = tile("rest_col", [P, QB], F32)
+        nc.scalar.activation(rest_col[:], lm_ps[:, P - QB : P], COPY, scale=-1.0, bias=1.0)
+        bring_v(2)
+        bring_v(3)
+
+        def product(acc, g, b):
+            nc.tensor.matmul_mx(
+                acc,
+                lhsT=y_code[b // 2][:, (b % 2) * P : (b % 2 + 1) * P].bitcast(FP8X4),
+                lhsT_scale=y_scale[b // 2][:, (b % 2) * P : (b % 2 + 1) * P],
+                rhs=v_code[g][:].bitcast(FP8X4),
+                rhs_scale=v_scale[g][:],
+                start=True,
+                stop=True,
             )
 
-        def products(g, blocks, number):
-            lo, hi = groups[g]
-            acc = bank("o%d_%d" % (g, blocks[0]), [P, len(blocks), hi - lo], number)
-            for j, b in enumerate(blocks):
-                nc.tensor.matmul_mx(
-                    acc[:, j, :],
-                    lhsT=y_code[:, b * P : (b + 1) * P].bitcast(FP8X4),
-                    lhsT_scale=y_scale[:, b * P : (b + 1) * P],
-                    rhs=v_code[g][:].bitcast(FP8X4),
-                    rhs_scale=v_scale[g][:],
-                    start=True,
-                    stop=True,
-                )
-            return [acc[:, j, :] for j in range(len(blocks))]
-
-        score = [bank("score%d" % b, [P, N], b) for b in range(QB)]
-        for b in range(0, QB, 2):
-            interleave_q(nc.scalar.copy, 0, b * P, (b + 2) * P)
-            quantize_q(0, b * P, (b + 2) * P)
-            score_pass(score[b], b, 0)
-            score_pass(score[b + 1], b + 1, 0)
+        sums = [bank("sum%d" % b, [P, DV], (1, 2, 3, 0)[b]) for b in range(QB)]
+        for h in range(2):
+            quantize(y_code[h][:], y_scale[h][:], y_bf[h])
+            quantize(v_code[h][:], v_scale[h][:], v_bf[h])
         for b in range(QB):
-            interleave_q(nc.scalar.copy, 1, b * P, (b + 1) * P)
+            for g in range(2):
+                product(sums[b][:, g * HALF : (g + 1) * HALF], g, b)
         for b in range(QB):
-            quantize_q(1, b * P, (b + 1) * P)
-            score_pass(score[b], b, 1)
-        nc.vector.tensor_tensor(weight[:], dc_ps[:, :, 0], us_t[:], MULT)
-        gather_v(0)
-        gather_v(1)
-        for b in range(QB):
-            weigh(b)
-        for c in range(2):
-            nc.scalar.copy(v_bf[0][:, c * P : (c + 1) * P, :].bitcast(F32), turn_v(c))
-
-        rest_col = shared("rest_col", [P, QB], F32, 1)
-        nc.scalar.activation(rest_col[:], lm_col[:], COPY, scale=-1.0, bias=1.0)
-        local = [tile("local%d" % b, [P, DV], F32) for b in range(QB)]
-
-        def scale_local(b):
-            nc.scalar.activation(local[b][:], pa_raw[b][:], COPY, scale=rest_col[:, b : b + 1])
-
-        def last_tiles(c, blocks):
-            gather_v(c)
-            turned = turn_v(c)
-            for b in blocks:
-                scale_local(b)
-            nc.scalar.copy(v_bf[c - 1][:].bitcast(F32), turned)
-
-        last_tiles(2, (0,))
-        quantize_y(0, NQ)
-        quantize_v(0)
-        sums = [products(0, (0, 1), 1) + products(0, (2, 3), 2)]
-        last_tiles(3, (1, 2, 3))
-        quantize_v(1)
-        sums.append(products(1, (0, 1, 2, 3), 0))
-        quantize_v(2)
-        sums.append(products(2, (0, 1), 7) + products(2, (2, 3), 3))
-
-        rows_out = out[0].rearrange("(p b) e -> p b e", b=QB)
-        for g, (lo, hi) in enumerate(groups):
-            res = tile("res%d" % g, [P, QB, hi - lo], F32)
-            for b in range(QB):
-                nc.vector.scalar_tensor_tensor(
-                    res[:, b, :], sums[g][b], lm_col[:, b : b + 1], local[b][:, lo:hi], MULT, ADD
-                )
-                if b % 2:
-                    nc.sync.dma_start(rows_out[:, b - 1 : b + 1, lo:hi], res[:, b - 1 : b + 1, :])
+            local = tile("local%d" % b, [P, DV], F32)
+            nc.scalar.activation(local[:], pa_raw[b][:], COPY, scale=rest_col[:, b : b + 1])
+            res = tile("res%d" % b, [P, DV], F32)
+            nc.vector.scalar_tensor_tensor(res[:], sums[b][:], lm_col[:, b : b + 1], local[:], MULT, ADD)
+            nc.sync.dma_start(out[0, b * P : (b + 1) * P, :], res[:])

@@ -171,12 +171,12 @@ def tile_attend_atb_decay_topk_kernel(tc, qT, k_words, k_scales, vT, dc, ls, lm,
         v_scale = [tile("v_scale%d" % g, [P, HALF], U8) for g in range(2)]
 
         def bring_v(c):
-            picked = placed("v_picked%d" % c, [P, 2, P, 2], BF16, 44 + c)
-            nc.vector.tensor_copy(picked[:].rearrange("e u m i -> e m u i"), v_pool[c][:].indirect(offsets[:]))
+            picked = placed("v_picked%d" % c, [P, N], BF16, 44 + c)
+            nc.vector.tensor_copy(picked[:], v_pool[c][:].indirect(offsets[:]))
             turned = bank("v_turned%d" % c, [P, 2, P], 2 if c == 0 else 7)
-            words = picked[:].rearrange("e u m i -> e (u m i)").bitcast(F32)
+            words = picked[:].bitcast(F32)
             for u in range(2):
-                nc.tensor.transpose(turned[:, u, :], words[:, u * P : (u + 1) * P], ident[:])
+                nc.tensor.transpose(turned[:, u, :], words[:, u::2], ident[:])
             nc.scalar.copy(
                 v_bf[c // 2][:, (c % 2) * P : (c % 2 + 1) * P, :].bitcast(F32), turned[:].rearrange("p u e -> p e u")
             )

@@ -163,17 +163,17 @@ def tile_attend_atb_decay_topk_kernel(tc, qT, k_words, k_scales, vT, dc, ls, lm,
         score_pass(2, 1)
         score_pass(3, 1)
 
-        y_bf = [placed("y_bf%d" % h, [P, 2 * P, PACK], BF16, 8 * h) for h in range(2)]
-        y_code = [placed("y_code%d" % h, [P, 2 * P], U32, 24 + h) for h in range(2)]
+        y_bf = [placed("y_bf0", [P, 2 * P, PACK], BF16, 0), tile("y_bf1", [P, 2 * P, PACK], BF16)]
+        y_code = [placed("y_code%d" % h, [P, 2 * P], U32, (8, 24)[h]) for h in range(2)]
         y_scale = [tile("y_scale%d" % h, [P, 2 * P], U8) for h in range(2)]
         v_bf = [tile("v_bf%d" % g, [P, HALF, PACK], BF16) for g in range(2)]
-        v_code = [placed("v_code%d" % g, [P, HALF], U32, 26 + g) for g in range(2)]
+        v_code = [placed("v_code0", [P, HALF], U32, 16), tile("v_code1", [P, HALF], U32)]
         v_scale = [tile("v_scale%d" % g, [P, HALF], U8) for g in range(2)]
 
         def bring_v(c):
             picked = placed("v_picked%d" % c, [P, N], BF16, 44 + c)
             nc.vector.tensor_copy(picked[:], v_pool[c][:].indirect(offsets[:]))
-            turned = bank("v_turned%d" % c, [P, 2, P], 2 if c == 0 else 7)
+            turned = bank("v_turned%d" % c, [P, 2, P], (2, 7, 4, 5)[c])
             words = picked[:].bitcast(F32)
             for u in range(2):
                 nc.tensor.transpose(turned[:, u, :], words[:, u::2], ident[:])
@@ -186,15 +186,20 @@ def tile_attend_atb_decay_topk_kernel(tc, qT, k_words, k_scales, vT, dc, ls, lm,
             nc.scalar.activation(
                 prob[:], score[b][:].rearrange("q (m t) -> q t m", t=PACK), EXP, bias=neg_ls[:, b : b + 1]
             )
-            turned = bank("p_turned%d" % b, [P, PACK, P], (4, 5, 6, 0)[b])
+            turned = bank("p_turned%d" % b, [P, PACK, P], (4, 5, 6, 7)[b])
             for t in range(PACK):
                 nc.tensor.transpose(turned[:, t, :], prob[:, t, :], ident[:])
-            nc.vector.tensor_tensor(
-                y_bf[b // 2][:, (b % 2) * P : (b % 2 + 1) * P, :],
-                turned[:].rearrange("p t q -> p q t"),
-                weight[:].unsqueeze(1).to_broadcast([P, P, PACK]),
-                MULT,
-            )
+            woven = y_bf[b // 2][:, (b % 2) * P : (b % 2 + 1) * P, :]
+            if b < 2:
+                nc.vector.tensor_tensor(
+                    woven,
+                    turned[:].rearrange("p t q -> p q t"),
+                    weight[:].unsqueeze(1).to_broadcast([P, P, PACK]),
+                    MULT,
+                )
+            else:
+                for t in range(PACK):
+                    nc.scalar.activation(woven[:, :, t], turned[:, t, :], COPY, scale=weight[:, t : t + 1])
 
         for h in range(2):
             bring_v(h)
@@ -206,8 +211,6 @@ def tile_attend_atb_decay_topk_kernel(tc, qT, k_words, k_scales, vT, dc, ls, lm,
         nc.scalar.copy(lm_col[:], lm_ps[:, P - QB : P])
         rest_col = tile("rest_col", [P, QB], F32)
         nc.scalar.activation(rest_col[:], lm_ps[:, P - QB : P], COPY, scale=-1.0, bias=1.0)
-        bring_v(2)
-        bring_v(3)
 
         def product(acc, g, b):
             nc.tensor.matmul_mx(
@@ -220,16 +223,42 @@ def tile_attend_atb_decay_topk_kernel(tc, qT, k_words, k_scales, vT, dc, ls, lm,
                 stop=True,
             )
 
-        sums = [bank("sum%d" % b, [P, DV], (1, 2, 3, 0)[b]) for b in range(QB)]
-        for h in range(2):
-            quantize(y_code[h][:], y_scale[h][:], y_bf[h])
-            quantize(v_code[h][:], v_scale[h][:], v_bf[h])
+        early = [bank("early%d" % h, [P, 2, HALF], h) for h in range(2)]
+        quantize(y_code[0][:], y_scale[0][:], y_bf[0])
+        bring_v(2)
+        quantize(v_code[0][:], v_scale[0][:], v_bf[0])
+        for b in range(2):
+            product(early[0][:, b, :], 0, b)
+        bring_v(3)
+        quantize(y_code[1][:], y_scale[1][:], y_bf[1])
+        for b in range(2):
+            product(early[1][:, b, :], 0, 2 + b)
+        local = []
         for b in range(QB):
-            for g in range(2):
-                product(sums[b][:, g * HALF : (g + 1) * HALF], g, b)
+            scaled = tile("local%d" % b, [P, DV], F32)
+            if b < 2:
+                nc.scalar.activation(scaled[:], pa_raw[b][:], COPY, scale=rest_col[:, b : b + 1])
+            else:
+                nc.gpsimd.tensor_scalar(scaled[:], pa_raw[b][:], rest_col[:, b : b + 1], 0.0, MULT, ADD)
+            local.append(scaled)
+        rows_out = out[0].rearrange("(b p) e -> p b e", p=P)
+        res = [tile("res%d" % g, [P, QB, HALF], F32) for g in range(2)]
+
+        def mix(g, b, acc):
+            cols = slice(g * HALF, (g + 1) * HALF)
+            nc.vector.scalar_tensor_tensor(res[g][:, b, :], acc, lm_col[:, b : b + 1], local[b][:, cols], MULT, ADD)
+            if b % 2:
+                nc.sync.dma_start(rows_out[:, b - 1 : b + 1, cols], res[g][:, b - 1 : b + 1, :])
+
+        for b in range(2):
+            mix(0, b, early[0][:, b, :])
+        quantize(v_code[1][:], v_scale[1][:], v_bf[1])
+        late = [bank("late%d" % b, [P, HALF], (2, 3, 6, 7)[b]) for b in range(QB)]
         for b in range(QB):
-            local = tile("local%d" % b, [P, DV], F32)
-            nc.scalar.activation(local[:], pa_raw[b][:], COPY, scale=rest_col[:, b : b + 1])
-            res = tile("res%d" % b, [P, DV], F32)
-            nc.vector.scalar_tensor_tensor(res[:], sums[b][:], lm_col[:, b : b + 1], local[:], MULT, ADD)
-            nc.sync.dma_start(out[0, b * P : (b + 1) * P, :], res[:])
+            product(late[b][:], 1, b)
+        mix(0, 2, early[1][:, 0, :])
+        mix(1, 0, late[0][:])
+        mix(1, 1, late[1][:])
+        mix(0, 3, early[1][:, 1, :])
+        mix(1, 2, late[2][:])
+        mix(1, 3, late[3][:])

@@ -56,7 +56,7 @@ def tile_attend_atb_decay_topk_kernel(tc, qT, k_words, k_scales, vT, dc, ls, lm,
         nc.gpsimd.memset(s_pool, 0)
         nc.gpsimd.memset(dc_pool[0 : P - 1, 0:512], 0.0)
         nc.vector.memset(dc_pool[0 : P - 1, 512:T], 0.0)
-        for quad in range(4):
+        for quad in (0, 2, 1, 3):
             nc.sync.dma_start(
                 s_area[32 * quad : 32 * quad + 8, 0 : T // 4],
                 k_scales[:, 4 * quad : 4 * quad + 4, :].bitcast(I32),
@@ -233,32 +233,31 @@ def tile_attend_atb_decay_topk_kernel(tc, qT, k_words, k_scales, vT, dc, ls, lm,
         quantize(y_code[1][:], y_scale[1][:], y_bf[1])
         for b in range(2):
             product(early[1][:, b, :], 0, 2 + b)
-        local = []
+        local = [[], []]
         for b in range(QB):
-            scaled = tile("local%d" % b, [P, DV], F32)
-            if b < 2:
-                nc.scalar.activation(scaled[:], pa_raw[b][:], COPY, scale=rest_col[:, b : b + 1])
-            else:
-                nc.gpsimd.tensor_scalar(scaled[:], pa_raw[b][:], rest_col[:, b : b + 1], 0.0, MULT, ADD)
-            local.append(scaled)
+            first = tile("local0_%d" % b, [P, HALF], F32)
+            nc.gpsimd.tensor_scalar(first[:], pa_raw[b][:, 0:HALF], rest_col[:, b : b + 1], 0.0, MULT, ADD)
+            second = tile("local1_%d" % b, [P, HALF], F32)
+            nc.scalar.activation(second[:], pa_raw[b][:, HALF:DV], COPY, scale=rest_col[:, b : b + 1])
+            local[0].append(first)
+            local[1].append(second)
         rows_out = out[0].rearrange("(b p) e -> p b e", p=P)
         res = [tile("res%d" % g, [P, QB, HALF], F32) for g in range(2)]
 
         def mix(g, b, acc):
             cols = slice(g * HALF, (g + 1) * HALF)
-            nc.vector.scalar_tensor_tensor(res[g][:, b, :], acc, lm_col[:, b : b + 1], local[b][:, cols], MULT, ADD)
-            if b % 2:
+            nc.vector.scalar_tensor_tensor(res[g][:, b, :], acc, lm_col[:, b : b + 1], local[g][b][:], MULT, ADD)
+            if g == 1 and b >= 2:
+                nc.sync.dma_start(rows_out[:, b, cols], res[g][:, b, :])
+            elif b % 2:
                 nc.sync.dma_start(rows_out[:, b - 1 : b + 1, cols], res[g][:, b - 1 : b + 1, :])
 
-        for b in range(2):
-            mix(0, b, early[0][:, b, :])
+        for b in range(QB - 1):
+            mix(0, b, early[b // 2][:, b % 2, :])
         quantize(v_code[1][:], v_scale[1][:], v_bf[1])
         late = [bank("late%d" % b, [P, HALF], (2, 3, 6, 7)[b]) for b in range(QB)]
         for b in range(QB):
             product(late[b][:], 1, b)
-        mix(0, 2, early[1][:, 0, :])
-        mix(1, 0, late[0][:])
-        mix(1, 1, late[1][:])
-        mix(0, 3, early[1][:, 1, :])
-        mix(1, 2, late[2][:])
-        mix(1, 3, late[3][:])
+        mix(0, QB - 1, early[1][:, 1, :])
+        for b in range(QB):
+            mix(1, b, late[b][:])

@@ -100,10 +100,9 @@ def tile_attend_atb_decay_topk_kernel(tc, qT, k_words, k_scales, vT, dc, ls, lm,
             raw = placed("pa_raw%d" % b, [P, DV], F32, 32 + 2 * b)
             nc.sync.dma_start(raw[:], pa[0, b * P : (b + 1) * P, :])
             pa_raw.append(raw)
-        k_code = tile("k_code", [P, PASSES, 2 * N], U8)
-        nc.vector.tensor_copy(
-            k_code[:].bitcast(U16), k_pair[:].bitcast(U16).rearrange("p (n o) -> p o n", o=PASSES)
-        )
+        k_code = [tile("k_code0", [P, 2 * N], U8), placed("k_code1", [P, 2 * N], U8, 59)]
+        k_halves = k_pair[:].bitcast(U16).rearrange("p (n o) -> p o n", o=PASSES)
+        nc.vector.tensor_copy(k_code[0][:].bitcast(U16), k_halves[:, 0, :])
 
         ls_ps = bank("ls_ps", [P, P], 7)
         nc.tensor.transpose(ls_ps[:], ls_rows[:], ident[:])
@@ -139,7 +138,7 @@ def tile_attend_atb_decay_topk_kernel(tc, qT, k_words, k_scales, vT, dc, ls, lm,
                 score[b][:],
                 lhsT=q_code[o][b // 2][:, (b % 2) * P : (b % 2 + 1) * P].bitcast(FP8X4),
                 lhsT_scale=q_scale[o][b // 2][:, (b % 2) * P : (b % 2 + 1) * P],
-                rhs=k_code[:, o, :].bitcast(FP4X4),
+                rhs=k_code[o][:].bitcast(FP4X4),
                 rhs_scale=k_scale[o][:],
                 start=(o == 0),
                 stop=(o == PASSES - 1),
@@ -151,23 +150,32 @@ def tile_attend_atb_decay_topk_kernel(tc, qT, k_words, k_scales, vT, dc, ls, lm,
             cols = slice((b % 2) * P, (b % 2 + 1) * P)
             quantize(q_code[0][b // 2][:, cols], q_scale[0][b // 2][:, cols], woven)
             score_pass(b, 0)
+        nc.vector.tensor_copy(k_code[1][:].bitcast(U16), k_halves[:, 1, :])
         for b in range(2):
             woven = placed("q_second%d" % b, [P, P, PACK], BF16, 42 + b)
             interleave_q(nc.scalar.copy, woven, 1, b * P)
             cols = slice(b * P, (b + 1) * P)
             quantize(q_code[1][0][:, cols], q_scale[1][0][:, cols], woven)
             score_pass(b, 1)
-        woven = tile("q_last", [P, 2 * P, PACK], BF16)
+        woven = placed("q_last", [P, 2 * P, PACK], BF16, 41)
         interleave_q(nc.vector.tensor_copy, woven, 1, 2 * P)
         quantize(q_code[1][1][:], q_scale[1][1][:], woven)
         score_pass(2, 1)
         score_pass(3, 1)
 
-        y_bf = [placed("y_bf0", [P, 2 * P, PACK], BF16, 0), tile("y_bf1", [P, 2 * P, PACK], BF16)]
-        y_code = [placed("y_code%d" % h, [P, 2 * P], U32, (8, 24)[h]) for h in range(2)]
-        y_scale = [tile("y_scale%d" % h, [P, 2 * P], U8) for h in range(2)]
+        y_bf = [
+            placed("y_bf0", [P, 2 * P, PACK], BF16, 0),
+            tile("y_bf2", [P, P, PACK], BF16),
+            placed("y_bf3", [P, P, PACK], BF16, 45),
+        ]
+        y_code = [
+            placed("y_code0", [P, 2 * P], U32, 8),
+            placed("y_code2", [P, P], U32, 18),
+            placed("y_code3", [P, P], U32, 24),
+        ]
+        y_scale = [tile("y_scale%d" % j, [P, w], U8) for j, w in enumerate((2 * P, P, P))]
         v_bf = [tile("v_bf%d" % g, [P, HALF, PACK], BF16) for g in range(2)]
-        v_code = [placed("v_code0", [P, HALF], U32, 16), tile("v_code1", [P, HALF], U32)]
+        v_code = [placed("v_code0", [P, HALF], U32, 16), placed("v_code1", [P, HALF], U32, 64)]
         v_scale = [tile("v_scale%d" % g, [P, HALF], U8) for g in range(2)]
 
         def bring_v(c):
@@ -186,10 +194,10 @@ def tile_attend_atb_decay_topk_kernel(tc, qT, k_words, k_scales, vT, dc, ls, lm,
             nc.scalar.activation(
                 prob[:], score[b][:].rearrange("q (m t) -> q t m", t=PACK), EXP, bias=neg_ls[:, b : b + 1]
             )
-            turned = bank("p_turned%d" % b, [P, PACK, P], (4, 5, 6, 7)[b])
+            turned = bank("p_turned%d" % b, [P, PACK, P], (4, 5, 6, 0)[b])
             for t in range(PACK):
                 nc.tensor.transpose(turned[:, t, :], prob[:, t, :], ident[:])
-            woven = y_bf[b // 2][:, (b % 2) * P : (b % 2 + 1) * P, :]
+            woven = y_bf[0][:, b * P : (b + 1) * P, :] if b < 2 else y_bf[b - 1][:]
             if b < 2:
                 nc.vector.tensor_tensor(
                     woven,
@@ -213,36 +221,45 @@ def tile_attend_atb_decay_topk_kernel(tc, qT, k_words, k_scales, vT, dc, ls, lm,
         nc.scalar.activation(rest_col[:], lm_ps[:, P - QB : P], COPY, scale=-1.0, bias=1.0)
 
         def product(acc, g, b):
+            j, cols = (0, slice(b * P, (b + 1) * P)) if b < 2 else (b - 1, slice(0, P))
             nc.tensor.matmul_mx(
                 acc,
-                lhsT=y_code[b // 2][:, (b % 2) * P : (b % 2 + 1) * P].bitcast(FP8X4),
-                lhsT_scale=y_scale[b // 2][:, (b % 2) * P : (b % 2 + 1) * P],
+                lhsT=y_code[j][:, cols].bitcast(FP8X4),
+                lhsT_scale=y_scale[j][:, cols],
                 rhs=v_code[g][:].bitcast(FP8X4),
                 rhs_scale=v_scale[g][:],
                 start=True,
                 stop=True,
             )
 
-        early = [bank("early%d" % h, [P, 2, HALF], h) for h in range(2)]
+        def warm_up(b, number, count):
+            unread = bank("unread%d" % b, [P, count, HALF], number)
+            for j in range(count):
+                product(unread[:, j, :], 0, b)
+
+        pair = bank("early_pair", [P, 2, HALF], 1)
+        early = [pair[:, 0, :], pair[:, 1, :], bank("early2", [P, HALF], 2), bank("early3", [P, HALF], 0)]
         quantize(y_code[0][:], y_scale[0][:], y_bf[0])
         bring_v(2)
-        quantize(v_code[0][:], v_scale[0][:], v_bf[0])
-        for b in range(2):
-            product(early[0][:, b, :], 0, b)
-        bring_v(3)
         quantize(y_code[1][:], y_scale[1][:], y_bf[1])
-        for b in range(2):
-            product(early[1][:, b, :], 0, 2 + b)
+        quantize(v_code[0][:], v_scale[0][:], v_bf[0])
+        for b in range(3):
+            product(early[b][:], 0, b)
+        warm_up(0, 3, 1)
+        bring_v(3)
+        quantize(y_code[2][:], y_scale[2][:], y_bf[2])
+        product(early[3][:], 0, 3)
+        warm_up(3, 4, 2)
         local = [[], []]
         for b in range(QB):
-            first = tile("local0_%d" % b, [P, HALF], F32)
+            first = placed("local0_%d" % b, [P, HALF], F32, 62 + b)
             nc.gpsimd.tensor_scalar(first[:], pa_raw[b][:, 0:HALF], rest_col[:, b : b + 1], 0.0, MULT, ADD)
             second = tile("local1_%d" % b, [P, HALF], F32)
             nc.scalar.activation(second[:], pa_raw[b][:, HALF:DV], COPY, scale=rest_col[:, b : b + 1])
             local[0].append(first)
             local[1].append(second)
         rows_out = out[0].rearrange("(b p) e -> p b e", p=P)
-        res = [tile("res%d" % g, [P, QB, HALF], F32) for g in range(2)]
+        res = [tile("res0", [P, QB, HALF], F32), placed("res1", [P, QB, HALF], F32, 65)]
 
         def mix(g, b, acc):
             cols = slice(g * HALF, (g + 1) * HALF)
@@ -253,11 +270,11 @@ def tile_attend_atb_decay_topk_kernel(tc, qT, k_words, k_scales, vT, dc, ls, lm,
                 nc.sync.dma_start(rows_out[:, b - 1 : b + 1, cols], res[g][:, b - 1 : b + 1, :])
 
         for b in range(QB - 1):
-            mix(0, b, early[b // 2][:, b % 2, :])
+            mix(0, b, early[b][:])
         quantize(v_code[1][:], v_scale[1][:], v_bf[1])
-        late = [bank("late%d" % b, [P, HALF], (2, 3, 6, 7)[b]) for b in range(QB)]
+        late = [bank("late%d" % b, [P, HALF], (3, 6, 7, 4)[b]) for b in range(QB)]
         for b in range(QB):
             product(late[b][:], 1, b)
-        mix(0, QB - 1, early[1][:, 1, :])
+        mix(0, QB - 1, early[QB - 1][:])
         for b in range(QB):
             mix(1, b, late[b][:])

@@ -232,11 +232,6 @@ def tile_attend_atb_decay_topk_kernel(tc, qT, k_words, k_scales, vT, dc, ls, lm,
                 stop=True,
             )
 
-        def warm_up(b, number, count):
-            unread = bank("unread%d" % b, [P, count, HALF], number)
-            for j in range(count):
-                product(unread[:, j, :], 0, b)
-
         pair = bank("early_pair", [P, 2, HALF], 1)
         early = [pair[:, 0, :], pair[:, 1, :], bank("early2", [P, HALF], 2), bank("early3", [P, HALF], 0)]
         quantize(y_code[0][:], y_scale[0][:], y_bf[0])
@@ -245,36 +240,42 @@ def tile_attend_atb_decay_topk_kernel(tc, qT, k_words, k_scales, vT, dc, ls, lm,
         quantize(v_code[0][:], v_scale[0][:], v_bf[0])
         for b in range(3):
             product(early[b][:], 0, b)
-        warm_up(0, 3, 1)
+        scaled_sum = [placed("scaled_sum%d" % b, [P, HALF], F32, 62 + b) for b in range(QB)]
+
+        def scale_sum(b):
+            nc.scalar.activation(scaled_sum[b][:], early[b][:], COPY, scale=lm_col[:, b : b + 1])
+
+        for b in range(3):
+            scale_sum(b)
         bring_v(3)
         quantize(y_code[2][:], y_scale[2][:], y_bf[2])
         product(early[3][:], 0, 3)
-        warm_up(3, 4, 2)
-        local = [[], []]
+        scale_sum(3)
+        local = []
         for b in range(QB):
-            first = placed("local0_%d" % b, [P, HALF], F32, 62 + b)
-            nc.gpsimd.tensor_scalar(first[:], pa_raw[b][:, 0:HALF], rest_col[:, b : b + 1], 0.0, MULT, ADD)
-            second = tile("local1_%d" % b, [P, HALF], F32)
-            nc.scalar.activation(second[:], pa_raw[b][:, HALF:DV], COPY, scale=rest_col[:, b : b + 1])
-            local[0].append(first)
-            local[1].append(second)
+            scaled = tile("local%d" % b, [P, HALF], F32)
+            nc.scalar.activation(scaled[:], pa_raw[b][:, HALF:DV], COPY, scale=rest_col[:, b : b + 1])
+            local.append(scaled)
         rows_out = out[0].rearrange("(b p) e -> p b e", p=P)
         res = [tile("res0", [P, QB, HALF], F32), placed("res1", [P, QB, HALF], F32, 65)]
 
-        def mix(g, b, acc):
-            cols = slice(g * HALF, (g + 1) * HALF)
-            nc.vector.scalar_tensor_tensor(res[g][:, b, :], acc, lm_col[:, b : b + 1], local[g][b][:], MULT, ADD)
-            if g == 1 and b >= 2:
-                nc.sync.dma_start(rows_out[:, b, cols], res[g][:, b, :])
-            elif b % 2:
-                nc.sync.dma_start(rows_out[:, b - 1 : b + 1, cols], res[g][:, b - 1 : b + 1, :])
+        def mix_first(b):
+            nc.vector.scalar_tensor_tensor(
+                res[0][:, b, :], pa_raw[b][:, 0:HALF], rest_col[:, b : b + 1], scaled_sum[b][:], MULT, ADD
+            )
+            if b % 2:
+                nc.sync.dma_start(rows_out[:, b - 1 : b + 1, 0:HALF], res[0][:, b - 1 : b + 1, :])
 
         for b in range(QB - 1):
-            mix(0, b, early[b][:])
+            mix_first(b)
         quantize(v_code[1][:], v_scale[1][:], v_bf[1])
         late = [bank("late%d" % b, [P, HALF], (3, 6, 7, 4)[b]) for b in range(QB)]
         for b in range(QB):
             product(late[b][:], 1, b)
-        mix(0, QB - 1, early[QB - 1][:])
+        mix_first(QB - 1)
         for b in range(QB):
-            mix(1, b, late[b][:])
+            nc.vector.scalar_tensor_tensor(res[1][:, b, :], late[b][:], lm_col[:, b : b + 1], local[b][:], MULT, ADD)
+            if b >= 2:
+                nc.sync.dma_start(rows_out[:, b, HALF:DV], res[1][:, b, :])
+            elif b == 1:
+                nc.sync.dma_start(rows_out[:, 0:2, HALF:DV], res[1][:, 0:2, :])

@@ -46,179 +46,174 @@ def tile_attend_atb_decay_topk_kernel(tc, qT, k_words, k_scales, vT, dc, ls, lm,
 
         offsets = sb.tile([P, N // 16], U16, name="offsets")
         nc.sync.dma_start(offsets[:], offs)
-        dc_pool = placed("dc_pool", [P, T], F32, 50)
+        s_area = placed("s_area", [P, 49 * 256], I32, 0)
+        s_pool = s_area[:, 0 : T // 4]
+        nc.sync.dma_start(s_area[0:32, 0 : T // 4], k_scales.rearrange("o f t -> f o t").bitcast(I32))
+        dc_pool = tile("dc_pool", [P, T], F32)
         nc.sync.dma_start(dc_pool[P - 1 : P, :], dc[0:1, :])
         k_pool = tile("k_pool", [P, T], I32)
         nc.sync.dma_start(k_pool[:], k_words[0].rearrange("p t b -> p (t b)").bitcast(I32))
-
-        s_area = placed("s_area", [P, 42 * 256], I32, 0)
-        s_pool = s_area[:, 0 : T // 4]
-        nc.gpsimd.memset(s_pool, 0)
-        nc.gpsimd.memset(dc_pool[0 : P - 1, 0:512], 0.0)
-        nc.vector.memset(dc_pool[0 : P - 1, 512:T], 0.0)
-        for quad in (0, 2, 1, 3):
-            nc.sync.dma_start(
-                s_area[32 * quad : 32 * quad + 8, 0 : T // 4],
-                k_scales[:, 4 * quad : 4 * quad + 4, :].bitcast(I32),
-            )
-        q_raw = [tile("q_raw%d" % o, [P, PACK, NQ], F32) for o in range(PASSES)]
+        ls_rows = tile("ls_rows", [P, P], F32)
+        nc.sync.dma_start(ls_rows[P - QB : P, :], ls[0, 0, :].rearrange("(b p) -> b p", p=P))
+        q_raw = [tile("q_raw0", [P, PACK, NQ], F32), placed("q_raw1", [P, PACK, NQ], F32, 0)]
 
         def load_q(o):
             nc.sync.dma_start(q_raw[o][:], qT[0, o * 512 : (o + 1) * 512, :].rearrange("(p j) q -> p j q", j=PACK))
 
         load_q(0)
-        ls_rows = tile("ls_rows", [P, P], F32)
-        nc.vector.memset(ls_rows[0 : P - QB, :], 0.0)
-        nc.sync.dma_start(ls_rows[P - QB : P, :], ls[0, 0, :].rearrange("(b p) -> b p", p=P))
-        load_q(1)
-        us_t = tile("us_t", [P, PACK], F32)
-        nc.sync.dma_start(us_t[:], us[0].rearrange("(p t) x -> p (t x)", t=PACK))
-        lm_rows = tile("lm_rows", [P, P], F32)
-        nc.vector.memset(lm_rows[0 : P - QB, :], 0.0)
-        nc.sync.dma_start(lm_rows[P - QB : P, :], lm[0].rearrange("(b p) x -> b (p x)", p=P))
-
+        nc.gpsimd.memset(s_area[32:64, 0 : T // 4], 0)
+        nc.gpsimd.memset(s_area[64:P, 0 : T // 4], 0)
+        nc.vector.memset(dc_pool[0 : P - 1, :], 0.0)
         ident = tile("ident", [P, P], F32)
         make_identity(nc, ident[:])
+        k_scale = tile("k_scale", [P, PASSES * N // 4], I32)
+        nc.gpsimd.memset(k_scale[:], 0)
+        nc.gpsimd.memset(ls_rows[0 : P - QB, :], 0.0)
 
-        dc_row = tile("dc_row", [P, N], F32)
-        nc.vector.tensor_copy(dc_row[:], dc_pool[:].indirect(offsets[:]))
-        k_scale = [placed("k_scale0", [P, N], U8, 50), tile("k_scale1", [P, N], U8)]
-        nc.vector.tensor_copy(k_scale[0][:], s_pool.bitcast(U8).indirect(offsets[:]))
-        k_pair = placed("k_pair", [P, N], U32, 40)
-        nc.vector.tensor_copy(k_pair[:], k_pool[:].bitcast(U32).indirect(offsets[:]))
-        both, second = k_scale[0][:].bitcast(I32), k_scale[1][:].bitcast(I32)
-        nc.gpsimd.memset(second[96:P, :], 0)
-        for lo, count in ((0, 64), (64, 32), (96, 4)):
-            nc.sync.dma_start(second[lo : lo + count, :], both[lo + 4 : lo + 4 + count, :])
-        v_pool = []
-        for c in range(EB):
-            pool_c = placed("v_pool%d" % c, [P, T], F32, 8 * c)
-            nc.sync.dma_start(pool_c[:], vT[c * P : (c + 1) * P, :])
-            v_pool.append(pool_c)
+        s_picked = tile("s_picked", [P, N], U8)
+        nc.vector.tensor_copy(s_picked[:], s_pool.bitcast(U8).indirect(offsets[:]))
+        for quad in range(4):
+            nc.sync.dma_start(
+                k_scale[32 * quad : 32 * quad + 4, :].rearrange("p (o n) -> p o n", o=PASSES),
+                s_picked[8 * quad : 8 * quad + 8, :].bitcast(I32),
+            )
+        load_q(1)
+        us_t = placed("us_t", [P, PACK], F32, 48)
+        nc.sync.dma_start(us_t[:], us[0].rearrange("(p t) x -> p (t x)", t=PACK))
+        v_pool = [placed("v_pool%d" % c, [P, T], F32, 8 + 8 * c) for c in range(EB)]
+        nc.sync.dma_start(v_pool[0][:], vT[0:P, :])
+        lm_rows = stream.tile([P, P], F32, name="lm_rows", align_bytes=64, offset=48 * 1024 + 512)
+        nc.sync.dma_start(lm_rows[P - QB : P, :], lm[0].rearrange("(b p) x -> b (p x)", p=P))
+        for c in range(1, EB):
+            nc.sync.dma_start(v_pool[c][:], vT[c * P : (c + 1) * P, :])
         pa_raw = []
         for b in range(QB):
-            raw = placed("pa_raw%d" % b, [P, DV], F32, 32 + 2 * b)
+            raw = placed("pa_raw%d" % b, [P, DV], F32, 40 + 2 * b)
             nc.sync.dma_start(raw[:], pa[0, b * P : (b + 1) * P, :])
             pa_raw.append(raw)
-        k_code = [tile("k_code0", [P, 2 * N], U8), placed("k_code1", [P, 2 * N], U8, 59)]
+
+        dc_row = tile("dc_row", [P, N], F32)
+        nc.vector.tensor_copy(dc_row[:, 0 : N // 2], dc_pool[:].indirect(offsets[:, 0 : N // 32]))
+        k_pair = tile("k_pair", [P, N], U32)
+        nc.vector.tensor_copy(k_pair[:], k_pool[:].bitcast(U32).indirect(offsets[:]))
+        k_code = [tile("k_code%d" % o, [P, 2 * N], U8) for o in range(PASSES)]
         k_halves = k_pair[:].bitcast(U16).rearrange("p (n o) -> p o n", o=PASSES)
-        nc.vector.tensor_copy(k_code[0][:].bitcast(U16), k_halves[:, 0, :])
+        for o in range(PASSES):
+            nc.vector.tensor_copy(k_code[o][:].bitcast(U16), k_halves[:, o, :])
+        nc.vector.memset(lm_rows[0 : P - QB, :], 0.0)
 
         ls_ps = bank("ls_ps", [P, P], 7)
         nc.tensor.transpose(ls_ps[:], ls_rows[:], ident[:])
         neg_ls = tile("neg_ls", [P, QB], F32)
         nc.scalar.activation(neg_ls[:], ls_ps[:, P - QB : P], COPY, scale=-1.0)
 
-        dc_ps = bank("dc_ps", [P, PACK, P], 6)
-        for t in range(PACK):
-            nc.tensor.transpose(dc_ps[:, t, :], dc_row[:, t::PACK], ident[:])
-        weight = tile("weight", [P, PACK], F32)
-        nc.vector.tensor_tensor(weight[:], dc_ps[:, :, P - 1], us_t[:], MULT)
-
-        q_code = [
-            [tile("q_code0_0", [P, 2 * P], U32), tile("q_code0_1", [P, 2 * P], U32)],
-            [tile("q_code1_0", [P, 2 * P], U32), placed("q_code1_1", [P, 2 * P], U32, 43)],
-        ]
-        q_scale = [[tile("q_scale%d_%d" % (o, h), [P, 2 * P], U8) for h in range(2)] for o in range(PASSES)]
-
-        def interleave_q(copy, woven, o, lo):
-            hi = lo + woven.shape[1]
-            copy(
-                woven[:].rearrange("p (c i) t -> p c t i", i=4),
-                q_raw[o][:, :, lo:hi].rearrange("p t (c i) -> p c t i", i=4),
-            )
-
         def quantize(code, scale, woven):
             nc.vector.quantize_mx(code.bitcast(FP8X4), scale, woven[:].rearrange("p q t -> p (q t)"))
 
         score = [bank("score%d" % b, [P, N], b) for b in range(QB)]
-
-        def score_pass(b, o):
-            nc.tensor.matmul_mx(
-                score[b][:],
-                lhsT=q_code[o][b // 2][:, (b % 2) * P : (b % 2 + 1) * P].bitcast(FP8X4),
-                lhsT_scale=q_scale[o][b // 2][:, (b % 2) * P : (b % 2 + 1) * P],
-                rhs=k_code[o][:].bitcast(FP4X4),
-                rhs_scale=k_scale[o][:],
-                start=(o == 0),
-                stop=(o == PASSES - 1),
-            )
-
-        for b in range(QB):
-            woven = placed("q_first%d" % b, [P, P, PACK], BF16, 58 + b % 3)
-            interleave_q(nc.scalar.copy if b < 3 else nc.vector.tensor_copy, woven, 0, b * P)
-            cols = slice((b % 2) * P, (b % 2 + 1) * P)
-            quantize(q_code[0][b // 2][:, cols], q_scale[0][b // 2][:, cols], woven)
-            score_pass(b, 0)
-        nc.vector.tensor_copy(k_code[1][:].bitcast(U16), k_halves[:, 1, :])
-        for b in range(2):
-            woven = placed("q_second%d" % b, [P, P, PACK], BF16, 42 + b)
-            interleave_q(nc.scalar.copy, woven, 1, b * P)
-            cols = slice(b * P, (b + 1) * P)
-            quantize(q_code[1][0][:, cols], q_scale[1][0][:, cols], woven)
-            score_pass(b, 1)
-        woven = placed("q_last", [P, 2 * P, PACK], BF16, 41)
-        interleave_q(nc.vector.tensor_copy, woven, 1, 2 * P)
-        quantize(q_code[1][1][:], q_scale[1][1][:], woven)
-        score_pass(2, 1)
-        score_pass(3, 1)
+        shares = [(b, 1, nc.vector.tensor_copy if b < 2 else nc.scalar.copy) for b in range(QB)]
+        for o in range(PASSES):
+            woven = []
+            for first, count, copy in shares:
+                if (o, first) == (0, 3):
+                    part = dc_row[:, N // 2 : N].bitcast(BF16).rearrange("p (q t) -> p q t", t=PACK)
+                else:
+                    part = tile("q_woven%d_%d" % (o, first), [P, count * P, PACK], BF16)[:]
+                copy(
+                    part.rearrange("p (c i) t -> p c t i", i=4),
+                    q_raw[o][:, :, first * P : (first + count) * P].rearrange("p t (c i) -> p c t i", i=4),
+                )
+                woven.append(part)
+            for (first, count, copy), part in zip(shares, woven):
+                code = tile("q_code%d_%d" % (o, first), [P, count * P], U32)
+                scale = tile("q_scale%d_%d" % (o, first), [P, count * P], U8)
+                quantize(code[:], scale[:], part)
+                for j in range(count):
+                    nc.tensor.matmul_mx(
+                        score[first + j][:],
+                        lhsT=code[:, j * P : (j + 1) * P].bitcast(FP8X4),
+                        lhsT_scale=scale[:, j * P : (j + 1) * P],
+                        rhs=k_code[o][:].bitcast(FP4X4),
+                        rhs_scale=k_scale[:].bitcast(U8)[:, o * N : (o + 1) * N],
+                        start=(o == 0),
+                        stop=(o == PASSES - 1),
+                    )
+            if o == 0:
+                nc.vector.tensor_copy(dc_row[:, N // 2 : N], dc_pool[:].indirect(offsets[:, N // 32 : N // 16]))
+        dc_ps = bank("dc_ps", [P, PACK, P], 6)
+        for t in range(PACK):
+            nc.tensor.transpose(dc_ps[:, t, :], dc_row[:, t::PACK], ident[:])
+        weight = placed("weight", [P, PACK], F32, 2)
+        nc.vector.tensor_tensor(weight[:], dc_ps[:, :, P - 1], us_t[:], MULT)
 
         y_bf = [
-            placed("y_bf0", [P, 2 * P, PACK], BF16, 0),
-            tile("y_bf2", [P, P, PACK], BF16),
-            placed("y_bf3", [P, P, PACK], BF16, 45),
+            placed("y_bf0", [P, 2 * P, PACK], BF16, 8),
+            placed("y_bf1", [P, P, PACK], BF16, 60),
+            placed("y_bf2", [P, P, PACK], BF16, 61),
         ]
         y_code = [
-            placed("y_code0", [P, 2 * P], U32, 8),
-            placed("y_code2", [P, P], U32, 18),
-            placed("y_code3", [P, P], U32, 24),
+            placed("y_code0", [P, 2 * P], U32, 16),
+            placed("y_code1", [P, P], U32, 24),
+            placed("y_code2", [P, P], U32, 25),
         ]
         y_scale = [tile("y_scale%d" % j, [P, w], U8) for j, w in enumerate((2 * P, P, P))]
-        v_bf = [tile("v_bf%d" % g, [P, HALF, PACK], BF16) for g in range(2)]
-        v_code = [placed("v_code0", [P, HALF], U32, 16), placed("v_code1", [P, HALF], U32, 64)]
+        v_bf = [placed("v_bf0", [P, HALF, PACK], BF16, 58), tile("v_bf1", [P, HALF, PACK], BF16)]
+        v_code = [placed("v_code0", [P, HALF], U32, 26), placed("v_code1", [P, HALF], U32, 64)]
         v_scale = [tile("v_scale%d" % g, [P, HALF], U8) for g in range(2)]
 
-        def bring_v(c):
-            picked = placed("v_picked%d" % c, [P, N], BF16, 44 + c)
-            nc.vector.tensor_copy(picked[:], v_pool[c][:].indirect(offsets[:]))
-            turned = bank("v_turned%d" % c, [P, 2, P], (2, 7, 4, 5)[c])
-            words = picked[:].bitcast(F32)
+        def gather_v(c):
+            picked = placed("v_picked%d" % c, [P, (1, 1, 1, 4)[c] * N], BF16, (0, 52, 56, 58)[c])[:, 0:N]
+            nc.vector.tensor_copy(picked, v_pool[c][:].indirect(offsets[:]))
+            return picked
+
+        def turn_v(c, picked):
+            turned = bank("v_turned%d" % c, [P, 2, P], (1, 3, 2, 0)[c])
+            words = picked.bitcast(F32)
             for u in range(2):
                 nc.tensor.transpose(turned[:, u, :], words[:, u::2], ident[:])
             nc.scalar.copy(
                 v_bf[c // 2][:, (c % 2) * P : (c % 2 + 1) * P, :].bitcast(F32), turned[:].rearrange("p u e -> p e u")
             )
 
-        def weigh(b):
-            prob = tile("prob%d" % b, [P, PACK, P], F32)
+        def turn_p(b):
+            prob = placed("prob%d" % b, [P, PACK, P], F32, 50 + 2 * b)
             nc.scalar.activation(
                 prob[:], score[b][:].rearrange("q (m t) -> q t m", t=PACK), EXP, bias=neg_ls[:, b : b + 1]
             )
-            turned = bank("p_turned%d" % b, [P, PACK, P], (4, 5, 6, 0)[b])
+            turned = bank("p_turned%d" % b, [P, PACK, P], 4 + b)
             for t in range(PACK):
                 nc.tensor.transpose(turned[:, t, :], prob[:, t, :], ident[:])
-            woven = y_bf[0][:, b * P : (b + 1) * P, :] if b < 2 else y_bf[b - 1][:]
-            if b < 2:
-                nc.vector.tensor_tensor(
-                    woven,
-                    turned[:].rearrange("p t q -> p q t"),
-                    weight[:].unsqueeze(1).to_broadcast([P, P, PACK]),
-                    MULT,
-                )
-            else:
-                for t in range(PACK):
-                    nc.scalar.activation(woven[:, :, t], turned[:, t, :], COPY, scale=weight[:, t : t + 1])
+            return turned
 
-        for h in range(2):
-            bring_v(h)
-            weigh(2 * h)
-            weigh(2 * h + 1)
-        lm_ps = bank("lm_ps", [P, P], 3)
+        def weigh(woven, turned):
+            nc.vector.tensor_tensor(
+                woven,
+                turned[:].rearrange("p t q -> p q t"),
+                weight[:].unsqueeze(1).to_broadcast([P, P, PACK]),
+                MULT,
+            )
+
+        picked0 = gather_v(0)
+        p_turned = [turn_p(b) for b in range(QB)]
+        lm_ps = bank("lm_ps", [P, P], 0)
         nc.tensor.transpose(lm_ps[:], lm_rows[:], ident[:])
+        weigh(y_bf[0][:, 0:P, :], p_turned[0])
+        weigh(y_bf[0][:, P : 2 * P, :], p_turned[1])
+        turn_v(0, picked0)
+        picked1 = gather_v(1)
+        quantize(y_code[0][:], y_scale[0][:], y_bf[0])
+        weigh(y_bf[1][:], p_turned[2])
+        for t in range(PACK):
+            nc.scalar.activation(y_bf[2][:, :, t], p_turned[3][:, t, :], COPY, scale=weight[:, t : t + 1])
+        turn_v(1, picked1)
         lm_col = tile("lm_col", [P, QB], F32)
         nc.scalar.copy(lm_col[:], lm_ps[:, P - QB : P])
         rest_col = tile("rest_col", [P, QB], F32)
         nc.scalar.activation(rest_col[:], lm_ps[:, P - QB : P], COPY, scale=-1.0, bias=1.0)
+        turn_v(2, gather_v(2))
+        quantize(y_code[1][:], y_scale[1][:], y_bf[1])
+        quantize(y_code[2][:], y_scale[2][:], y_bf[2])
+        quantize(v_code[0][:], v_scale[0][:], v_bf[0])
 
         def product(acc, g, b):
             j, cols = (0, slice(b * P, (b + 1) * P)) if b < 2 else (b - 1, slice(0, P))
@@ -232,32 +227,17 @@ def tile_attend_atb_decay_topk_kernel(tc, qT, k_words, k_scales, vT, dc, ls, lm,
                 stop=True,
             )
 
-        pair = bank("early_pair", [P, 2, HALF], 1)
-        early = [pair[:, 0, :], pair[:, 1, :], bank("early2", [P, HALF], 2), bank("early3", [P, HALF], 0)]
-        quantize(y_code[0][:], y_scale[0][:], y_bf[0])
-        bring_v(2)
-        quantize(y_code[1][:], y_scale[1][:], y_bf[1])
-        quantize(v_code[0][:], v_scale[0][:], v_bf[0])
-        for b in range(3):
-            product(early[b][:], 0, b)
         scaled_sum = [placed("scaled_sum%d" % b, [P, HALF], F32, 62 + b) for b in range(QB)]
-
-        def scale_sum(b):
-            nc.scalar.activation(scaled_sum[b][:], early[b][:], COPY, scale=lm_col[:, b : b + 1])
-
-        for b in range(3):
-            scale_sum(b)
-        bring_v(3)
-        quantize(y_code[2][:], y_scale[2][:], y_bf[2])
-        product(early[3][:], 0, 3)
-        scale_sum(3)
-        local = []
         for b in range(QB):
-            scaled = tile("local%d" % b, [P, HALF], F32)
-            nc.scalar.activation(scaled[:], pa_raw[b][:, HALF:DV], COPY, scale=rest_col[:, b : b + 1])
-            local.append(scaled)
+            early = bank("early%d" % b, [P, HALF], 4 + b)
+            product(early[:], 0, b)
+            nc.scalar.activation(scaled_sum[b][:], early[:], COPY, scale=lm_col[:, b : b + 1])
+        turn_v(3, gather_v(3))
+        local = placed("local", [P, QB, HALF], F32, 58)
+        for b in range(QB):
+            nc.scalar.activation(local[:, b, :], pa_raw[b][:, HALF:DV], COPY, scale=rest_col[:, b : b + 1])
         rows_out = out[0].rearrange("(b p) e -> p b e", p=P)
-        res = [tile("res0", [P, QB, HALF], F32), placed("res1", [P, QB, HALF], F32, 65)]
+        res = [placed("res0", [P, QB, HALF], F32, 32), placed("res1", [P, QB, HALF], F32, 65)]
 
         def mix_first(b):
             nc.vector.scalar_tensor_tensor(
@@ -269,12 +249,12 @@ def tile_attend_atb_decay_topk_kernel(tc, qT, k_words, k_scales, vT, dc, ls, lm,
         for b in range(QB - 1):
             mix_first(b)
         quantize(v_code[1][:], v_scale[1][:], v_bf[1])
-        late = [bank("late%d" % b, [P, HALF], (3, 6, 7, 4)[b]) for b in range(QB)]
+        late = [bank("late%d" % b, [P, HALF], (1, 3, 2, 0)[b]) for b in range(QB)]
         for b in range(QB):
             product(late[b][:], 1, b)
         mix_first(QB - 1)
         for b in range(QB):
-            nc.vector.scalar_tensor_tensor(res[1][:, b, :], late[b][:], lm_col[:, b : b + 1], local[b][:], MULT, ADD)
+            nc.vector.scalar_tensor_tensor(res[1][:, b, :], late[b][:], lm_col[:, b : b + 1], local[:, b, :], MULT, ADD)
             if b >= 2:
                 nc.sync.dma_start(rows_out[:, b, HALF:DV], res[1][:, b, :])
             elif b == 1:

@@ -53,28 +53,28 @@ def tile_attend_atb_decay_topk_kernel(tc, qT, k_words, k_scales, vT, dc, ls, lm,
         nc.sync.dma_start(dc_pool[P - 1 : P, :], dc[0:1, :])
         k_pool = tile("k_pool", [P, T], I32)
         nc.sync.dma_start(k_pool[:], k_words[0].rearrange("p t b -> p (t b)").bitcast(I32))
-        ls_rows = tile("ls_rows", [P, P], F32)
-        nc.sync.dma_start(ls_rows[P - QB : P, :], ls[0, 0, :].rearrange("(b p) -> b p", p=P))
+        ls_rows = tile("ls_rows", [P, P + 1], F32)
+        nc.sync.dma_start(ls_rows[P - QB : P, 0:P], ls[0, 0, :].rearrange("(b p) -> b p", p=P))
         q_raw = [tile("q_raw0", [P, PACK, NQ], F32), placed("q_raw1", [P, PACK, NQ], F32, 0)]
 
         def load_q(o):
             nc.sync.dma_start(q_raw[o][:], qT[0, o * 512 : (o + 1) * 512, :].rearrange("(p j) q -> p j q", j=PACK))
 
         load_q(0)
-        nc.gpsimd.memset(s_area[32:64, 0 : T // 4], 0)
-        nc.gpsimd.memset(s_area[64:P, 0 : T // 4], 0)
-        nc.vector.memset(dc_pool[0 : P - 1, :], 0.0)
+        nc.vector.memset(s_area[32:64, 0 : T // 4 + 1], 0)
+        nc.vector.memset(s_area[64:P, 0 : T // 4 + 1], 0)
+        nc.gpsimd.memset(dc_pool[0 : P - 1, :], 0.0)
+        k_scale = tile("k_scale", [P, PASSES * N // 4 + 1], I32)
+        nc.vector.memset(k_scale[:], 0)
+        nc.vector.memset(ls_rows[0 : P - QB, :], 0.0)
         ident = tile("ident", [P, P], F32)
         make_identity(nc, ident[:])
-        k_scale = tile("k_scale", [P, PASSES * N // 4], I32)
-        nc.gpsimd.memset(k_scale[:], 0)
-        nc.gpsimd.memset(ls_rows[0 : P - QB, :], 0.0)
 
         s_picked = tile("s_picked", [P, N], U8)
         nc.vector.tensor_copy(s_picked[:], s_pool.bitcast(U8).indirect(offsets[:]))
         for quad in range(4):
             nc.sync.dma_start(
-                k_scale[32 * quad : 32 * quad + 4, :].rearrange("p (o n) -> p o n", o=PASSES),
+                k_scale[32 * quad : 32 * quad + 4, 0 : PASSES * N // 4].rearrange("p (o n) -> p o n", o=PASSES),
                 s_picked[8 * quad : 8 * quad + 8, :].bitcast(I32),
             )
         load_q(1)
@@ -93,19 +93,21 @@ def tile_attend_atb_decay_topk_kernel(tc, qT, k_words, k_scales, vT, dc, ls, lm,
             pa_raw.append(raw)
 
         dc_row = tile("dc_row", [P, N], F32)
-        nc.vector.tensor_copy(dc_row[:, 0 : N // 2], dc_pool[:].indirect(offsets[:, 0 : N // 32]))
+        nc.vector.tensor_copy(dc_row[:], dc_pool[:].indirect(offsets[:]))
         k_pair = tile("k_pair", [P, N], U32)
         nc.vector.tensor_copy(k_pair[:], k_pool[:].bitcast(U32).indirect(offsets[:]))
-        k_code = [tile("k_code%d" % o, [P, 2 * N], U8) for o in range(PASSES)]
+        k_code = [tile("k_code0", [P, 2 * N], U8), placed("k_code1", [P, 2 * N], U8, 70)]
         k_halves = k_pair[:].bitcast(U16).rearrange("p (n o) -> p o n", o=PASSES)
-        for o in range(PASSES):
-            nc.vector.tensor_copy(k_code[o][:].bitcast(U16), k_halves[:, o, :])
+        nc.vector.tensor_copy(k_code[0][:].bitcast(U16), k_halves[:, 0, :])
         nc.vector.memset(lm_rows[0 : P - QB, :], 0.0)
 
         ls_ps = bank("ls_ps", [P, P], 7)
-        nc.tensor.transpose(ls_ps[:], ls_rows[:], ident[:])
+        nc.tensor.transpose(ls_ps[:], ls_rows[:, 0:P], ident[:])
         neg_ls = tile("neg_ls", [P, QB], F32)
         nc.scalar.activation(neg_ls[:], ls_ps[:, P - QB : P], COPY, scale=-1.0)
+        dc_ps = bank("dc_ps", [P, PACK, P], 6)
+        for t in range(PACK):
+            nc.tensor.transpose(dc_ps[:, t, :], dc_row[:, t::PACK], ident[:])
 
         def quantize(code, scale, woven):
             nc.vector.quantize_mx(code.bitcast(FP8X4), scale, woven[:].rearrange("p q t -> p (q t)"))
@@ -115,8 +117,8 @@ def tile_attend_atb_decay_topk_kernel(tc, qT, k_words, k_scales, vT, dc, ls, lm,
         for o in range(PASSES):
             woven = []
             for first, count, copy in shares:
-                if (o, first) == (0, 3):
-                    part = dc_row[:, N // 2 : N].bitcast(BF16).rearrange("p (q t) -> p q t", t=PACK)
+                if (o, first) == (0, 2):
+                    part = placed("q_woven0_2", [P, P, PACK], BF16, 70)[:]
                 else:
                     part = tile("q_woven%d_%d" % (o, first), [P, count * P, PACK], BF16)[:]
                 copy(
@@ -139,10 +141,7 @@ def tile_attend_atb_decay_topk_kernel(tc, qT, k_words, k_scales, vT, dc, ls, lm,
                         stop=(o == PASSES - 1),
                     )
             if o == 0:
-                nc.vector.tensor_copy(dc_row[:, N // 2 : N], dc_pool[:].indirect(offsets[:, N // 32 : N // 16]))
-        dc_ps = bank("dc_ps", [P, PACK, P], 6)
-        for t in range(PACK):
-            nc.tensor.transpose(dc_ps[:, t, :], dc_row[:, t::PACK], ident[:])
+                nc.vector.tensor_copy(k_code[1][:].bitcast(U16), k_halves[:, 1, :])
         weight = placed("weight", [P, PACK], F32, 2)
         nc.vector.tensor_tensor(weight[:], dc_ps[:, :, P - 1], us_t[:], MULT)
 
@@ -157,9 +156,17 @@ def tile_attend_atb_decay_topk_kernel(tc, qT, k_words, k_scales, vT, dc, ls, lm,
             placed("y_code2", [P, P], U32, 25),
         ]
         y_scale = [tile("y_scale%d" % j, [P, w], U8) for j, w in enumerate((2 * P, P, P))]
-        v_bf = [placed("v_bf0", [P, HALF, PACK], BF16, 58), tile("v_bf1", [P, HALF, PACK], BF16)]
-        v_code = [placed("v_code0", [P, HALF], U32, 26), placed("v_code1", [P, HALF], U32, 64)]
-        v_scale = [tile("v_scale%d" % g, [P, HALF], U8) for g in range(2)]
+        v_bf = [
+            placed("v_bf0", [P, HALF, PACK], BF16, 58),
+            tile("v_bf1", [P, P, PACK], BF16),
+            tile("v_bf2", [P, P, PACK], BF16),
+        ]
+        v_code = [
+            placed("v_code0", [P, HALF], U32, 26),
+            placed("v_code1", [P, P], U32, 36),
+            placed("v_code2", [P, P], U32, 64),
+        ]
+        v_scale = [tile("v_scale%d" % g, [P, w], U8) for g, w in enumerate((HALF, P, P))]
 
         def gather_v(c):
             picked = placed("v_picked%d" % c, [P, (1, 1, 1, 4)[c] * N], BF16, (0, 52, 56, 58)[c])[:, 0:N]
@@ -171,9 +178,8 @@ def tile_attend_atb_decay_topk_kernel(tc, qT, k_words, k_scales, vT, dc, ls, lm,
             words = picked.bitcast(F32)
             for u in range(2):
                 nc.tensor.transpose(turned[:, u, :], words[:, u::2], ident[:])
-            nc.scalar.copy(
-                v_bf[c // 2][:, (c % 2) * P : (c % 2 + 1) * P, :].bitcast(F32), turned[:].rearrange("p u e -> p e u")
-            )
+            woven = v_bf[0][:, c * P : (c + 1) * P, :] if c < 2 else v_bf[c - 1][:]
+            nc.scalar.copy(woven.bitcast(F32), turned[:].rearrange("p u e -> p e u"))
 
         def turn_p(b):
             prob = placed("prob%d" % b, [P, PACK, P], F32, 50 + 2 * b)
@@ -202,9 +208,9 @@ def tile_attend_atb_decay_topk_kernel(tc, qT, k_words, k_scales, vT, dc, ls, lm,
         turn_v(0, picked0)
         picked1 = gather_v(1)
         quantize(y_code[0][:], y_scale[0][:], y_bf[0])
-        weigh(y_bf[1][:], p_turned[2])
-        for t in range(PACK):
-            nc.scalar.activation(y_bf[2][:, :, t], p_turned[3][:, t, :], COPY, scale=weight[:, t : t + 1])
+        for b in (2, 3):
+            for t in range(PACK):
+                nc.scalar.activation(y_bf[b - 1][:, :, t], p_turned[b][:, t, :], COPY, scale=weight[:, t : t + 1])
         turn_v(1, picked1)
         lm_col = tile("lm_col", [P, QB], F32)
         nc.scalar.copy(lm_col[:], lm_ps[:, P - QB : P])
@@ -246,12 +252,15 @@ def tile_attend_atb_decay_topk_kernel(tc, qT, k_words, k_scales, vT, dc, ls, lm,
             if b % 2:
                 nc.sync.dma_start(rows_out[:, b - 1 : b + 1, 0:HALF], res[0][:, b - 1 : b + 1, :])
 
+        quantize(v_code[1][:], v_scale[1][:], v_bf[1])
+        late = [bank("late%d" % b, [P, HALF], 4 + b) for b in range(QB)]
+        for b in range(QB):
+            product(late[b][:, 0:P], 1, b)
         for b in range(QB - 1):
             mix_first(b)
-        quantize(v_code[1][:], v_scale[1][:], v_bf[1])
-        late = [bank("late%d" % b, [P, HALF], (1, 3, 2, 0)[b]) for b in range(QB)]
+        quantize(v_code[2][:], v_scale[2][:], v_bf[2])
         for b in range(QB):
-            product(late[b][:], 1, b)
+            product(late[b][:, P:HALF], 2, b)
         mix_first(QB - 1)
         for b in range(QB):
             nc.vector.scalar_tensor_tensor(res[1][:, b, :], late[b][:], lm_col[:, b : b + 1], local[:, b, :], MULT, ADD)

@@ -51,10 +51,13 @@ def tile_attend_atb_decay_topk_kernel(tc, qT, k_words, k_scales, vT, dc, ls, lm,
         nc.sync.dma_start(s_area[0:32, 0 : T // 4], k_scales.rearrange("o f t -> f o t").bitcast(I32))
         dc_pool = tile("dc_pool", [P, T], F32)
         nc.sync.dma_start(dc_pool[P - 1 : P, :], dc[0:1, :])
-        k_pool = tile("k_pool", [P, T], I32)
+        k_pool = placed("k_pool", [P, T], I32, 72)
         nc.sync.dma_start(k_pool[:], k_words[0].rearrange("p t b -> p (t b)").bitcast(I32))
         ls_rows = tile("ls_rows", [P, P + 1], F32)
         nc.sync.dma_start(ls_rows[P - QB : P, 0:P], ls[0, 0, :].rearrange("(b p) -> b p", p=P))
+        nc.sync.dma_start(ls_rows[P - 2 * QB : P - QB, 0:P], lm[0].rearrange("(b p) x -> b (p x)", p=P))
+        us_t = tile("us_t", [P, PACK], F32)
+        nc.sync.dma_start(us_t[:], us[0].rearrange("(p t) x -> p (t x)", t=PACK))
         q_raw = [tile("q_raw0", [P, PACK, NQ], F32), placed("q_raw1", [P, PACK, NQ], F32, 0)]
 
         def load_q(o):
@@ -66,7 +69,7 @@ def tile_attend_atb_decay_topk_kernel(tc, qT, k_words, k_scales, vT, dc, ls, lm,
         nc.gpsimd.memset(dc_pool[0 : P - 1, :], 0.0)
         k_scale = tile("k_scale", [P, PASSES * N // 4 + 1], I32)
         nc.vector.memset(k_scale[:], 0)
-        nc.vector.memset(ls_rows[0 : P - QB, :], 0.0)
+        nc.vector.memset(ls_rows[0 : P - 2 * QB, :], 0.0)
         ident = tile("ident", [P, P], F32)
         make_identity(nc, ident[:])
 
@@ -78,12 +81,8 @@ def tile_attend_atb_decay_topk_kernel(tc, qT, k_words, k_scales, vT, dc, ls, lm,
                 s_picked[8 * quad : 8 * quad + 8, :].bitcast(I32),
             )
         load_q(1)
-        us_t = placed("us_t", [P, PACK], F32, 48)
-        nc.sync.dma_start(us_t[:], us[0].rearrange("(p t) x -> p (t x)", t=PACK))
         v_pool = [placed("v_pool%d" % c, [P, T], F32, 8 + 8 * c) for c in range(EB)]
         nc.sync.dma_start(v_pool[0][:], vT[0:P, :])
-        lm_rows = stream.tile([P, P], F32, name="lm_rows", align_bytes=64, offset=48 * 1024 + 512)
-        nc.sync.dma_start(lm_rows[P - QB : P, :], lm[0].rearrange("(b p) x -> b (p x)", p=P))
         for c in range(1, EB):
             nc.sync.dma_start(v_pool[c][:], vT[c * P : (c + 1) * P, :])
         pa_raw = []
@@ -99,15 +98,24 @@ def tile_attend_atb_decay_topk_kernel(tc, qT, k_words, k_scales, vT, dc, ls, lm,
         k_code = [tile("k_code0", [P, 2 * N], U8), placed("k_code1", [P, 2 * N], U8, 70)]
         k_halves = k_pair[:].bitcast(U16).rearrange("p (n o) -> p o n", o=PASSES)
         nc.vector.tensor_copy(k_code[0][:].bitcast(U16), k_halves[:, 0, :])
-        nc.vector.memset(lm_rows[0 : P - QB, :], 0.0)
 
         ls_ps = bank("ls_ps", [P, P], 7)
         nc.tensor.transpose(ls_ps[:], ls_rows[:, 0:P], ident[:])
         neg_ls = tile("neg_ls", [P, QB], F32)
         nc.scalar.activation(neg_ls[:], ls_ps[:, P - QB : P], COPY, scale=-1.0)
+        lm_col = tile("lm_col", [P, QB], F32)
+        nc.scalar.copy(lm_col[:], ls_ps[:, P - 2 * QB : P - QB])
+        rest_col = tile("rest_col", [P, QB], F32)
+        nc.scalar.activation(rest_col[:], ls_ps[:, P - 2 * QB : P - QB], COPY, scale=-1.0, bias=1.0)
         dc_ps = bank("dc_ps", [P, PACK, P], 6)
         for t in range(PACK):
             nc.tensor.transpose(dc_ps[:, t, :], dc_row[:, t::PACK], ident[:])
+        weight = placed("weight", [P, PACK], F32, 72)
+        nc.vector.tensor_tensor(weight[:], dc_ps[:, :, P - 1], us_t[:], MULT)
+        row_ps = bank("row_ps", [P, PACK, P], 5)
+        for t in range(PACK):
+            nc.tensor.transpose(row_ps[:, t, :], weight[:, t : t + 1].to_broadcast([P, P]), ident[:])
+        weight_row = tile("weight_row", [P, P, PACK], F32)
 
         def quantize(code, scale, woven):
             nc.vector.quantize_mx(code.bitcast(FP8X4), scale, woven[:].rearrange("p q t -> p (q t)"))
@@ -142,27 +150,18 @@ def tile_attend_atb_decay_topk_kernel(tc, qT, k_words, k_scales, vT, dc, ls, lm,
                     )
             if o == 0:
                 nc.vector.tensor_copy(k_code[1][:].bitcast(U16), k_halves[:, 1, :])
-        weight = placed("weight", [P, PACK], F32, 2)
-        nc.vector.tensor_tensor(weight[:], dc_ps[:, :, P - 1], us_t[:], MULT)
+                nc.scalar.copy(weight_row[:], row_ps[:].rearrange("q t m -> q m t"))
 
-        y_bf = [
-            placed("y_bf0", [P, 2 * P, PACK], BF16, 8),
-            placed("y_bf1", [P, P, PACK], BF16, 60),
-            placed("y_bf2", [P, P, PACK], BF16, 61),
-        ]
-        y_code = [
-            placed("y_code0", [P, 2 * P], U32, 16),
-            placed("y_code1", [P, P], U32, 24),
-            placed("y_code2", [P, P], U32, 25),
-        ]
-        y_scale = [tile("y_scale%d" % j, [P, w], U8) for j, w in enumerate((2 * P, P, P))]
+        y_bf = [placed("y_bf0", [P, 2 * P, PACK], BF16, 8), placed("y_bf1", [P, 2 * P, PACK], BF16, 60)]
+        y_code = [placed("y_code0", [P, 2 * P], U32, 16), placed("y_code1", [P, 2 * P], U32, 28)]
+        y_scale = [tile("y_scale%d" % j, [P, 2 * P], U8) for j in range(2)]
         v_bf = [
             placed("v_bf0", [P, HALF, PACK], BF16, 58),
             tile("v_bf1", [P, P, PACK], BF16),
             tile("v_bf2", [P, P, PACK], BF16),
         ]
         v_code = [
-            placed("v_code0", [P, HALF], U32, 26),
+            placed("v_code0", [P, HALF], U32, 29),
             placed("v_code1", [P, P], U32, 36),
             placed("v_code2", [P, P], U32, 64),
         ]
@@ -199,30 +198,37 @@ def tile_attend_atb_decay_topk_kernel(tc, qT, k_words, k_scales, vT, dc, ls, lm,
                 MULT,
             )
 
+        def weigh_rows(b):
+            prob = placed("prob%d" % b, [P, N], F32, 50 + 2 * b)
+            nc.scalar.activation(prob[:], score[b][:], EXP, bias=neg_ls[:, b : b + 1])
+            rows = tile("y_rows%d" % b, [P, N], BF16)
+            nc.gpsimd.tensor_tensor(rows[:], prob[:], weight_row[:].rearrange("q m t -> q (m t)"), MULT)
+            return rows
+
+        def turn_rows(b, rows):
+            turned = bank("y_turned%d" % b, [P, 2, P], 4 + b)
+            words = rows[:].bitcast(F32)
+            for u in range(2):
+                nc.tensor.transpose(turned[:, u, :], words[:, u::2], ident[:])
+            nc.scalar.copy(y_bf[1][:, (b - 2) * P : (b - 1) * P, :].bitcast(F32), turned[:].rearrange("p u q -> p q u"))
+
         picked0 = gather_v(0)
-        p_turned = [turn_p(b) for b in range(QB)]
-        lm_ps = bank("lm_ps", [P, P], 0)
-        nc.tensor.transpose(lm_ps[:], lm_rows[:], ident[:])
+        p_turned = [turn_p(b) for b in range(2)]
+        y_rows = [weigh_rows(b) for b in (2, 3)]
         weigh(y_bf[0][:, 0:P, :], p_turned[0])
         weigh(y_bf[0][:, P : 2 * P, :], p_turned[1])
-        turn_v(0, picked0)
         picked1 = gather_v(1)
         quantize(y_code[0][:], y_scale[0][:], y_bf[0])
-        for b in (2, 3):
-            for t in range(PACK):
-                nc.scalar.activation(y_bf[b - 1][:, :, t], p_turned[b][:, t, :], COPY, scale=weight[:, t : t + 1])
+        turn_v(0, picked0)
+        turn_rows(2, y_rows[0])
+        turn_rows(3, y_rows[1])
         turn_v(1, picked1)
-        lm_col = tile("lm_col", [P, QB], F32)
-        nc.scalar.copy(lm_col[:], lm_ps[:, P - QB : P])
-        rest_col = tile("rest_col", [P, QB], F32)
-        nc.scalar.activation(rest_col[:], lm_ps[:, P - QB : P], COPY, scale=-1.0, bias=1.0)
         turn_v(2, gather_v(2))
         quantize(y_code[1][:], y_scale[1][:], y_bf[1])
-        quantize(y_code[2][:], y_scale[2][:], y_bf[2])
         quantize(v_code[0][:], v_scale[0][:], v_bf[0])
 
         def product(acc, g, b):
-            j, cols = (0, slice(b * P, (b + 1) * P)) if b < 2 else (b - 1, slice(0, P))
+            j, cols = b // 2, slice((b % 2) * P, (b % 2 + 1) * P)
             nc.tensor.matmul_mx(
                 acc,
                 lhsT=y_code[j][:, cols].bitcast(FP8X4),
@@ -238,10 +244,16 @@ def tile_attend_atb_decay_topk_kernel(tc, qT, k_words, k_scales, vT, dc, ls, lm,
             early = bank("early%d" % b, [P, HALF], 4 + b)
             product(early[:], 0, b)
             nc.scalar.activation(scaled_sum[b][:], early[:], COPY, scale=lm_col[:, b : b + 1])
-        turn_v(3, gather_v(3))
-        local = placed("local", [P, QB, HALF], F32, 58)
-        for b in range(QB):
+        local = placed("local", [P, QB, HALF], F32, 24)
+
+        def scale_local(b):
             nc.scalar.activation(local[:, b, :], pa_raw[b][:, HALF:DV], COPY, scale=rest_col[:, b : b + 1])
+
+        picked3 = gather_v(3)
+        for b in range(QB - 1):
+            scale_local(b)
+        turn_v(3, picked3)
+        scale_local(QB - 1)
         rows_out = out[0].rearrange("(b p) e -> p b e", p=P)
         res = [placed("res0", [P, QB, HALF], F32, 32), placed("res1", [P, QB, HALF], F32, 65)]
 

@@ -261,8 +261,7 @@ def tile_attend_atb_decay_topk_kernel(tc, qT, k_words, k_scales, vT, dc, ls, lm,
             nc.vector.scalar_tensor_tensor(
                 res[0][:, b, :], pa_raw[b][:, 0:HALF], rest_col[:, b : b + 1], scaled_sum[b][:], MULT, ADD
             )
-            if b % 2:
-                nc.sync.dma_start(rows_out[:, b - 1 : b + 1, 0:HALF], res[0][:, b - 1 : b + 1, :])
+            nc.sync.dma_start(rows_out[:, b, 0:HALF], res[0][:, b, :])
 
         quantize(v_code[1][:], v_scale[1][:], v_bf[1])
         late = [bank("late%d" % b, [P, HALF], 4 + b) for b in range(QB)]
@@ -276,7 +275,4 @@ def tile_attend_atb_decay_topk_kernel(tc, qT, k_words, k_scales, vT, dc, ls, lm,
         mix_first(QB - 1)
         for b in range(QB):
             nc.vector.scalar_tensor_tensor(res[1][:, b, :], late[b][:], lm_col[:, b : b + 1], local[:, b, :], MULT, ADD)
-            if b >= 2:
-                nc.sync.dma_start(rows_out[:, b, HALF:DV], res[1][:, b, :])
-            elif b == 1:
-                nc.sync.dma_start(rows_out[:, 0:2, HALF:DV], res[1][:, 0:2, :])
+            nc.sync.dma_start(rows_out[:, b, HALF:DV], res[1][:, b, :])

@@ -53,9 +53,9 @@ def tile_attend_atb_decay_topk_kernel(tc, qT, k_words, k_scales, vT, dc, ls, lm,
         nc.sync.dma_start(dc_pool[P - 1 : P, :], dc[0:1, :])
         k_pool = placed("k_pool", [P, T], I32, 72)
         nc.sync.dma_start(k_pool[:], k_words[0].rearrange("p t b -> p (t b)").bitcast(I32))
-        ls_rows = tile("ls_rows", [P, P + 1], F32)
-        nc.sync.dma_start(ls_rows[P - QB : P, 0:P], ls[0, 0, :].rearrange("(b p) -> b p", p=P))
-        nc.sync.dma_start(ls_rows[P - 2 * QB : P - QB, 0:P], lm[0].rearrange("(b p) x -> b (p x)", p=P))
+        ls_rows = tile("ls_rows", [P, P], F32)
+        nc.sync.dma_start(ls_rows[P - QB : P, :], ls[0, 0, :].rearrange("(b p) -> b p", p=P))
+        nc.sync.dma_start(ls_rows[P - 2 * QB : P - QB, :], lm[0].rearrange("(b p) x -> b (p x)", p=P))
         us_t = tile("us_t", [P, PACK], F32)
         nc.sync.dma_start(us_t[:], us[0].rearrange("(p t) x -> p (t x)", t=PACK))
         q_raw = [tile("q_raw0", [P, PACK, NQ], F32), placed("q_raw1", [P, PACK, NQ], F32, 0)]
@@ -67,9 +67,9 @@ def tile_attend_atb_decay_topk_kernel(tc, qT, k_words, k_scales, vT, dc, ls, lm,
         nc.vector.memset(s_area[32:64, 0 : T // 4 + 1], 0)
         nc.vector.memset(s_area[64:P, 0 : T // 4 + 1], 0)
         nc.gpsimd.memset(dc_pool[0 : P - 1, :], 0.0)
-        k_scale = tile("k_scale", [P, PASSES * N // 4 + 1], I32)
-        nc.vector.memset(k_scale[:], 0)
-        nc.vector.memset(ls_rows[0 : P - 2 * QB, :], 0.0)
+        k_scale = tile("k_scale", [P, PASSES * N // 4], I32)
+        nc.gpsimd.memset(k_scale[:], 0)
+        nc.gpsimd.memset(ls_rows[0 : P - 2 * QB, :], 0.0)
         ident = tile("ident", [P, P], F32)
         make_identity(nc, ident[:])
 
@@ -77,7 +77,7 @@ def tile_attend_atb_decay_topk_kernel(tc, qT, k_words, k_scales, vT, dc, ls, lm,
         nc.vector.tensor_copy(s_picked[:], s_pool.bitcast(U8).indirect(offsets[:]))
         for quad in range(4):
             nc.sync.dma_start(
-                k_scale[32 * quad : 32 * quad + 4, 0 : PASSES * N // 4].rearrange("p (o n) -> p o n", o=PASSES),
+                k_scale[32 * quad : 32 * quad + 4, :].rearrange("p (o n) -> p o n", o=PASSES),
                 s_picked[8 * quad : 8 * quad + 8, :].bitcast(I32),
             )
         load_q(1)
@@ -100,7 +100,7 @@ def tile_attend_atb_decay_topk_kernel(tc, qT, k_words, k_scales, vT, dc, ls, lm,
         nc.vector.tensor_copy(k_code[0][:].bitcast(U16), k_halves[:, 0, :])
 
         ls_ps = bank("ls_ps", [P, P], 7)
-        nc.tensor.transpose(ls_ps[:], ls_rows[:, 0:P], ident[:])
+        nc.tensor.transpose(ls_ps[:], ls_rows[:], ident[:])
         neg_ls = tile("neg_ls", [P, QB], F32)
         nc.scalar.activation(neg_ls[:], ls_ps[:, P - QB : P], COPY, scale=-1.0)
         lm_col = tile("lm_col", [P, QB], F32)
@@ -121,23 +121,23 @@ def tile_attend_atb_decay_topk_kernel(tc, qT, k_words, k_scales, vT, dc, ls, lm,
             nc.vector.quantize_mx(code.bitcast(FP8X4), scale, woven[:].rearrange("p q t -> p (q t)"))
 
         score = [bank("score%d" % b, [P, N], b) for b in range(QB)]
-        shares = [(b, 1, nc.vector.tensor_copy if b < 2 else nc.scalar.copy) for b in range(QB)]
         for o in range(PASSES):
-            woven = []
-            for first, count, copy in shares:
-                if (o, first) == (0, 2):
-                    part = placed("q_woven0_2", [P, P, PACK], BF16, 70)[:]
-                else:
-                    part = tile("q_woven%d_%d" % (o, first), [P, count * P, PACK], BF16)[:]
+            woven = [
+                tile("q_woven%d_0" % o, [P, P, PACK], BF16),
+                tile("q_woven%d_1" % o, [P, P, PACK], BF16),
+                placed("q_woven%d_2" % o, [P, 2 * P, PACK], BF16, 70 + 14 * o),
+            ]
+            for b in range(QB):
+                copy = nc.vector.tensor_copy if b < 2 else nc.scalar.copy
+                part = woven[b][:] if b < 2 else woven[2][:, (b - 2) * P : (b - 1) * P, :]
                 copy(
                     part.rearrange("p (c i) t -> p c t i", i=4),
-                    q_raw[o][:, :, first * P : (first + count) * P].rearrange("p t (c i) -> p c t i", i=4),
+                    q_raw[o][:, :, b * P : (b + 1) * P].rearrange("p t (c i) -> p c t i", i=4),
                 )
-                woven.append(part)
-            for (first, count, copy), part in zip(shares, woven):
+            for first, count in ((0, 1), (1, 1), (2, 2)):
                 code = tile("q_code%d_%d" % (o, first), [P, count * P], U32)
                 scale = tile("q_scale%d_%d" % (o, first), [P, count * P], U8)
-                quantize(code[:], scale[:], part)
+                quantize(code[:], scale[:], woven[first])
                 for j in range(count):
                     nc.tensor.matmul_mx(
                         score[first + j][:],

@@ -51,7 +51,7 @@ def tile_attend_atb_decay_topk_kernel(tc, qT, k_words, k_scales, vT, dc, ls, lm,
         nc.sync.dma_start(s_area[0:32, 0 : T // 4], k_scales.rearrange("o f t -> f o t").bitcast(I32))
         dc_pool = tile("dc_pool", [P, T], F32)
         nc.sync.dma_start(dc_pool[P - 1 : P, :], dc[0:1, :])
-        k_pool = placed("k_pool", [P, T], I32, 72)
+        k_pool = tile("k_pool", [P, T], I32)
         nc.sync.dma_start(k_pool[:], k_words[0].rearrange("p t b -> p (t b)").bitcast(I32))
         ls_rows = tile("ls_rows", [P, P], F32)
         nc.sync.dma_start(ls_rows[P - QB : P, :], ls[0, 0, :].rearrange("(b p) -> b p", p=P))
@@ -110,12 +110,13 @@ def tile_attend_atb_decay_topk_kernel(tc, qT, k_words, k_scales, vT, dc, ls, lm,
         dc_ps = bank("dc_ps", [P, PACK, P], 6)
         for t in range(PACK):
             nc.tensor.transpose(dc_ps[:, t, :], dc_row[:, t::PACK], ident[:])
-        weight = placed("weight", [P, PACK], F32, 72)
-        nc.vector.tensor_tensor(weight[:], dc_ps[:, :, P - 1], us_t[:], MULT)
+        weight = tile("weight", [P, PACK], F32)
+        for t in range(PACK):
+            nc.scalar.activation(weight[:, t : t + 1], dc_ps[:, t, P - 1 : P], COPY, scale=us_t[:, t : t + 1])
         row_ps = bank("row_ps", [P, PACK, P], 5)
         for t in range(PACK):
             nc.tensor.transpose(row_ps[:, t, :], weight[:, t : t + 1].to_broadcast([P, P]), ident[:])
-        weight_row = tile("weight_row", [P, P, PACK], F32)
+        weight_row = tile("weight_row", [P, N], F32)
 
         def quantize(code, scale, woven):
             nc.vector.quantize_mx(code.bitcast(FP8X4), scale, woven[:].rearrange("p q t -> p (q t)"))
@@ -150,33 +151,31 @@ def tile_attend_atb_decay_topk_kernel(tc, qT, k_words, k_scales, vT, dc, ls, lm,
                     )
             if o == 0:
                 nc.vector.tensor_copy(k_code[1][:].bitcast(U16), k_halves[:, 1, :])
-                nc.scalar.copy(weight_row[:], row_ps[:].rearrange("q t m -> q m t"))
+                nc.scalar.copy(
+                    weight_row[:].rearrange("q (u m i) -> q u m i", u=2, i=2),
+                    row_ps[:].rearrange("q (u i) m -> q u m i", u=2),
+                )
 
-        y_bf = [placed("y_bf0", [P, 2 * P, PACK], BF16, 8), placed("y_bf1", [P, 2 * P, PACK], BF16, 60)]
-        y_code = [placed("y_code0", [P, 2 * P], U32, 16), placed("y_code1", [P, 2 * P], U32, 28)]
-        y_scale = [tile("y_scale%d" % j, [P, 2 * P], U8) for j in range(2)]
-        v_bf = [
-            placed("v_bf0", [P, HALF, PACK], BF16, 58),
-            tile("v_bf1", [P, P, PACK], BF16),
-            tile("v_bf2", [P, P, PACK], BF16),
-        ]
-        v_code = [
-            placed("v_code0", [P, HALF], U32, 29),
-            placed("v_code1", [P, P], U32, 36),
-            placed("v_code2", [P, P], U32, 64),
-        ]
-        v_scale = [tile("v_scale%d" % g, [P, w], U8) for g, w in enumerate((HALF, P, P))]
+        both_bf = placed("both_bf", [P, 2 * HALF, PACK], BF16, 58)
+        both_code = placed("both_code", [P, 2 * HALF], U32, 28)
+        both_scale = tile("both_scale", [P, 2 * HALF], U8)
+        y_bf = [placed("y_bf0", [P, HALF, PACK], BF16, 8)[:], both_bf[:, HALF:, :]]
+        y_code = [placed("y_code0", [P, HALF], U32, 16)[:], both_code[:, HALF:]]
+        y_scale = [tile("y_scale0", [P, HALF], U8)[:], both_scale[:, HALF:]]
+        v_bf = [both_bf[:, 0:HALF, :], tile("v_bf1", [P, P, PACK], BF16)[:], tile("v_bf2", [P, P, PACK], BF16)[:]]
+        v_code = [both_code[:, 0:HALF], placed("v_code1", [P, P], U32, 36)[:], placed("v_code2", [P, P], U32, 64)[:]]
+        v_scale = [both_scale[:, 0:HALF], tile("v_scale1", [P, P], U8)[:], tile("v_scale2", [P, P], U8)[:]]
 
         def gather_v(c):
             picked = placed("v_picked%d" % c, [P, (1, 1, 1, 4)[c] * N], BF16, (0, 52, 56, 58)[c])[:, 0:N]
-            nc.vector.tensor_copy(picked, v_pool[c][:].indirect(offsets[:]))
+            nc.vector.tensor_copy(picked.rearrange("p (u m i) -> p m u i", u=2, i=2), v_pool[c][:].indirect(offsets[:]))
             return picked
 
         def turn_v(c, picked):
             turned = bank("v_turned%d" % c, [P, 2, P], (1, 3, 2, 0)[c])
             words = picked.bitcast(F32)
             for u in range(2):
-                nc.tensor.transpose(turned[:, u, :], words[:, u::2], ident[:])
+                nc.tensor.transpose(turned[:, u, :], words[:, u * P : (u + 1) * P], ident[:])
             woven = v_bf[0][:, c * P : (c + 1) * P, :] if c < 2 else v_bf[c - 1][:]
             nc.scalar.copy(woven.bitcast(F32), turned[:].rearrange("p u e -> p e u"))
 
@@ -200,16 +199,21 @@ def tile_attend_atb_decay_topk_kernel(tc, qT, k_words, k_scales, vT, dc, ls, lm,
 
         def weigh_rows(b):
             prob = placed("prob%d" % b, [P, N], F32, 50 + 2 * b)
-            nc.scalar.activation(prob[:], score[b][:], EXP, bias=neg_ls[:, b : b + 1])
+            nc.scalar.activation(
+                prob[:].rearrange("q (u m i) -> q u m i", u=2, i=2),
+                score[b][:].rearrange("q (m u i) -> q u m i", u=2, i=2),
+                EXP,
+                bias=neg_ls[:, b : b + 1],
+            )
             rows = tile("y_rows%d" % b, [P, N], BF16)
-            nc.gpsimd.tensor_tensor(rows[:], prob[:], weight_row[:].rearrange("q m t -> q (m t)"), MULT)
+            nc.gpsimd.tensor_tensor(rows[:], prob[:], weight_row[:], MULT)
             return rows
 
         def turn_rows(b, rows):
             turned = bank("y_turned%d" % b, [P, 2, P], 4 + b)
             words = rows[:].bitcast(F32)
             for u in range(2):
-                nc.tensor.transpose(turned[:, u, :], words[:, u::2], ident[:])
+                nc.tensor.transpose(turned[:, u, :], words[:, u * P : (u + 1) * P], ident[:])
             nc.scalar.copy(y_bf[1][:, (b - 2) * P : (b - 1) * P, :].bitcast(F32), turned[:].rearrange("p u q -> p q u"))
 
         picked0 = gather_v(0)
@@ -224,8 +228,7 @@ def tile_attend_atb_decay_topk_kernel(tc, qT, k_words, k_scales, vT, dc, ls, lm,
         turn_rows(3, y_rows[1])
         turn_v(1, picked1)
         turn_v(2, gather_v(2))
-        quantize(y_code[1][:], y_scale[1][:], y_bf[1])
-        quantize(v_code[0][:], v_scale[0][:], v_bf[0])
+        quantize(both_code[:], both_scale[:], both_bf)
 
         def product(acc, g, b):
             j, cols = b // 2, slice((b % 2) * P, (b % 2 + 1) * P)

@@ -85,11 +85,14 @@ def tile_attend_atb_decay_topk_kernel(tc, qT, k_words, k_scales, vT, dc, ls, lm,
         nc.sync.dma_start(v_pool[0][:], vT[0:P, :])
         for c in range(1, EB):
             nc.sync.dma_start(v_pool[c][:], vT[c * P : (c + 1) * P, :])
-        pa_raw = []
-        for b in range(QB):
-            raw = placed("pa_raw%d" % b, [P, DV], F32, 40 + 2 * b)
-            nc.sync.dma_start(raw[:], pa[0, b * P : (b + 1) * P, :])
-            pa_raw.append(raw)
+        pa_rows = pa[0].rearrange("(b p) e -> p b e", p=P)
+        pa_head = placed("pa_head", [P, QB - 1, HALF], F32, 40)
+        nc.sync.dma_start(pa_head[:], pa_rows[:, 0 : QB - 1, 0:HALF])
+        pa_tail = placed("pa_tail", [P, HALF], F32, 43)
+        nc.sync.dma_start(pa_tail[:], pa_rows[:, QB - 1, 0:HALF])
+        pa_second = placed("pa_second", [P, QB, HALF], F32, 44)
+        nc.sync.dma_start(pa_second[:], pa_rows[:, :, HALF:DV])
+        pa_first = [pa_head[:, b, :] for b in range(QB - 1)] + [pa_tail[:]]
 
         dc_row = tile("dc_row", [P, N], F32)
         nc.vector.tensor_copy(dc_row[:], dc_pool[:].indirect(offsets[:]))
@@ -163,7 +166,7 @@ def tile_attend_atb_decay_topk_kernel(tc, qT, k_words, k_scales, vT, dc, ls, lm,
         y_code = [placed("y_code0", [P, HALF], U32, 16)[:], both_code[:, HALF:]]
         y_scale = [tile("y_scale0", [P, HALF], U8)[:], both_scale[:, HALF:]]
         v_bf = [both_bf[:, 0:HALF, :], tile("v_bf1", [P, P, PACK], BF16)[:], tile("v_bf2", [P, P, PACK], BF16)[:]]
-        v_code = [both_code[:, 0:HALF], placed("v_code1", [P, P], U32, 36)[:], placed("v_code2", [P, P], U32, 64)[:]]
+        v_code = [both_code[:, 0:HALF], placed("v_code1", [P, P], U32, 36)[:], placed("v_code2", [P, P], U32, 63)[:]]
         v_scale = [both_scale[:, 0:HALF], tile("v_scale1", [P, P], U8)[:], tile("v_scale2", [P, P], U8)[:]]
 
         def gather_v(c):
@@ -247,35 +250,38 @@ def tile_attend_atb_decay_topk_kernel(tc, qT, k_words, k_scales, vT, dc, ls, lm,
             early = bank("early%d" % b, [P, HALF], 4 + b)
             product(early[:], 0, b)
             nc.scalar.activation(scaled_sum[b][:], early[:], COPY, scale=lm_col[:, b : b + 1])
-        local = placed("local", [P, QB, HALF], F32, 24)
-
-        def scale_local(b):
-            nc.scalar.activation(local[:, b, :], pa_raw[b][:, HALF:DV], COPY, scale=rest_col[:, b : b + 1])
-
         picked3 = gather_v(3)
-        for b in range(QB - 1):
-            scale_local(b)
         turn_v(3, picked3)
-        scale_local(QB - 1)
+        local = [tile("local0", [P, QB, P], F32), tile("local1", [P, QB, P], F32)]
+        for g in range(2):
+            for b in range(QB):
+                cols = slice(g * P, (g + 1) * P)
+                nc.scalar.activation(local[g][:, b, :], pa_second[:, b, cols], COPY, scale=rest_col[:, b : b + 1])
         rows_out = out[0].rearrange("(b p) e -> p b e", p=P)
-        res = [placed("res0", [P, QB, HALF], F32, 32), placed("res1", [P, QB, HALF], F32, 65)]
+        first = tile("first", [P, QB, HALF], F32)
 
         def mix_first(b):
             nc.vector.scalar_tensor_tensor(
-                res[0][:, b, :], pa_raw[b][:, 0:HALF], rest_col[:, b : b + 1], scaled_sum[b][:], MULT, ADD
+                first[:, b, :], pa_first[b], rest_col[:, b : b + 1], scaled_sum[b][:], MULT, ADD
             )
-            nc.sync.dma_start(rows_out[:, b, 0:HALF], res[0][:, b, :])
+            nc.sync.dma_start(rows_out[:, b, 0:HALF], first[:, b, :])
 
         quantize(v_code[1][:], v_scale[1][:], v_bf[1])
-        late = [bank("late%d" % b, [P, HALF], 4 + b) for b in range(QB)]
+        third = bank("third", [P, QB, P], 1)
         for b in range(QB):
-            product(late[b][:, 0:P], 1, b)
+            product(third[:, b, :], 1, b)
         for b in range(QB - 1):
             mix_first(b)
         quantize(v_code[2][:], v_scale[2][:], v_bf[2])
+        fourth = [bank("fourth%d" % b, [P, P], 4 + b) for b in range(QB)]
         for b in range(QB):
-            product(late[b][:, P:HALF], 2, b)
-        mix_first(QB - 1)
+            product(fourth[b][:], 2, b)
+        mix_first(3)
+        res = [tile("res%d" % g, [P, QB, P], F32) for g in range(2)]
         for b in range(QB):
-            nc.vector.scalar_tensor_tensor(res[1][:, b, :], late[b][:], lm_col[:, b : b + 1], local[:, b, :], MULT, ADD)
-            nc.sync.dma_start(rows_out[:, b, HALF:DV], res[1][:, b, :])
+            nc.vector.scalar_tensor_tensor(res[0][:, b, :], third[:, b, :], lm_col[:, b : b + 1], local[0][:, b, :], MULT, ADD)
+            if b % 2 == 1:
+                nc.sync.dma_start(rows_out[:, b - 1 : b + 1, HALF : HALF + P], res[0][:, b - 1 : b + 1, :])
+        for b in range(QB):
+            nc.vector.scalar_tensor_tensor(res[1][:, b, :], fourth[b][:], lm_col[:, b : b + 1], local[1][:, b, :], MULT, ADD)
+            nc.sync.dma_start(rows_out[:, b, HALF + P : DV], res[1][:, b, :])

@@ -82,17 +82,20 @@ def tile_attend_atb_decay_topk_kernel(tc, qT, k_words, k_scales, vT, dc, ls, lm,
             )
         load_q(1)
         v_pool = [placed("v_pool%d" % c, [P, T], F32, 8 + 8 * c) for c in range(EB)]
-        nc.sync.dma_start(v_pool[0][:], vT[0:P, :])
-        for c in range(1, EB):
-            nc.sync.dma_start(v_pool[c][:], vT[c * P : (c + 1) * P, :])
+        for c in range(EB):
+            row = (c + 1) % EB * P
+            nc.sync.dma_start(v_pool[c][:], vT[row : row + P, :])
         pa_rows = pa[0].rearrange("(b p) e -> p b e", p=P)
-        pa_head = placed("pa_head", [P, QB - 1, HALF], F32, 40)
-        nc.sync.dma_start(pa_head[:], pa_rows[:, 0 : QB - 1, 0:HALF])
-        pa_tail = placed("pa_tail", [P, HALF], F32, 43)
-        nc.sync.dma_start(pa_tail[:], pa_rows[:, QB - 1, 0:HALF])
-        pa_second = placed("pa_second", [P, QB, HALF], F32, 44)
-        nc.sync.dma_start(pa_second[:], pa_rows[:, :, HALF:DV])
-        pa_first = [pa_head[:, b, :] for b in range(QB - 1)] + [pa_tail[:]]
+        pa_third = placed("pa_third", [P, QB, P], F32, 46)
+        pa_small = placed("pa_small", [P, 2, P], F32, 40)
+        pa_wide = placed("pa_wide", [P, 2, HALF], F32, 41)
+        nc.sync.dma_start(pa_small[:], pa_rows[:, 0:2, 0:P])
+        nc.sync.dma_start(pa_wide[:], pa_rows[:, 0:2, P : P + HALF])
+        pa_back = placed("pa_back", [P, 2, P + HALF], F32, 43)
+        nc.sync.dma_start(pa_back[:], pa_rows[:, 2:QB, 0 : P + HALF])
+        pa_fourth = [pa_small[:, 0, :], pa_small[:, 1, :], pa_back[:, 0, 0:P], pa_back[:, 1, 0:P]]
+        pa_first = [pa_wide[:, 0, :], pa_wide[:, 1, :], pa_back[:, 0, P:], pa_back[:, 1, P:]]
+        nc.sync.dma_start(pa_third[:], pa_rows[:, :, P + HALF : DV])
 
         dc_row = tile("dc_row", [P, N], F32)
         nc.vector.tensor_copy(dc_row[:], dc_pool[:].indirect(offsets[:]))
@@ -159,18 +162,15 @@ def tile_attend_atb_decay_topk_kernel(tc, qT, k_words, k_scales, vT, dc, ls, lm,
                     row_ps[:].rearrange("q (u i) m -> q u m i", u=2),
                 )
 
-        both_bf = placed("both_bf", [P, 2 * HALF, PACK], BF16, 58)
-        both_code = placed("both_code", [P, 2 * HALF], U32, 28)
-        both_scale = tile("both_scale", [P, 2 * HALF], U8)
-        y_bf = [placed("y_bf0", [P, HALF, PACK], BF16, 8)[:], both_bf[:, HALF:, :]]
-        y_code = [placed("y_code0", [P, HALF], U32, 16)[:], both_code[:, HALF:]]
-        y_scale = [tile("y_scale0", [P, HALF], U8)[:], both_scale[:, HALF:]]
-        v_bf = [both_bf[:, 0:HALF, :], tile("v_bf1", [P, P, PACK], BF16)[:], tile("v_bf2", [P, P, PACK], BF16)[:]]
-        v_code = [both_code[:, 0:HALF], placed("v_code1", [P, P], U32, 36)[:], placed("v_code2", [P, P], U32, 63)[:]]
-        v_scale = [both_scale[:, 0:HALF], tile("v_scale1", [P, P], U8)[:], tile("v_scale2", [P, P], U8)[:]]
+        y_bf = [placed("y_bf0", [P, HALF, PACK], BF16, 8), tile("y_bf1", [P, HALF, PACK], BF16)]
+        y_code = [placed("y_code0", [P, HALF], U32, 16), placed("y_code1", [P, HALF], U32, 29)]
+        y_scale = [tile("y_scale%d" % j, [P, HALF], U8) for j in range(2)]
+        v_bf = [tile("v_bf%d" % g, [P, width, PACK], BF16) for g, width in enumerate((HALF, P, P))]
+        v_code = [placed("v_code0", [P, HALF], U32, 28), placed("v_code1", [P, P], U32, 62), placed("v_code2", [P, P], U32, 64)]
+        v_scale = [tile("v_scale%d" % g, [P, width], U8) for g, width in enumerate((HALF, P, P))]
 
         def gather_v(c):
-            picked = placed("v_picked%d" % c, [P, (1, 1, 1, 4)[c] * N], BF16, (0, 52, 56, 58)[c])[:, 0:N]
+            picked = placed("v_picked%d" % c, [P, N], BF16, (0, 52, 56, 58)[c])[:]
             nc.vector.tensor_copy(picked.rearrange("p (u m i) -> p m u i", u=2, i=2), v_pool[c][:].indirect(offsets[:]))
             return picked
 
@@ -231,7 +231,8 @@ def tile_attend_atb_decay_topk_kernel(tc, qT, k_words, k_scales, vT, dc, ls, lm,
         turn_rows(3, y_rows[1])
         turn_v(1, picked1)
         turn_v(2, gather_v(2))
-        quantize(both_code[:], both_scale[:], both_bf)
+        quantize(v_code[0][:], v_scale[0][:], v_bf[0])
+        quantize(y_code[1][:], y_scale[1][:], y_bf[1])
 
         def product(acc, g, b):
             j, cols = b // 2, slice((b % 2) * P, (b % 2 + 1) * P)
@@ -250,13 +251,17 @@ def tile_attend_atb_decay_topk_kernel(tc, qT, k_words, k_scales, vT, dc, ls, lm,
             early = bank("early%d" % b, [P, HALF], 4 + b)
             product(early[:], 0, b)
             nc.scalar.activation(scaled_sum[b][:], early[:], COPY, scale=lm_col[:, b : b + 1])
+        local = []
+
+        def scale_local(h):
+            pair = placed("local%d" % h, [P, 2, P], F32, (66, 62)[h])
+            for b in (2 * h, 2 * h + 1):
+                nc.scalar.activation(pair[:, b % 2, :], pa_fourth[b], COPY, scale=rest_col[:, b : b + 1])
+                local.append(pair[:, b % 2, :])
+
         picked3 = gather_v(3)
+        scale_local(0)
         turn_v(3, picked3)
-        local = [tile("local0", [P, QB, P], F32), tile("local1", [P, QB, P], F32)]
-        for g in range(2):
-            for b in range(QB):
-                cols = slice(g * P, (g + 1) * P)
-                nc.scalar.activation(local[g][:, b, :], pa_second[:, b, cols], COPY, scale=rest_col[:, b : b + 1])
         rows_out = out[0].rearrange("(b p) e -> p b e", p=P)
         first = tile("first", [P, QB, HALF], F32)
 
@@ -264,24 +269,30 @@ def tile_attend_atb_decay_topk_kernel(tc, qT, k_words, k_scales, vT, dc, ls, lm,
             nc.vector.scalar_tensor_tensor(
                 first[:, b, :], pa_first[b], rest_col[:, b : b + 1], scaled_sum[b][:], MULT, ADD
             )
-            nc.sync.dma_start(rows_out[:, b, 0:HALF], first[:, b, :])
+            nc.sync.dma_start(rows_out[:, b, P : P + HALF], first[:, b, :])
 
+        mix_first(0)
+        mix_first(1)
         quantize(v_code[1][:], v_scale[1][:], v_bf[1])
-        third = bank("third", [P, QB, P], 1)
+        scaled_third = tile("scaled_third", [P, QB, P], F32)
         for b in range(QB):
-            product(third[:, b, :], 1, b)
-        for b in range(QB - 1):
-            mix_first(b)
+            third = bank("third%d" % b, [P, P], 4 + b)
+            product(third[:], 1, b)
+            nc.scalar.activation(scaled_third[:, b, :], third[:], COPY, scale=lm_col[:, b : b + 1])
+        scale_local(1)
+        mix_first(2)
+        mix_first(3)
         quantize(v_code[2][:], v_scale[2][:], v_bf[2])
-        fourth = [bank("fourth%d" % b, [P, P], 4 + b) for b in range(QB)]
+        fourth = [bank("fourth%d" % b, [P, P], (1, 2, 3, 0)[b]) for b in range(QB)]
         for b in range(QB):
             product(fourth[b][:], 2, b)
-        mix_first(3)
         res = [tile("res%d" % g, [P, QB, P], F32) for g in range(2)]
         for b in range(QB):
-            nc.vector.scalar_tensor_tensor(res[0][:, b, :], third[:, b, :], lm_col[:, b : b + 1], local[0][:, b, :], MULT, ADD)
+            nc.vector.scalar_tensor_tensor(
+                res[0][:, b, :], pa_third[:, b, :], rest_col[:, b : b + 1], scaled_third[:, b, :], MULT, ADD
+            )
             if b % 2 == 1:
-                nc.sync.dma_start(rows_out[:, b - 1 : b + 1, HALF : HALF + P], res[0][:, b - 1 : b + 1, :])
+                nc.sync.dma_start(rows_out[:, b - 1 : b + 1, P + HALF : DV], res[0][:, b - 1 : b + 1, :])
         for b in range(QB):
-            nc.vector.scalar_tensor_tensor(res[1][:, b, :], fourth[b][:], lm_col[:, b : b + 1], local[1][:, b, :], MULT, ADD)
-            nc.sync.dma_start(rows_out[:, b, HALF + P : DV], res[1][:, b, :])
+            nc.vector.scalar_tensor_tensor(res[1][:, b, :], fourth[b][:], lm_col[:, b : b + 1], local[b], MULT, ADD)
+            nc.sync.dma_start(rows_out[:, b, 0:P], res[1][:, b, :])

@@ -23,9 +23,11 @@ PASSES = D // (P * PACK)
 QB = NQ // P
 EB = DV // P
 HALF = DV // 2
+LIST_COLS = N // 16
 
 FLOPS = 2 * N * NQ * D + 2 * N * NQ * DV
 BYTES = 4 * (D * NQ + P * T + DV * T + T + 2 * NQ + N + 2 * NQ * DV) + PASSES * 16 * T + 2 * P * N // 16
+SPLIT = 18
 
 
 def tile_attend_atb_decay_topk_kernel(tc, qT, k_words, k_scales, vT, dc, ls, lm, pa, us, offs, out):
@@ -39,12 +41,12 @@ def tile_attend_atb_decay_topk_kernel(tc, qT, k_words, k_scales, vT, dc, ls, lm,
             return sb.tile(shape, dtype, name=name, align_bytes=64)
 
         def placed(name, shape, dtype, kib):
-            return stream.tile(shape, dtype, name=name, align_bytes=64, offset=1024 * kib)
+            return stream.tile(shape, dtype, name=name, align_bytes=64, offset=int(1024 * kib))
 
         def bank(name, shape, number):
             return ps.tile(shape, F32, name=name, offset=2048 * number)
 
-        offsets = sb.tile([P, N // 16], U16, name="offsets")
+        offsets = sb.tile([P, LIST_COLS], U16, name="offsets")
         nc.sync.dma_start(offsets[:], offs)
         s_area = placed("s_area", [P, 49 * 256], I32, 0)
         s_pool = s_area[:, 0 : T // 4]
@@ -56,12 +58,15 @@ def tile_attend_atb_decay_topk_kernel(tc, qT, k_words, k_scales, vT, dc, ls, lm,
         ls_rows = tile("ls_rows", [P, P], F32)
         nc.sync.dma_start(ls_rows[P - QB : P, :], ls[0, 0, :].rearrange("(b p) -> b p", p=P))
         nc.sync.dma_start(ls_rows[P - 2 * QB : P - QB, :], lm[0].rearrange("(b p) x -> b (p x)", p=P))
-        us_t = tile("us_t", [P, PACK], F32)
-        nc.sync.dma_start(us_t[:], us[0].rearrange("(p t) x -> p (t x)", t=PACK))
-        q_raw = [tile("q_raw0", [P, PACK, NQ], F32), placed("q_raw1", [P, PACK, NQ], F32, 0)]
+        q_raw = [
+            [tile("q_raw0_%d" % o, [P, PACK, HALF], F32) for o in range(PASSES)],
+            [placed("q_raw1_%d" % o, [P, PACK, HALF], F32, 4 * o) for o in range(PASSES)],
+        ]
 
-        def load_q(o):
-            nc.sync.dma_start(q_raw[o][:], qT[0, o * 512 : (o + 1) * 512, :].rearrange("(p j) q -> p j q", j=PACK))
+        def load_q(h):
+            for o in range(PASSES):
+                rows = qT[0, o * 512 : (o + 1) * 512, h * HALF : (h + 1) * HALF]
+                nc.sync.dma_start(q_raw[h][o][:], rows.rearrange("(p j) q -> p j q", j=PACK))
 
         load_q(0)
         nc.vector.memset(s_area[32:64, 0 : T // 4 + 1], 0)
@@ -80,30 +85,27 @@ def tile_attend_atb_decay_topk_kernel(tc, qT, k_words, k_scales, vT, dc, ls, lm,
                 k_scale[32 * quad : 32 * quad + 4, :].rearrange("p (o n) -> p o n", o=PASSES),
                 s_picked[8 * quad : 8 * quad + 8, :].bitcast(I32),
             )
+        us_t = placed("us_t", [P, PACK], F32, 48)
+        nc.sync.dma_start(us_t[:], us[0].rearrange("(p t) x -> p (t x)", t=PACK))
         load_q(1)
         v_pool = [placed("v_pool%d" % c, [P, T], F32, 8 + 8 * c) for c in range(EB)]
         for c in range(EB):
-            row = (c + 1) % EB * P
-            nc.sync.dma_start(v_pool[c][:], vT[row : row + P, :])
+            nc.sync.dma_start(v_pool[c][:], vT[c * P : (c + 1) * P, :])
         pa_rows = pa[0].rearrange("(b p) e -> p b e", p=P)
-        pa_third = placed("pa_third", [P, QB, P], F32, 46)
-        pa_small = placed("pa_small", [P, 2, P], F32, 40)
-        pa_wide = placed("pa_wide", [P, 2, HALF], F32, 41)
-        nc.sync.dma_start(pa_small[:], pa_rows[:, 0:2, 0:P])
-        nc.sync.dma_start(pa_wide[:], pa_rows[:, 0:2, P : P + HALF])
-        pa_back = placed("pa_back", [P, 2, P + HALF], F32, 43)
-        nc.sync.dma_start(pa_back[:], pa_rows[:, 2:QB, 0 : P + HALF])
-        pa_fourth = [pa_small[:, 0, :], pa_small[:, 1, :], pa_back[:, 0, 0:P], pa_back[:, 1, 0:P]]
-        pa_first = [pa_wide[:, 0, :], pa_wide[:, 1, :], pa_back[:, 0, P:], pa_back[:, 1, P:]]
-        nc.sync.dma_start(pa_third[:], pa_rows[:, :, P + HALF : DV])
+        pa_part = [[placed("pa%d_%d" % (g, h), [P, 2, HALF], F32, 40 + 4 * g + 2 * h) for h in range(2)] for g in range(2)]
+        for g in range(2):
+            for h in range(2):
+                nc.sync.dma_start(pa_part[g][h][:], pa_rows[:, 2 * h : 2 * h + 2, g * HALF : (g + 1) * HALF])
 
         dc_row = tile("dc_row", [P, N], F32)
-        nc.vector.tensor_copy(dc_row[:], dc_pool[:].indirect(offsets[:]))
+        nc.scalar.activation(dc_row[:], dc_pool[:].indirect(offsets[:]), COPY)
         k_pair = tile("k_pair", [P, N], U32)
         nc.vector.tensor_copy(k_pair[:], k_pool[:].bitcast(U32).indirect(offsets[:]))
-        k_code = [tile("k_code0", [P, 2 * N], U8), placed("k_code1", [P, 2 * N], U8, 70)]
-        k_halves = k_pair[:].bitcast(U16).rearrange("p (n o) -> p o n", o=PASSES)
-        nc.vector.tensor_copy(k_code[0][:].bitcast(U16), k_halves[:, 0, :])
+        k_code = tile("k_code", [P, PASSES * 2 * N], U8)
+        nc.vector.tensor_copy(
+            k_code[:].bitcast(U16).rearrange("p (o n) -> p o n", o=PASSES),
+            k_pair[:].bitcast(U16).rearrange("p (n o) -> p o n", o=PASSES),
+        )
 
         ls_ps = bank("ls_ps", [P, P], 7)
         nc.tensor.transpose(ls_ps[:], ls_rows[:], ident[:])
@@ -116,123 +118,95 @@ def tile_attend_atb_decay_topk_kernel(tc, qT, k_words, k_scales, vT, dc, ls, lm,
         dc_ps = bank("dc_ps", [P, PACK, P], 6)
         for t in range(PACK):
             nc.tensor.transpose(dc_ps[:, t, :], dc_row[:, t::PACK], ident[:])
-        weight = tile("weight", [P, PACK], F32)
-        for t in range(PACK):
-            nc.scalar.activation(weight[:, t : t + 1], dc_ps[:, t, P - 1 : P], COPY, scale=us_t[:, t : t + 1])
-        row_ps = bank("row_ps", [P, PACK, P], 5)
-        for t in range(PACK):
-            nc.tensor.transpose(row_ps[:, t, :], weight[:, t : t + 1].to_broadcast([P, P]), ident[:])
-        weight_row = tile("weight_row", [P, N], F32)
 
         def quantize(code, scale, woven):
             nc.vector.quantize_mx(code.bitcast(FP8X4), scale, woven[:].rearrange("p q t -> p (q t)"))
 
         score = [bank("score%d" % b, [P, N], b) for b in range(QB)]
-        for o in range(PASSES):
-            woven = [
-                tile("q_woven%d_0" % o, [P, P, PACK], BF16),
-                tile("q_woven%d_1" % o, [P, P, PACK], BF16),
-                placed("q_woven%d_2" % o, [P, 2 * P, PACK], BF16, 70 + 14 * o),
-            ]
-            for b in range(QB):
-                copy = nc.vector.tensor_copy if b < 2 else nc.scalar.copy
-                part = woven[b][:] if b < 2 else woven[2][:, (b - 2) * P : (b - 1) * P, :]
-                copy(
-                    part.rearrange("p (c i) t -> p c t i", i=4),
-                    q_raw[o][:, :, b * P : (b + 1) * P].rearrange("p t (c i) -> p c t i", i=4),
-                )
-            for first, count in ((0, 1), (1, 1), (2, 2)):
-                code = tile("q_code%d_%d" % (o, first), [P, count * P], U32)
-                scale = tile("q_scale%d_%d" % (o, first), [P, count * P], U8)
-                quantize(code[:], scale[:], woven[first])
-                for j in range(count):
-                    nc.tensor.matmul_mx(
-                        score[first + j][:],
-                        lhsT=code[:, j * P : (j + 1) * P].bitcast(FP8X4),
-                        lhsT_scale=scale[:, j * P : (j + 1) * P],
-                        rhs=k_code[o][:].bitcast(FP4X4),
-                        rhs_scale=k_scale[:].bitcast(U8)[:, o * N : (o + 1) * N],
-                        start=(o == 0),
-                        stop=(o == PASSES - 1),
-                    )
-            if o == 0:
-                nc.vector.tensor_copy(k_code[1][:].bitcast(U16), k_halves[:, 1, :])
-                nc.scalar.copy(
-                    weight_row[:].rearrange("q (u m i) -> q u m i", u=2, i=2),
-                    row_ps[:].rearrange("q (u i) m -> q u m i", u=2),
-                )
+        def weave(copy, woven, raw):
+            copy(woven.rearrange("p (c i) t -> p c t i", i=4), raw.rearrange("p t (c i) -> p c t i", i=4))
 
-        y_bf = [placed("y_bf0", [P, HALF, PACK], BF16, 8), tile("y_bf1", [P, HALF, PACK], BF16)]
-        y_code = [placed("y_code0", [P, HALF], U32, 16), placed("y_code1", [P, HALF], U32, 29)]
+        def score_pass(b, o, code, scale):
+            nc.tensor.matmul_mx(
+                score[b][:],
+                lhsT=code.bitcast(FP8X4),
+                lhsT_scale=scale,
+                rhs=k_code[:, o * 2 * N : (o + 1) * 2 * N].bitcast(FP4X4),
+                rhs_scale=k_scale[:].bitcast(U8)[:, o * N : (o + 1) * N],
+                start=(o == 0),
+                stop=(o == PASSES - 1),
+            )
+
+        for h, o in ((0, 0), (0, 1), (1, 0)):
+            woven = tile("q_woven%d_%d" % (h, o), [P, HALF, PACK], BF16)
+            if h == 0:
+                weave(nc.vector.tensor_copy, woven[:, 0:P, :], q_raw[h][o][:, :, 0:P])
+                weave(nc.scalar.copy, woven[:, P:HALF, :], q_raw[h][o][:, :, P:HALF])
+            else:
+                weave(nc.vector.tensor_copy, woven[:], q_raw[h][o][:])
+            code = tile("q_code%d_%d" % (h, o), [P, HALF], U32)
+            scale = tile("q_scale%d_%d" % (h, o), [P, HALF], U8)
+            quantize(code[:], scale[:], woven)
+            for j in range(2):
+                score_pass(2 * h + j, o, code[:, j * P : (j + 1) * P], scale[:, j * P : (j + 1) * P])
+        last_woven = [placed("q_woven_last%d" % j, [P, P, PACK], BF16, 86 + j) for j in range(2)]
+        for j in range(2):
+            weave(nc.vector.tensor_copy, last_woven[j][:], q_raw[1][1][:, :, j * P : (j + 1) * P])
+        for j in range(2):
+            code = tile("q_code_last%d" % j, [P, P], U32)
+            scale = tile("q_scale_last%d" % j, [P, P], U8)
+            quantize(code[:], scale[:], last_woven[j])
+            score_pass(2 + j, 1, code[:], scale[:])
+
+        weight = placed("weight", [P, PACK], F32, 87)
+        nc.vector.tensor_tensor(weight[:], dc_ps[:, :, P - 1], us_t[:], MULT)
+        y_bf = [placed("y_bf0", [P, HALF, PACK], BF16, 6), placed("y_bf1", [P, HALF, PACK], BF16, 21)]
+        y_code = [tile("y_code0", [P, HALF], U32), placed("y_code1", [P, HALF], U32, 24)]
         y_scale = [tile("y_scale%d" % j, [P, HALF], U8) for j in range(2)]
-        v_bf = [tile("v_bf%d" % g, [P, width, PACK], BF16) for g, width in enumerate((HALF, P, P))]
-        v_code = [placed("v_code0", [P, HALF], U32, 28), placed("v_code1", [P, P], U32, 62), placed("v_code2", [P, P], U32, 64)]
+        v_bf = [placed("v_bf0", [P, HALF, PACK], BF16, 16), placed("v_bf1", [P, P, PACK], BF16, 32), tile("v_bf2", [P, P, PACK], BF16)]
+        v_code = [tile("v_code0", [P, HALF], U32), placed("v_code1", [P, P], U32, 25), placed("v_code2", [P, P], U32, 33)]
         v_scale = [tile("v_scale%d" % g, [P, width], U8) for g, width in enumerate((HALF, P, P))]
 
-        def gather_v(c):
-            picked = placed("v_picked%d" % c, [P, N], BF16, (0, 52, 56, 58)[c])[:]
-            nc.vector.tensor_copy(picked.rearrange("p (u m i) -> p m u i", u=2, i=2), v_pool[c][:].indirect(offsets[:]))
-            return picked
-
-        def turn_v(c, picked):
-            turned = bank("v_turned%d" % c, [P, 2, P], (1, 3, 2, 0)[c])
+        def gather_in_order(c, split):
+            picked = placed("v_picked%d" % c, [P, N], BF16, 54 + c)[:]
+            if split:
+                nc.vector.tensor_copy(picked[:, 0 : 16 * split], v_pool[c][:].indirect(offsets[:, 0:split]))
+            nc.scalar.activation(picked[:, 16 * split : N], v_pool[c][:].indirect(offsets[:, split:LIST_COLS]), COPY)
             words = picked.bitcast(F32)
+            return [words[:, u::2] for u in range(2)]
+
+        def turn_v(c, words):
+            turned = bank("v_turned%d" % c, [P, 2, P], (c + 3) % 4)
             for u in range(2):
-                nc.tensor.transpose(turned[:, u, :], words[:, u * P : (u + 1) * P], ident[:])
+                nc.tensor.transpose(turned[:, u, :], words[u], ident[:])
+            return turned
+
+        def copy_v(c, turned):
             woven = v_bf[0][:, c * P : (c + 1) * P, :] if c < 2 else v_bf[c - 1][:]
             nc.scalar.copy(woven.bitcast(F32), turned[:].rearrange("p u e -> p e u"))
 
-        def turn_p(b):
-            prob = placed("prob%d" % b, [P, PACK, P], F32, 50 + 2 * b)
+        words = []
+        for b in range(QB):
+            if b == 2:
+                words.append(gather_in_order(1, SPLIT))
+            prob = placed("prob%d" % b, [P, PACK, P], F32, (0, 4, 50, 52)[b])
             nc.scalar.activation(
                 prob[:], score[b][:].rearrange("q (m t) -> q t m", t=PACK), EXP, bias=neg_ls[:, b : b + 1]
             )
-            turned = bank("p_turned%d" % b, [P, PACK, P], 4 + b)
+            turned = bank("p_turned%d" % b, [P, PACK, P], (4, 6, 5, 7)[b])
             for t in range(PACK):
                 nc.tensor.transpose(turned[:, t, :], prob[:, t, :], ident[:])
-            return turned
-
-        def weigh(woven, turned):
             nc.vector.tensor_tensor(
-                woven,
+                y_bf[b // 2][:, (b % 2) * P : (b % 2 + 1) * P, :],
                 turned[:].rearrange("p t q -> p q t"),
                 weight[:].unsqueeze(1).to_broadcast([P, P, PACK]),
                 MULT,
             )
-
-        def weigh_rows(b):
-            prob = placed("prob%d" % b, [P, N], F32, 50 + 2 * b)
-            nc.scalar.activation(
-                prob[:].rearrange("q (u m i) -> q u m i", u=2, i=2),
-                score[b][:].rearrange("q (m u i) -> q u m i", u=2, i=2),
-                EXP,
-                bias=neg_ls[:, b : b + 1],
-            )
-            rows = tile("y_rows%d" % b, [P, N], BF16)
-            nc.gpsimd.tensor_tensor(rows[:], prob[:], weight_row[:], MULT)
-            return rows
-
-        def turn_rows(b, rows):
-            turned = bank("y_turned%d" % b, [P, 2, P], 4 + b)
-            words = rows[:].bitcast(F32)
-            for u in range(2):
-                nc.tensor.transpose(turned[:, u, :], words[:, u * P : (u + 1) * P], ident[:])
-            nc.scalar.copy(y_bf[1][:, (b - 2) * P : (b - 1) * P, :].bitcast(F32), turned[:].rearrange("p u q -> p q u"))
-
-        picked0 = gather_v(0)
-        p_turned = [turn_p(b) for b in range(2)]
-        y_rows = [weigh_rows(b) for b in (2, 3)]
-        weigh(y_bf[0][:, 0:P, :], p_turned[0])
-        weigh(y_bf[0][:, P : 2 * P, :], p_turned[1])
-        picked1 = gather_v(1)
-        quantize(y_code[0][:], y_scale[0][:], y_bf[0])
-        turn_v(0, picked0)
-        turn_rows(2, y_rows[0])
-        turn_rows(3, y_rows[1])
-        turn_v(1, picked1)
-        turn_v(2, gather_v(2))
+            if b == 1:
+                quantize(y_code[0][:], y_scale[0][:], y_bf[0])
+        copy_v(0, turn_v(0, gather_in_order(0, 0)))
+        copy_v(1, turn_v(1, words[0]))
         quantize(v_code[0][:], v_scale[0][:], v_bf[0])
-        quantize(y_code[1][:], y_scale[1][:], y_bf[1])
 
         def product(acc, g, b):
             j, cols = b // 2, slice((b % 2) * P, (b % 2 + 1) * P)
@@ -246,30 +220,33 @@ def tile_attend_atb_decay_topk_kernel(tc, qT, k_words, k_scales, vT, dc, ls, lm,
                 stop=True,
             )
 
-        scaled_sum = [placed("scaled_sum%d" % b, [P, HALF], F32, 62 + b) for b in range(QB)]
-        for b in range(QB):
-            early = bank("early%d" % b, [P, HALF], 4 + b)
-            product(early[:], 0, b)
-            nc.scalar.activation(scaled_sum[b][:], early[:], COPY, scale=lm_col[:, b : b + 1])
-        local = []
+        scaled_sum = [placed("scaled_sum%d" % b, [P, HALF], F32, (25, 26, 33, 34)[b]) for b in range(QB)]
+        early = [bank("early%d" % b, [P, HALF], 4 + b) for b in range(QB)]
 
-        def scale_local(h):
-            pair = placed("local%d" % h, [P, 2, P], F32, (66, 62)[h])
-            for b in (2 * h, 2 * h + 1):
-                nc.scalar.activation(pair[:, b % 2, :], pa_fourth[b], COPY, scale=rest_col[:, b : b + 1])
-                local.append(pair[:, b % 2, :])
+        def scale_early(b):
+            nc.scalar.activation(scaled_sum[b][:], early[b][:], COPY, scale=lm_col[:, b : b + 1])
 
-        picked3 = gather_v(3)
-        scale_local(0)
-        turn_v(3, picked3)
+        words2 = gather_in_order(2, 0)
+        for b in range(2):
+            product(early[b][:], 0, b)
+            scale_early(b)
+        turned2 = turn_v(2, words2)
+        quantize(y_code[1][:], y_scale[1][:], y_bf[1])
+        for b in range(2, QB):
+            product(early[b][:], 0, b)
+        words3 = gather_in_order(3, SPLIT)
+        copy_v(2, turned2)
+        for b in range(2, QB):
+            scale_early(b)
+        copy_v(3, turn_v(3, words3))
         rows_out = out[0].rearrange("(b p) e -> p b e", p=P)
         first = tile("first", [P, QB, HALF], F32)
 
         def mix_first(b):
             nc.vector.scalar_tensor_tensor(
-                first[:, b, :], pa_first[b], rest_col[:, b : b + 1], scaled_sum[b][:], MULT, ADD
+                first[:, b, :], pa_part[0][b // 2][:, b % 2, :], rest_col[:, b : b + 1], scaled_sum[b][:], MULT, ADD
             )
-            nc.sync.dma_start(rows_out[:, b, P : P + HALF], first[:, b, :])
+            nc.sync.dma_start(rows_out[:, b, 0:HALF], first[:, b, :])
 
         mix_first(0)
         mix_first(1)
@@ -279,20 +256,26 @@ def tile_attend_atb_decay_topk_kernel(tc, qT, k_words, k_scales, vT, dc, ls, lm,
             third = bank("third%d" % b, [P, P], 4 + b)
             product(third[:], 1, b)
             nc.scalar.activation(scaled_third[:, b, :], third[:], COPY, scale=lm_col[:, b : b + 1])
-        scale_local(1)
+        local = placed("local", [P, QB, P], F32, 25)
+        for b in range(QB):
+            nc.scalar.activation(
+                local[:, b, :], pa_part[1][b // 2][:, b % 2, P:HALF], COPY, scale=rest_col[:, b : b + 1]
+            )
         mix_first(2)
         mix_first(3)
         quantize(v_code[2][:], v_scale[2][:], v_bf[2])
-        fourth = [bank("fourth%d" % b, [P, P], (1, 2, 3, 0)[b]) for b in range(QB)]
+        fourth = [bank("fourth%d" % b, [P, P], b) for b in range(QB)]
         for b in range(QB):
             product(fourth[b][:], 2, b)
         res = [tile("res%d" % g, [P, QB, P], F32) for g in range(2)]
         for b in range(QB):
             nc.vector.scalar_tensor_tensor(
-                res[0][:, b, :], pa_third[:, b, :], rest_col[:, b : b + 1], scaled_third[:, b, :], MULT, ADD
+                res[0][:, b, :], pa_part[1][b // 2][:, b % 2, 0:P], rest_col[:, b : b + 1], scaled_third[:, b, :], MULT, ADD
             )
             if b % 2 == 1:
-                nc.sync.dma_start(rows_out[:, b - 1 : b + 1, P + HALF : DV], res[0][:, b - 1 : b + 1, :])
+                nc.sync.dma_start(rows_out[:, b - 1 : b + 1, HALF : HALF + P], res[0][:, b - 1 : b + 1, :])
         for b in range(QB):
-            nc.vector.scalar_tensor_tensor(res[1][:, b, :], fourth[b][:], lm_col[:, b : b + 1], local[b], MULT, ADD)
-            nc.sync.dma_start(rows_out[:, b, 0:P], res[1][:, b, :])
+            nc.vector.scalar_tensor_tensor(
+                res[1][:, b, :], fourth[b][:], lm_col[:, b : b + 1], local[:, b, :], MULT, ADD
+            )
+            nc.sync.dma_start(rows_out[:, b, HALF + P : DV], res[1][:, b, :])

@@ -58,15 +58,12 @@ def tile_attend_atb_decay_topk_kernel(tc, qT, k_words, k_scales, vT, dc, ls, lm,
         ls_rows = tile("ls_rows", [P, P], F32)
         nc.sync.dma_start(ls_rows[P - QB : P, :], ls[0, 0, :].rearrange("(b p) -> b p", p=P))
         nc.sync.dma_start(ls_rows[P - 2 * QB : P - QB, :], lm[0].rearrange("(b p) x -> b (p x)", p=P))
-        q_raw = [
-            [tile("q_raw0_%d" % o, [P, PACK, HALF], F32) for o in range(PASSES)],
-            [placed("q_raw1_%d" % o, [P, PACK, HALF], F32, 4 * o) for o in range(PASSES)],
-        ]
+        us_t = tile("us_t", [P, PACK], F32)
+        nc.sync.dma_start(us_t[:], us[0].rearrange("(p t) x -> p (t x)", t=PACK))
+        q_raw = [tile("q_raw0", [P, PACK, NQ], F32), placed("q_raw1", [P, PACK, NQ], F32, 0)]
 
-        def load_q(h):
-            for o in range(PASSES):
-                rows = qT[0, o * 512 : (o + 1) * 512, h * HALF : (h + 1) * HALF]
-                nc.sync.dma_start(q_raw[h][o][:], rows.rearrange("(p j) q -> p j q", j=PACK))
+        def load_q(o):
+            nc.sync.dma_start(q_raw[o][:], qT[0, o * 512 : (o + 1) * 512, :].rearrange("(p j) q -> p j q", j=PACK))
 
         load_q(0)
         nc.vector.memset(s_area[32:64, 0 : T // 4 + 1], 0)
@@ -85,8 +82,6 @@ def tile_attend_atb_decay_topk_kernel(tc, qT, k_words, k_scales, vT, dc, ls, lm,
                 k_scale[32 * quad : 32 * quad + 4, :].rearrange("p (o n) -> p o n", o=PASSES),
                 s_picked[8 * quad : 8 * quad + 8, :].bitcast(I32),
             )
-        us_t = placed("us_t", [P, PACK], F32, 48)
-        nc.sync.dma_start(us_t[:], us[0].rearrange("(p t) x -> p (t x)", t=PACK))
         load_q(1)
         v_pool = [placed("v_pool%d" % c, [P, T], F32, 8 + 8 * c) for c in range(EB)]
         for c in range(EB):
@@ -137,35 +132,36 @@ def tile_attend_atb_decay_topk_kernel(tc, qT, k_words, k_scales, vT, dc, ls, lm,
                 stop=(o == PASSES - 1),
             )
 
-        for h, o in ((0, 0), (0, 1), (1, 0)):
-            woven = tile("q_woven%d_%d" % (h, o), [P, HALF, PACK], BF16)
-            if h == 0:
-                weave(nc.vector.tensor_copy, woven[:, 0:P, :], q_raw[h][o][:, :, 0:P])
-                weave(nc.scalar.copy, woven[:, P:HALF, :], q_raw[h][o][:, :, P:HALF])
-            else:
-                weave(nc.vector.tensor_copy, woven[:], q_raw[h][o][:])
-            code = tile("q_code%d_%d" % (h, o), [P, HALF], U32)
-            scale = tile("q_scale%d_%d" % (h, o), [P, HALF], U8)
-            quantize(code[:], scale[:], woven)
-            for j in range(2):
-                score_pass(2 * h + j, o, code[:, j * P : (j + 1) * P], scale[:, j * P : (j + 1) * P])
-        last_woven = [placed("q_woven_last%d" % j, [P, P, PACK], BF16, 86 + j) for j in range(2)]
-        for j in range(2):
-            weave(nc.vector.tensor_copy, last_woven[j][:], q_raw[1][1][:, :, j * P : (j + 1) * P])
-        for j in range(2):
-            code = tile("q_code_last%d" % j, [P, P], U32)
-            scale = tile("q_scale_last%d" % j, [P, P], U8)
-            quantize(code[:], scale[:], last_woven[j])
-            score_pass(2 + j, 1, code[:], scale[:])
-
-        weight = placed("weight", [P, PACK], F32, 87)
+        weight = tile("weight", [P, PACK], F32)
         nc.vector.tensor_tensor(weight[:], dc_ps[:, :, P - 1], us_t[:], MULT)
-        y_bf = [placed("y_bf0", [P, HALF, PACK], BF16, 6), placed("y_bf1", [P, HALF, PACK], BF16, 21)]
-        y_code = [tile("y_code0", [P, HALF], U32), placed("y_code1", [P, HALF], U32, 24)]
+        for o in range(PASSES):
+            groups = ((0, 2), (2, 2)) if o == 0 else ((0, 1), (1, 1), (2, 2))
+            woven = [tile("q_woven%d_%d" % (o, first), [P, count * P, PACK], BF16) for first, count in groups]
+            for (first, count), part in zip(groups, woven):
+                if first < 2:
+                    weave(nc.vector.tensor_copy, part[:], q_raw[o][:, :, first * P : (first + count) * P])
+                else:
+                    for j in range(count):
+                        weave(nc.scalar.copy, part[:, j * P : (j + 1) * P, :], q_raw[o][:, :, (first + j) * P : (first + j + 1) * P])
+            for (first, count), part in zip(groups, woven):
+                code = tile("q_code%d_%d" % (o, first), [P, count * P], U32)
+                scale = tile("q_scale%d_%d" % (o, first), [P, count * P], U8)
+                quantize(code[:], scale[:], part)
+                for j in range(count):
+                    score_pass(first + j, o, code[:, j * P : (j + 1) * P], scale[:, j * P : (j + 1) * P])
+
+        y_bf = [placed("y_bf0", [P, HALF, PACK], BF16, 8), placed("y_bf1", [P, HALF, PACK], BF16, 21)]
+        y_code = [placed("y_code0", [P, HALF], U32, 23), placed("y_code1", [P, HALF], U32, 24)]
         y_scale = [tile("y_scale%d" % j, [P, HALF], U8) for j in range(2)]
-        v_bf = [placed("v_bf0", [P, HALF, PACK], BF16, 16), placed("v_bf1", [P, P, PACK], BF16, 32), tile("v_bf2", [P, P, PACK], BF16)]
-        v_code = [tile("v_code0", [P, HALF], U32), placed("v_code1", [P, P], U32, 25), placed("v_code2", [P, P], U32, 33)]
-        v_scale = [tile("v_scale%d" % g, [P, width], U8) for g, width in enumerate((HALF, P, P))]
+        v_bf = [placed("v_bf%d" % c, [P, P, PACK], BF16, (16, 60, 32, 61)[c]) for c in range(EB)]
+        v_code = [placed("v_code%d" % c, [P, P], U32, (62, 63, 25, 33)[c]) for c in range(EB)]
+        v_scale = [tile("v_scale%d" % c, [P, P], U8) for c in range(EB)]
+
+        def gather_in_runs(c):
+            picked = tile("v_picked%d" % c, [P, N], BF16)[:]
+            nc.vector.tensor_copy(picked.rearrange("p (u m i) -> p m u i", u=2, i=2), v_pool[c][:].indirect(offsets[:]))
+            words = picked.bitcast(F32)
+            return [words[:, u * P : (u + 1) * P] for u in range(2)]
 
         def gather_in_order(c, split):
             picked = placed("v_picked%d" % c, [P, N], BF16, 54 + c)[:]
@@ -182,18 +178,17 @@ def tile_attend_atb_decay_topk_kernel(tc, qT, k_words, k_scales, vT, dc, ls, lm,
             return turned
 
         def copy_v(c, turned):
-            woven = v_bf[0][:, c * P : (c + 1) * P, :] if c < 2 else v_bf[c - 1][:]
-            nc.scalar.copy(woven.bitcast(F32), turned[:].rearrange("p u e -> p e u"))
+            nc.scalar.copy(v_bf[c][:].bitcast(F32), turned[:].rearrange("p u e -> p e u"))
 
-        words = []
+        words = [gather_in_runs(0)]
         for b in range(QB):
             if b == 2:
                 words.append(gather_in_order(1, SPLIT))
-            prob = placed("prob%d" % b, [P, PACK, P], F32, (0, 4, 50, 52)[b])
+            prob = tile("prob%d" % b, [P, PACK, P], F32)
             nc.scalar.activation(
                 prob[:], score[b][:].rearrange("q (m t) -> q t m", t=PACK), EXP, bias=neg_ls[:, b : b + 1]
             )
-            turned = bank("p_turned%d" % b, [P, PACK, P], (4, 6, 5, 7)[b])
+            turned = bank("p_turned%d" % b, [P, PACK, P], 4 + b)
             for t in range(PACK):
                 nc.tensor.transpose(turned[:, t, :], prob[:, t, :], ident[:])
             nc.vector.tensor_tensor(
@@ -204,9 +199,9 @@ def tile_attend_atb_decay_topk_kernel(tc, qT, k_words, k_scales, vT, dc, ls, lm,
             )
             if b == 1:
                 quantize(y_code[0][:], y_scale[0][:], y_bf[0])
-        copy_v(0, turn_v(0, gather_in_order(0, 0)))
-        copy_v(1, turn_v(1, words[0]))
-        quantize(v_code[0][:], v_scale[0][:], v_bf[0])
+        for c in range(2):
+            copy_v(c, turn_v(c, words[c]))
+            quantize(v_code[c][:], v_scale[c][:], v_bf[c])
 
         def product(acc, g, b):
             j, cols = b // 2, slice((b % 2) * P, (b % 2 + 1) * P)
@@ -226,14 +221,17 @@ def tile_attend_atb_decay_topk_kernel(tc, qT, k_words, k_scales, vT, dc, ls, lm,
         def scale_early(b):
             nc.scalar.activation(scaled_sum[b][:], early[b][:], COPY, scale=lm_col[:, b : b + 1])
 
-        words2 = gather_in_order(2, 0)
+        words2 = gather_in_order(2, 12)
+        for c in range(2):
+            for b in range(2):
+                product(early[b][:, c * P : (c + 1) * P], c, b)
         for b in range(2):
-            product(early[b][:], 0, b)
             scale_early(b)
         turned2 = turn_v(2, words2)
         quantize(y_code[1][:], y_scale[1][:], y_bf[1])
         for b in range(2, QB):
-            product(early[b][:], 0, b)
+            for c in range(2):
+                product(early[b][:, c * P : (c + 1) * P], c, b)
         words3 = gather_in_order(3, SPLIT)
         copy_v(2, turned2)
         for b in range(2, QB):
@@ -250,11 +248,11 @@ def tile_attend_atb_decay_topk_kernel(tc, qT, k_words, k_scales, vT, dc, ls, lm,
 
         mix_first(0)
         mix_first(1)
-        quantize(v_code[1][:], v_scale[1][:], v_bf[1])
+        quantize(v_code[2][:], v_scale[2][:], v_bf[2])
         scaled_third = tile("scaled_third", [P, QB, P], F32)
         for b in range(QB):
             third = bank("third%d" % b, [P, P], 4 + b)
-            product(third[:], 1, b)
+            product(third[:], 2, b)
             nc.scalar.activation(scaled_third[:, b, :], third[:], COPY, scale=lm_col[:, b : b + 1])
         local = placed("local", [P, QB, P], F32, 25)
         for b in range(QB):
@@ -263,10 +261,10 @@ def tile_attend_atb_decay_topk_kernel(tc, qT, k_words, k_scales, vT, dc, ls, lm,
             )
         mix_first(2)
         mix_first(3)
-        quantize(v_code[2][:], v_scale[2][:], v_bf[2])
+        quantize(v_code[3][:], v_scale[3][:], v_bf[3])
         fourth = [bank("fourth%d" % b, [P, P], b) for b in range(QB)]
         for b in range(QB):
-            product(fourth[b][:], 2, b)
+            product(fourth[b][:], 3, b)
         res = [tile("res%d" % g, [P, QB, P], F32) for g in range(2)]
         for b in range(QB):
             nc.vector.scalar_tensor_tensor(

@@ -150,8 +150,8 @@ def tile_attend_atb_decay_topk_kernel(tc, qT, k_words, k_scales, vT, dc, ls, lm,
                 for j in range(count):
                     score_pass(first + j, o, code[:, j * P : (j + 1) * P], scale[:, j * P : (j + 1) * P])
 
-        y_bf = [placed("y_bf0", [P, HALF, PACK], BF16, 8), placed("y_bf1", [P, HALF, PACK], BF16, 21)]
-        y_code = [placed("y_code0", [P, HALF], U32, 23), placed("y_code1", [P, HALF], U32, 24)]
+        y_bf = [placed("y_bf%d" % j, [P, HALF, PACK], BF16, 8 + 2 * j) for j in range(2)]
+        y_code = [tile("y_code0", [P, HALF], U32), tile("y_code1", [P, HALF], U32)]
         y_scale = [tile("y_scale%d" % j, [P, HALF], U8) for j in range(2)]
         v_bf = [placed("v_bf%d" % c, [P, P, PACK], BF16, (16, 60, 32, 61)[c]) for c in range(EB)]
         v_code = [placed("v_code%d" % c, [P, P], U32, (62, 63, 25, 33)[c]) for c in range(EB)]
@@ -180,10 +180,8 @@ def tile_attend_atb_decay_topk_kernel(tc, qT, k_words, k_scales, vT, dc, ls, lm,
         def copy_v(c, turned):
             nc.scalar.copy(v_bf[c][:].bitcast(F32), turned[:].rearrange("p u e -> p e u"))
 
-        words = [gather_in_runs(0)]
+        words0 = gather_in_runs(0)
         for b in range(QB):
-            if b == 2:
-                words.append(gather_in_order(1, SPLIT))
             prob = tile("prob%d" % b, [P, PACK, P], F32)
             nc.scalar.activation(
                 prob[:], score[b][:].rearrange("q (m t) -> q t m", t=PACK), EXP, bias=neg_ls[:, b : b + 1]
@@ -197,8 +195,9 @@ def tile_attend_atb_decay_topk_kernel(tc, qT, k_words, k_scales, vT, dc, ls, lm,
                 weight[:].unsqueeze(1).to_broadcast([P, P, PACK]),
                 MULT,
             )
-            if b == 1:
-                quantize(y_code[0][:], y_scale[0][:], y_bf[0])
+            if b % 2 == 1:
+                quantize(y_code[b // 2][:], y_scale[b // 2][:], y_bf[b // 2])
+        words = [words0, gather_in_order(1, 0)]
         for c in range(2):
             copy_v(c, turn_v(c, words[c]))
             quantize(v_code[c][:], v_scale[c][:], v_bf[c])
@@ -223,15 +222,11 @@ def tile_attend_atb_decay_topk_kernel(tc, qT, k_words, k_scales, vT, dc, ls, lm,
 
         words2 = gather_in_order(2, 12)
         for c in range(2):
-            for b in range(2):
+            for b in range(QB):
                 product(early[b][:, c * P : (c + 1) * P], c, b)
-        for b in range(2):
-            scale_early(b)
+        scale_early(0)
+        nc.vector.tensor_scalar(scaled_sum[1][:], early[1][:], lm_col[:, 1:2], None, MULT)
         turned2 = turn_v(2, words2)
-        quantize(y_code[1][:], y_scale[1][:], y_bf[1])
-        for b in range(2, QB):
-            for c in range(2):
-                product(early[b][:, c * P : (c + 1) * P], c, b)
         words3 = gather_in_order(3, SPLIT)
         copy_v(2, turned2)
         for b in range(2, QB):

@@ -50,14 +50,14 @@ def tile_attend_atb_decay_topk_kernel(tc, qT, k_words, k_scales, vT, dc, ls, lm,
         nc.sync.dma_start(offsets[:], offs)
         s_area = placed("s_area", [P, 49 * 256], I32, 0)
         s_pool = s_area[:, 0 : T // 4]
-        nc.sync.dma_start(s_area[0:32, 0 : T // 4], k_scales.rearrange("o f t -> f o t").bitcast(I32))
+        nc.sync.dma_start(s_area[P - 32 : P, 0 : T // 4], k_scales.rearrange("o f t -> f o t").bitcast(I32))
         dc_pool = tile("dc_pool", [P, T], F32)
-        nc.sync.dma_start(dc_pool[P - 1 : P, :], dc[0:1, :])
         k_pool = tile("k_pool", [P, T], I32)
         nc.sync.dma_start(k_pool[:], k_words[0].rearrange("p t b -> p (t b)").bitcast(I32))
-        ls_rows = tile("ls_rows", [P, P], F32)
+        ls_rows = placed("ls_rows", [P, P], F32, 76)
         nc.sync.dma_start(ls_rows[P - QB : P, :], ls[0, 0, :].rearrange("(b p) -> b p", p=P))
         nc.sync.dma_start(ls_rows[P - 2 * QB : P - QB, :], lm[0].rearrange("(b p) x -> b (p x)", p=P))
+        nc.sync.dma_start(dc_pool[P - 1 : P, :], dc[0:1, :])
         us_t = tile("us_t", [P, PACK], F32)
         nc.sync.dma_start(us_t[:], us[0].rearrange("(p t) x -> p (t x)", t=PACK))
         q_raw = [tile("q_raw0", [P, PACK, NQ], F32), placed("q_raw1", [P, PACK, NQ], F32, 0)]
@@ -66,21 +66,20 @@ def tile_attend_atb_decay_topk_kernel(tc, qT, k_words, k_scales, vT, dc, ls, lm,
             nc.sync.dma_start(q_raw[o][:], qT[0, o * 512 : (o + 1) * 512, :].rearrange("(p j) q -> p j q", j=PACK))
 
         load_q(0)
-        nc.vector.memset(s_area[32:64, 0 : T // 4 + 1], 0)
-        nc.vector.memset(s_area[64:P, 0 : T // 4 + 1], 0)
-        nc.gpsimd.memset(dc_pool[0 : P - 1, :], 0.0)
+        nc.vector.memset(s_area[0 : P - 32, 0 : T // 4], 0)
         k_scale = tile("k_scale", [P, PASSES * N // 4], I32)
         nc.gpsimd.memset(k_scale[:], 0)
         nc.gpsimd.memset(ls_rows[0 : P - 2 * QB, :], 0.0)
         ident = tile("ident", [P, P], F32)
         make_identity(nc, ident[:])
+        nc.gpsimd.memset(dc_pool[0 : P - 1, :], 0.0)
 
         s_picked = tile("s_picked", [P, N], U8)
         nc.vector.tensor_copy(s_picked[:], s_pool.bitcast(U8).indirect(offsets[:]))
         for quad in range(4):
             nc.sync.dma_start(
                 k_scale[32 * quad : 32 * quad + 4, :].rearrange("p (o n) -> p o n", o=PASSES),
-                s_picked[8 * quad : 8 * quad + 8, :].bitcast(I32),
+                s_picked[P - 32 + 8 * quad : P - 24 + 8 * quad, :].bitcast(I32),
             )
         load_q(1)
         v_pool = [placed("v_pool%d" % c, [P, T], F32, 8 + 8 * c) for c in range(EB)]
@@ -92,8 +91,6 @@ def tile_attend_atb_decay_topk_kernel(tc, qT, k_words, k_scales, vT, dc, ls, lm,
             for h in range(2):
                 nc.sync.dma_start(pa_part[g][h][:], pa_rows[:, 2 * h : 2 * h + 2, g * HALF : (g + 1) * HALF])
 
-        dc_row = tile("dc_row", [P, N], F32)
-        nc.scalar.activation(dc_row[:], dc_pool[:].indirect(offsets[:]), COPY)
         k_pair = tile("k_pair", [P, N], U32)
         nc.vector.tensor_copy(k_pair[:], k_pool[:].bitcast(U32).indirect(offsets[:]))
         k_code = tile("k_code", [P, PASSES * 2 * N], U8)
@@ -110,6 +107,8 @@ def tile_attend_atb_decay_topk_kernel(tc, qT, k_words, k_scales, vT, dc, ls, lm,
         nc.scalar.copy(lm_col[:], ls_ps[:, P - 2 * QB : P - QB])
         rest_col = tile("rest_col", [P, QB], F32)
         nc.scalar.activation(rest_col[:], ls_ps[:, P - 2 * QB : P - QB], COPY, scale=-1.0, bias=1.0)
+        dc_row = placed("dc_row", [P, N], F32, 76)
+        nc.scalar.activation(dc_row[:], dc_pool[:].indirect(offsets[:]), COPY)
         dc_ps = bank("dc_ps", [P, PACK, P], 6)
         for t in range(PACK):
             nc.tensor.transpose(dc_ps[:, t, :], dc_row[:, t::PACK], ident[:])
@@ -132,11 +131,11 @@ def tile_attend_atb_decay_topk_kernel(tc, qT, k_words, k_scales, vT, dc, ls, lm,
                 stop=(o == PASSES - 1),
             )
 
-        weight = tile("weight", [P, PACK], F32)
-        nc.vector.tensor_tensor(weight[:], dc_ps[:, :, P - 1], us_t[:], MULT)
         for o in range(PASSES):
-            groups = ((0, 2), (2, 2)) if o == 0 else ((0, 1), (1, 1), (2, 2))
-            woven = [tile("q_woven%d_%d" % (o, first), [P, count * P, PACK], BF16) for first, count in groups]
+            groups = ((0, 1), (1, 1), (2, 2))
+            woven = [
+                placed("q_woven%d_%d" % (o, first), [P, count * P, PACK], BF16, 80 + 4 * o + first) for first, count in groups
+            ]
             for (first, count), part in zip(groups, woven):
                 if first < 2:
                     weave(nc.vector.tensor_copy, part[:], q_raw[o][:, :, first * P : (first + count) * P])
@@ -150,8 +149,10 @@ def tile_attend_atb_decay_topk_kernel(tc, qT, k_words, k_scales, vT, dc, ls, lm,
                 for j in range(count):
                     score_pass(first + j, o, code[:, j * P : (j + 1) * P], scale[:, j * P : (j + 1) * P])
 
+        weight = placed("weight", [P, PACK], F32, 80)
+        nc.vector.tensor_tensor(weight[:], dc_ps[:, :, P - 1], us_t[:], MULT)
         y_bf = [placed("y_bf%d" % j, [P, HALF, PACK], BF16, 8 + 2 * j) for j in range(2)]
-        y_code = [tile("y_code0", [P, HALF], U32), tile("y_code1", [P, HALF], U32)]
+        y_code = [placed("y_code0", [P, HALF], U32, 70), tile("y_code1", [P, HALF], U32)]
         y_scale = [tile("y_scale%d" % j, [P, HALF], U8) for j in range(2)]
         v_bf = [placed("v_bf%d" % c, [P, P, PACK], BF16, (16, 60, 32, 61)[c]) for c in range(EB)]
         v_code = [placed("v_code%d" % c, [P, P], U32, (62, 63, 25, 33)[c]) for c in range(EB)]
@@ -182,7 +183,7 @@ def tile_attend_atb_decay_topk_kernel(tc, qT, k_words, k_scales, vT, dc, ls, lm,
 
         words0 = gather_in_runs(0)
         for b in range(QB):
-            prob = tile("prob%d" % b, [P, PACK, P], F32)
+            prob = placed("prob%d" % b, [P, PACK, P], F32, 66 + 2 * b)
             nc.scalar.activation(
                 prob[:], score[b][:].rearrange("q (m t) -> q t m", t=PACK), EXP, bias=neg_ls[:, b : b + 1]
             )
@@ -195,8 +196,8 @@ def tile_attend_atb_decay_topk_kernel(tc, qT, k_words, k_scales, vT, dc, ls, lm,
                 weight[:].unsqueeze(1).to_broadcast([P, P, PACK]),
                 MULT,
             )
-            if b % 2 == 1:
-                quantize(y_code[b // 2][:], y_scale[b // 2][:], y_bf[b // 2])
+            if b >= 2:
+                quantize(y_code[b - 2][:], y_scale[b - 2][:], y_bf[b - 2])
         words = [words0, gather_in_order(1, 0)]
         for c in range(2):
             copy_v(c, turn_v(c, words[c]))

@@ -112,6 +112,10 @@ def tile_attend_atb_decay_topk_kernel(tc, qT, k_words, k_scales, vT, dc, ls, lm,
         dc_ps = bank("dc_ps", [P, PACK, P], 6)
         for t in range(PACK):
             nc.tensor.transpose(dc_ps[:, t, :], dc_row[:, t::PACK], ident[:])
+        dc_col = tile("dc_col", [P, PACK], F32)
+        nc.scalar.copy(dc_col[:], dc_ps[:, :, P - 1])
+        weight = tile("weight", [P, PACK], F32)
+        nc.gpsimd.tensor_tensor(weight[:], dc_col[:], us_t[:], MULT)
 
         def quantize(code, scale, woven):
             nc.vector.quantize_mx(code.bitcast(FP8X4), scale, woven[:].rearrange("p q t -> p (q t)"))
@@ -132,7 +136,7 @@ def tile_attend_atb_decay_topk_kernel(tc, qT, k_words, k_scales, vT, dc, ls, lm,
             )
 
         for o in range(PASSES):
-            groups = ((0, 1), (1, 1), (2, 2))
+            groups = ((0, 2), (2, 2)) if o == 0 else ((0, 1), (1, 1), (2, 2))
             woven = [
                 placed("q_woven%d_%d" % (o, first), [P, count * P, PACK], BF16, 80 + 4 * o + first) for first, count in groups
             ]
@@ -149,8 +153,6 @@ def tile_attend_atb_decay_topk_kernel(tc, qT, k_words, k_scales, vT, dc, ls, lm,
                 for j in range(count):
                     score_pass(first + j, o, code[:, j * P : (j + 1) * P], scale[:, j * P : (j + 1) * P])
 
-        weight = placed("weight", [P, PACK], F32, 80)
-        nc.vector.tensor_tensor(weight[:], dc_ps[:, :, P - 1], us_t[:], MULT)
         y_bf = [placed("y_bf%d" % j, [P, HALF, PACK], BF16, 8 + 2 * j) for j in range(2)]
         y_code = [placed("y_code0", [P, HALF], U32, 70), tile("y_code1", [P, HALF], U32)]
         y_scale = [tile("y_scale%d" % j, [P, HALF], U8) for j in range(2)]

@@ -66,13 +66,14 @@ def tile_attend_atb_decay_topk_kernel(tc, qT, k_words, k_scales, vT, dc, ls, lm,
             nc.sync.dma_start(q_raw[o][:], qT[0, o * 512 : (o + 1) * 512, :].rearrange("(p j) q -> p j q", j=PACK))
 
         load_q(0)
-        nc.vector.memset(s_area[0 : P - 32, 0 : T // 4], 0)
+        nc.vector.memset(s_area[0 : P - 32, 0 : T // 8 - 1], 0)
+        nc.vector.memset(s_area[0 : P - 32, T // 8 - 1 : T // 4], 0)
+        nc.gpsimd.memset(dc_pool[0 : P - 1, :], 0.0)
         k_scale = tile("k_scale", [P, PASSES * N // 4], I32)
         nc.gpsimd.memset(k_scale[:], 0)
         nc.gpsimd.memset(ls_rows[0 : P - 2 * QB, :], 0.0)
         ident = tile("ident", [P, P], F32)
         make_identity(nc, ident[:])
-        nc.gpsimd.memset(dc_pool[0 : P - 1, :], 0.0)
 
         s_picked = tile("s_picked", [P, N], U8)
         nc.vector.tensor_copy(s_picked[:], s_pool.bitcast(U8).indirect(offsets[:]))

@@ -52,12 +52,12 @@ def tile_attend_atb_decay_topk_kernel(tc, qT, k_words, k_scales, vT, dc, ls, lm,
         s_pool = s_area[:, 0 : T // 4]
         nc.sync.dma_start(s_area[P - 32 : P, 0 : T // 4], k_scales.rearrange("o f t -> f o t").bitcast(I32))
         dc_pool = tile("dc_pool", [P, T], F32)
+        nc.sync.dma_start(dc_pool[P - 1 : P, :], dc[0:1, :])
         k_pool = tile("k_pool", [P, T], I32)
         nc.sync.dma_start(k_pool[:], k_words[0].rearrange("p t b -> p (t b)").bitcast(I32))
-        ls_rows = placed("ls_rows", [P, P], F32, 76)
+        ls_rows = tile("ls_rows", [P, P], F32)
         nc.sync.dma_start(ls_rows[P - QB : P, :], ls[0, 0, :].rearrange("(b p) -> b p", p=P))
         nc.sync.dma_start(ls_rows[P - 2 * QB : P - QB, :], lm[0].rearrange("(b p) x -> b (p x)", p=P))
-        nc.sync.dma_start(dc_pool[P - 1 : P, :], dc[0:1, :])
         us_t = tile("us_t", [P, PACK], F32)
         nc.sync.dma_start(us_t[:], us[0].rearrange("(p t) x -> p (t x)", t=PACK))
         q_raw = [tile("q_raw0", [P, PACK, NQ], F32), placed("q_raw1", [P, PACK, NQ], F32, 0)]
@@ -92,6 +92,8 @@ def tile_attend_atb_decay_topk_kernel(tc, qT, k_words, k_scales, vT, dc, ls, lm,
             for h in range(2):
                 nc.sync.dma_start(pa_part[g][h][:], pa_rows[:, 2 * h : 2 * h + 2, g * HALF : (g + 1) * HALF])
 
+        dc_row = tile("dc_row", [P, N], F32)
+        nc.scalar.activation(dc_row[:], dc_pool[:].indirect(offsets[:]), COPY)
         k_pair = tile("k_pair", [P, N], U32)
         nc.vector.tensor_copy(k_pair[:], k_pool[:].bitcast(U32).indirect(offsets[:]))
         k_code = tile("k_code", [P, PASSES * 2 * N], U8)
@@ -108,8 +110,6 @@ def tile_attend_atb_decay_topk_kernel(tc, qT, k_words, k_scales, vT, dc, ls, lm,
         nc.scalar.copy(lm_col[:], ls_ps[:, P - 2 * QB : P - QB])
         rest_col = tile("rest_col", [P, QB], F32)
         nc.scalar.activation(rest_col[:], ls_ps[:, P - 2 * QB : P - QB], COPY, scale=-1.0, bias=1.0)
-        dc_row = placed("dc_row", [P, N], F32, 76)
-        nc.scalar.activation(dc_row[:], dc_pool[:].indirect(offsets[:]), COPY)
         dc_ps = bank("dc_ps", [P, PACK, P], 6)
         for t in range(PACK):
             nc.tensor.transpose(dc_ps[:, t, :], dc_row[:, t::PACK], ident[:])

@@ -47,10 +47,10 @@ def tile_attend_atb_decay_topk_kernel(tc, qT, k_words, k_scales, vT, dc, ls, lm,
             return ps.tile(shape, F32, name=name, offset=2048 * number)
 
         offsets = sb.tile([P, LIST_COLS], U16, name="offsets")
-        nc.sync.dma_start(offsets[:], offs)
         s_area = placed("s_area", [P, 49 * 256], I32, 0)
         s_pool = s_area[:, 0 : T // 4]
         nc.sync.dma_start(s_area[P - 32 : P, 0 : T // 4], k_scales.rearrange("o f t -> f o t").bitcast(I32))
+        nc.sync.dma_start(offsets[:], offs)
         dc_pool = tile("dc_pool", [P, T], F32)
         nc.sync.dma_start(dc_pool[P - 1 : P, :], dc[0:1, :])
         k_pool = tile("k_pool", [P, T], I32)
@@ -158,8 +158,12 @@ def tile_attend_atb_decay_topk_kernel(tc, qT, k_words, k_scales, vT, dc, ls, lm,
         y_code = [placed("y_code0", [P, HALF], U32, 70), tile("y_code1", [P, HALF], U32)]
         y_scale = [tile("y_scale%d" % j, [P, HALF], U8) for j in range(2)]
         v_bf = [placed("v_bf%d" % c, [P, P, PACK], BF16, (16, 60, 32, 61)[c]) for c in range(EB)]
-        v_code = [placed("v_code%d" % c, [P, P], U32, (62, 63, 25, 33)[c]) for c in range(EB)]
-        v_scale = [tile("v_scale%d" % c, [P, P], U8) for c in range(EB)]
+        front_code = tile("front_code", [P, HALF], U32)
+        front_scale = tile("front_scale", [P, HALF], U8)
+        v_code = [front_code[:, 0:P], front_code[:, P:HALF]]
+        v_code += [placed("v_code%d" % c, [P, P], U32, (25, 33)[c - 2])[:] for c in range(2, EB)]
+        v_scale = [front_scale[:, 0:P], front_scale[:, P:HALF]]
+        v_scale += [tile("v_scale%d" % c, [P, P], U8)[:] for c in range(2, EB)]
 
         def gather_in_runs(c):
             picked = tile("v_picked%d" % c, [P, N], BF16)[:]
@@ -204,16 +208,16 @@ def tile_attend_atb_decay_topk_kernel(tc, qT, k_words, k_scales, vT, dc, ls, lm,
         words = [words0, gather_in_order(1, 0)]
         for c in range(2):
             copy_v(c, turn_v(c, words[c]))
-            quantize(v_code[c][:], v_scale[c][:], v_bf[c])
+            quantize(v_code[c], v_scale[c], v_bf[c])
 
-        def product(acc, g, b):
+        def product(acc, code, scale, b):
             j, cols = b // 2, slice((b % 2) * P, (b % 2 + 1) * P)
             nc.tensor.matmul_mx(
                 acc,
                 lhsT=y_code[j][:, cols].bitcast(FP8X4),
                 lhsT_scale=y_scale[j][:, cols],
-                rhs=v_code[g][:].bitcast(FP8X4),
-                rhs_scale=v_scale[g][:],
+                rhs=code.bitcast(FP8X4),
+                rhs_scale=scale,
                 start=True,
                 stop=True,
             )
@@ -225,9 +229,8 @@ def tile_attend_atb_decay_topk_kernel(tc, qT, k_words, k_scales, vT, dc, ls, lm,
             nc.scalar.activation(scaled_sum[b][:], early[b][:], COPY, scale=lm_col[:, b : b + 1])
 
         words2 = gather_in_order(2, 12)
-        for c in range(2):
-            for b in range(QB):
-                product(early[b][:, c * P : (c + 1) * P], c, b)
+        for b in range(QB):
+            product(early[b][:], front_code[:], front_scale[:], b)
         scale_early(0)
         nc.vector.tensor_scalar(scaled_sum[1][:], early[1][:], lm_col[:, 1:2], None, MULT)
         turned2 = turn_v(2, words2)
@@ -247,11 +250,11 @@ def tile_attend_atb_decay_topk_kernel(tc, qT, k_words, k_scales, vT, dc, ls, lm,
 
         mix_first(0)
         mix_first(1)
-        quantize(v_code[2][:], v_scale[2][:], v_bf[2])
+        quantize(v_code[2], v_scale[2], v_bf[2])
         scaled_third = tile("scaled_third", [P, QB, P], F32)
         for b in range(QB):
             third = bank("third%d" % b, [P, P], 4 + b)
-            product(third[:], 2, b)
+            product(third[:], v_code[2], v_scale[2], b)
             nc.scalar.activation(scaled_third[:, b, :], third[:], COPY, scale=lm_col[:, b : b + 1])
         local = placed("local", [P, QB, P], F32, 25)
         for b in range(QB):
@@ -260,10 +263,10 @@ def tile_attend_atb_decay_topk_kernel(tc, qT, k_words, k_scales, vT, dc, ls, lm,
             )
         mix_first(2)
         mix_first(3)
-        quantize(v_code[3][:], v_scale[3][:], v_bf[3])
+        quantize(v_code[3], v_scale[3], v_bf[3])
         fourth = [bank("fourth%d" % b, [P, P], b) for b in range(QB)]
         for b in range(QB):
-            product(fourth[b][:], 3, b)
+            product(fourth[b][:], v_code[3], v_scale[3], b)
         res = [tile("res%d" % g, [P, QB, P], F32) for g in range(2)]
         for b in range(QB):
             nc.vector.scalar_tensor_tensor(

from contextlib import ExitStack

import concourse.mybir as mybir
from concourse.masks import make_identity

F32 = mybir.dt.float32
BF16 = mybir.dt.bfloat16
I32 = mybir.dt.int32
U32 = mybir.dt.uint32
U16 = mybir.dt.uint16
U8 = mybir.dt.uint8
FP8X4 = mybir.dt.float8_e4m3fn_x4
FP4X4 = mybir.dt.float4_e2m1fn_x4
MULT = mybir.AluOpType.mult
ADD = mybir.AluOpType.add
COPY = mybir.ActivationFunctionType.Copy
EXP = mybir.ActivationFunctionType.Exp

P = 128
PACK = 4
N, T, D, NQ, DV = 512, 2048, 1024, 512, 512
PASSES = D // (P * PACK)
QB = NQ // P
EB = DV // P
HALF = DV // 2
LIST_COLS = N // 16

FLOPS = 2 * N * NQ * D + 2 * N * NQ * DV
BYTES = 4 * (D * NQ + P * T + DV * T + T + 2 * NQ + N + 2 * NQ * DV) + PASSES * 16 * T + 2 * P * N // 16
SPLIT = 18


def tile_attend_atb_decay_topk_kernel(tc, qT, k_words, k_scales, vT, dc, ls, lm, pa, us, offs, out):
    nc = tc.nc
    with ExitStack() as ctx:
        sb = ctx.enter_context(tc.tile_pool(name="sb", bufs=1))
        stream = ctx.enter_context(tc.tile_pool(name="stream", bufs=1))
        ps = ctx.enter_context(tc.psum_pool(name="ps", bufs=1))

        def tile(name, shape, dtype):
            return sb.tile(shape, dtype, name=name, align_bytes=64)

        def placed(name, shape, dtype, kib):
            return stream.tile(shape, dtype, name=name, align_bytes=64, offset=int(1024 * kib))

        def bank(name, shape, number):
            return ps.tile(shape, F32, name=name, offset=2048 * number)

        offsets = sb.tile([P, LIST_COLS], U16, name="offsets")
        s_area = placed("s_area", [P, 49 * 256], I32, 0)
        s_pool = s_area[:, 0 : T // 4]
        nc.sync.dma_start(s_area[P - 32 : P, 0 : T // 4], k_scales.rearrange("o f t -> f o t").bitcast(I32))
        nc.sync.dma_start(offsets[:], offs)
        dc_pool = tile("dc_pool", [P, T], F32)
        nc.sync.dma_start(dc_pool[P - 1 : P, :], dc[0:1, :])
        k_pool = tile("k_pool", [P, T], I32)
        nc.sync.dma_start(k_pool[:], k_words[0].rearrange("p t b -> p (t b)").bitcast(I32))
        ls_rows = tile("ls_rows", [P, P], F32)
        nc.sync.dma_start(ls_rows[P - QB : P, :], ls[0, 0, :].rearrange("(b p) -> b p", p=P))
        nc.sync.dma_start(ls_rows[P - 2 * QB : P - QB, :], lm[0].rearrange("(b p) x -> b (p x)", p=P))
        us_t = tile("us_t", [P, PACK], F32)
        nc.sync.dma_start(us_t[:], us[0].rearrange("(p t) x -> p (t x)", t=PACK))
        q_raw = [tile("q_raw0", [P, PACK, NQ], F32), placed("q_raw1", [P, PACK, NQ], F32, 0)]

        def load_q(o):
            nc.sync.dma_start(q_raw[o][:], qT[0, o * 512 : (o + 1) * 512, :].rearrange("(p j) q -> p j q", j=PACK))

        load_q(0)
        nc.vector.memset(s_area[0 : P - 32, 0 : T // 8 - 1], 0)
        nc.vector.memset(s_area[0 : P - 32, T // 8 - 1 : T // 4], 0)
        nc.gpsimd.memset(dc_pool[0 : P - 1, :], 0.0)
        k_scale = tile("k_scale", [P, PASSES * N // 4], I32)
        nc.gpsimd.memset(k_scale[:], 0)
        nc.gpsimd.memset(ls_rows[0 : P - 2 * QB, :], 0.0)
        ident = tile("ident", [P, P], F32)
        make_identity(nc, ident[:])

        s_picked = tile("s_picked", [P, N], U8)
        nc.vector.tensor_copy(s_picked[:], s_pool.bitcast(U8).indirect(offsets[:]))
        for quad in range(4):
            nc.sync.dma_start(
                k_scale[32 * quad : 32 * quad + 4, :].rearrange("p (o n) -> p o n", o=PASSES),
                s_picked[P - 32 + 8 * quad : P - 24 + 8 * quad, :].bitcast(I32),
            )
        load_q(1)
        v_pool = [placed("v_pool%d" % c, [P, T], F32, 8 + 8 * c) for c in range(EB)]
        for c in range(EB):
            nc.sync.dma_start(v_pool[c][:], vT[c * P : (c + 1) * P, :])
        pa_rows = pa[0].rearrange("(b p) e -> p b e", p=P)
        pa_part = [[placed("pa%d_%d" % (g, h), [P, 2, HALF], F32, 40 + 4 * g + 2 * h) for h in range(2)] for g in range(2)]
        for g in range(2):
            for h in range(2):
                nc.sync.dma_start(pa_part[g][h][:], pa_rows[:, 2 * h : 2 * h + 2, g * HALF : (g + 1) * HALF])

        dc_row = tile("dc_row", [P, N], F32)
        nc.scalar.activation(dc_row[:], dc_pool[:].indirect(offsets[:]), COPY)
        k_pair = tile("k_pair", [P, N], U32)
        nc.vector.tensor_copy(k_pair[:], k_pool[:].bitcast(U32).indirect(offsets[:]))
        k_code = tile("k_code", [P, PASSES * 2 * N], U8)
        nc.vector.tensor_copy(
            k_code[:].bitcast(U16).rearrange("p (o n) -> p o n", o=PASSES),
            k_pair[:].bitcast(U16).rearrange("p (n o) -> p o n", o=PASSES),
        )

        ls_ps = bank("ls_ps", [P, P], 7)
        nc.tensor.transpose(ls_ps[:], ls_rows[:], ident[:])
        neg_ls = tile("neg_ls", [P, QB], F32)
        nc.scalar.activation(neg_ls[:], ls_ps[:, P - QB : P], COPY, scale=-1.0)
        lm_col = tile("lm_col", [P, QB], F32)
        nc.scalar.copy(lm_col[:], ls_ps[:, P - 2 * QB : P - QB])
        rest_col = tile("rest_col", [P, QB], F32)
        nc.scalar.activation(rest_col[:], ls_ps[:, P - 2 * QB : P - QB], COPY, scale=-1.0, bias=1.0)
        dc_ps = bank("dc_ps", [P, PACK, P], 6)
        for t in range(PACK):
            nc.tensor.transpose(dc_ps[:, t, :], dc_row[:, t::PACK], ident[:])
        dc_col = tile("dc_col", [P, PACK], F32)
        nc.scalar.copy(dc_col[:], dc_ps[:, :, P - 1])
        weight = tile("weight", [P, PACK], F32)
        nc.gpsimd.tensor_tensor(weight[:], dc_col[:], us_t[:], MULT)

        def quantize(code, scale, woven):
            nc.vector.quantize_mx(code.bitcast(FP8X4), scale, woven[:].rearrange("p q t -> p (q t)"))

        score = [bank("score%d" % b, [P, N], b) for b in range(QB)]
        def weave(copy, woven, raw):
            copy(woven.rearrange("p (c i) t -> p c t i", i=4), raw.rearrange("p t (c i) -> p c t i", i=4))

        def score_pass(b, o, code, scale):
            nc.tensor.matmul_mx(
                score[b][:],
                lhsT=code.bitcast(FP8X4),
                lhsT_scale=scale,
                rhs=k_code[:, o * 2 * N : (o + 1) * 2 * N].bitcast(FP4X4),
                rhs_scale=k_scale[:].bitcast(U8)[:, o * N : (o + 1) * N],
                start=(o == 0),
                stop=(o == PASSES - 1),
            )

        for o in range(PASSES):
            groups = ((0, 2), (2, 2)) if o == 0 else ((0, 1), (1, 1), (2, 2))
            woven = [
                placed("q_woven%d_%d" % (o, first), [P, count * P, PACK], BF16, 80 + 4 * o + first) for first, count in groups
            ]
            for (first, count), part in zip(groups, woven):
                if first < 2:
                    weave(nc.vector.tensor_copy, part[:], q_raw[o][:, :, first * P : (first + count) * P])
                else:
                    for j in range(count):
                        weave(nc.scalar.copy, part[:, j * P : (j + 1) * P, :], q_raw[o][:, :, (first + j) * P : (first + j + 1) * P])
            for (first, count), part in zip(groups, woven):
                code = tile("q_code%d_%d" % (o, first), [P, count * P], U32)
                scale = tile("q_scale%d_%d" % (o, first), [P, count * P], U8)
                quantize(code[:], scale[:], part)
                for j in range(count):
                    score_pass(first + j, o, code[:, j * P : (j + 1) * P], scale[:, j * P : (j + 1) * P])

        y_bf = [placed("y_bf%d" % j, [P, HALF, PACK], BF16, 8 + 2 * j) for j in range(2)]
        y_code = [placed("y_code0", [P, HALF], U32, 70), tile("y_code1", [P, HALF], U32)]
        y_scale = [tile("y_scale%d" % j, [P, HALF], U8) for j in range(2)]
        v_bf = [placed("v_bf%d" % c, [P, P, PACK], BF16, (16, 60, 32, 61)[c]) for c in range(EB)]
        front_code = tile("front_code", [P, HALF], U32)
        front_scale = tile("front_scale", [P, HALF], U8)
        v_code = [front_code[:, 0:P], front_code[:, P:HALF]]
        v_code += [placed("v_code%d" % c, [P, P], U32, (25, 33)[c - 2])[:] for c in range(2, EB)]
        v_scale = [front_scale[:, 0:P], front_scale[:, P:HALF]]
        v_scale += [tile("v_scale%d" % c, [P, P], U8)[:] for c in range(2, EB)]

        def gather_in_runs(c):
            picked = tile("v_picked%d" % c, [P, N], BF16)[:]
            nc.vector.tensor_copy(picked.rearrange("p (u m i) -> p m u i", u=2, i=2), v_pool[c][:].indirect(offsets[:]))
            words = picked.bitcast(F32)
            return [words[:, u * P : (u + 1) * P] for u in range(2)]

        def gather_in_order(c, split):
            picked = placed("v_picked%d" % c, [P, N], BF16, 54 + c)[:]
            if split:
                nc.vector.tensor_copy(picked[:, 0 : 16 * split], v_pool[c][:].indirect(offsets[:, 0:split]))
            nc.scalar.activation(picked[:, 16 * split : N], v_pool[c][:].indirect(offsets[:, split:LIST_COLS]), COPY)
            words = picked.bitcast(F32)
            return [words[:, u::2] for u in range(2)]

        def turn_v(c, words):
            turned = bank("v_turned%d" % c, [P, 2, P], (c + 3) % 4)
            for u in range(2):
                nc.tensor.transpose(turned[:, u, :], words[u], ident[:])
            return turned

        def copy_v(c, turned):
            nc.scalar.copy(v_bf[c][:].bitcast(F32), turned[:].rearrange("p u e -> p e u"))

        words0 = gather_in_runs(0)
        for b in range(QB):
            prob = placed("prob%d" % b, [P, PACK, P], F32, 66 + 2 * b)
            nc.scalar.activation(
                prob[:], score[b][:].rearrange("q (m t) -> q t m", t=PACK), EXP, bias=neg_ls[:, b : b + 1]
            )
            turned = bank("p_turned%d" % b, [P, PACK, P], 4 + b)
            for t in range(PACK):
                nc.tensor.transpose(turned[:, t, :], prob[:, t, :], ident[:])
            nc.vector.tensor_tensor(
                y_bf[b // 2][:, (b % 2) * P : (b % 2 + 1) * P, :],
                turned[:].rearrange("p t q -> p q t"),
                weight[:].unsqueeze(1).to_broadcast([P, P, PACK]),
                MULT,
            )
            if b >= 2:
                quantize(y_code[b - 2][:], y_scale[b - 2][:], y_bf[b - 2])
        words = [words0, gather_in_order(1, 0)]
        for c in range(2):
            copy_v(c, turn_v(c, words[c]))
            quantize(v_code[c], v_scale[c], v_bf[c])

        def product(acc, code, scale, b):
            j, cols = b // 2, slice((b % 2) * P, (b % 2 + 1) * P)
            nc.tensor.matmul_mx(
                acc,
                lhsT=y_code[j][:, cols].bitcast(FP8X4),
                lhsT_scale=y_scale[j][:, cols],
                rhs=code.bitcast(FP8X4),
                rhs_scale=scale,
                start=True,
                stop=True,
            )

        scaled_sum = [placed("scaled_sum%d" % b, [P, HALF], F32, (25, 26, 33, 34)[b]) for b in range(QB)]
        early = [bank("early%d" % b, [P, HALF], 4 + b) for b in range(QB)]

        def scale_early(b):
            nc.scalar.activation(scaled_sum[b][:], early[b][:], COPY, scale=lm_col[:, b : b + 1])

        words2 = gather_in_order(2, 12)
        for b in range(QB):
            product(early[b][:], front_code[:], front_scale[:], b)
        scale_early(0)
        nc.vector.tensor_scalar(scaled_sum[1][:], early[1][:], lm_col[:, 1:2], None, MULT)
        turned2 = turn_v(2, words2)
        words3 = gather_in_order(3, SPLIT)
        copy_v(2, turned2)
        for b in range(2, QB):
            scale_early(b)
        copy_v(3, turn_v(3, words3))
        rows_out = out[0].rearrange("(b p) e -> p b e", p=P)
        first = tile("first", [P, QB, HALF], F32)

        def mix_first(b):
            nc.vector.scalar_tensor_tensor(
                first[:, b, :], pa_part[0][b // 2][:, b % 2, :], rest_col[:, b : b + 1], scaled_sum[b][:], MULT, ADD
            )
            nc.sync.dma_start(rows_out[:, b, 0:HALF], first[:, b, :])

        mix_first(0)
        mix_first(1)
        quantize(v_code[2], v_scale[2], v_bf[2])
        scaled_third = tile("scaled_third", [P, QB, P], F32)
        for b in range(QB):
            third = bank("third%d" % b, [P, P], 4 + b)
            product(third[:], v_code[2], v_scale[2], b)
            nc.scalar.activation(scaled_third[:, b, :], third[:], COPY, scale=lm_col[:, b : b + 1])
        local = placed("local", [P, QB, P], F32, 25)
        for b in range(QB):
            nc.scalar.activation(
                local[:, b, :], pa_part[1][b // 2][:, b % 2, P:HALF], COPY, scale=rest_col[:, b : b + 1]
            )
        mix_first(2)
        mix_first(3)
        quantize(v_code[3], v_scale[3], v_bf[3])
        fourth = [bank("fourth%d" % b, [P, P], b) for b in range(QB)]
        for b in range(QB):
            product(fourth[b][:], v_code[3], v_scale[3], b)
        res = [tile("res%d" % g, [P, QB, P], F32) for g in range(2)]
        for b in range(QB):
            nc.vector.scalar_tensor_tensor(
                res[0][:, b, :], pa_part[1][b // 2][:, b % 2, 0:P], rest_col[:, b : b + 1], scaled_third[:, b, :], MULT, ADD
            )
            if b % 2 == 1:
                nc.sync.dma_start(rows_out[:, b - 1 : b + 1, HALF : HALF + P], res[0][:, b - 1 : b + 1, :])
        for b in range(QB):
            nc.vector.scalar_tensor_tensor(
                res[1][:, b, :], fourth[b][:], lm_col[:, b : b + 1], local[:, b, :], MULT, ADD
            )
            nc.sync.dma_start(rows_out[:, b, HALF + P : DV], res[1][:, b, :])
